import numpy as np, ml_dtypes
CORES = [16,17,18,19,32,33,34,35]
N = 8
import mx_ref
BF = ml_dtypes.bfloat16
def entries(a):
    return np.ascontiguousarray(a.T).reshape(-1)
def table(e):
    return np.ascontiguousarray(np.reshape(e, (-1, 16)).T).astype(np.int32)
def cols(t, e):
    v = np.concatenate([t.reshape(128, -1, 4), np.zeros((128, 1, 4), BF)], axis=1)
    return np.ascontiguousarray(v[:, e]).reshape(128, -1)
def cut(t, i, w=512):
    return t[:, w * i:w * i + w]
def f(rng, *shape):
    return mx_ref.flush((rng.standard_normal(shape, dtype=np.float32) * np.exp2(rng.integers(-2, 3, shape[:-1] + (1,)))).astype(BF))
def wide(rng, *shape, cols=0):
    v = rng.standard_normal(shape, dtype=np.float32) * np.exp2(rng.integers(-12, 13, shape)).astype(np.float32)
    if cols: v *= np.repeat(np.exp2(rng.integers(-cols, cols + 1, shape[:-2] + (1, shape[-1] // 4))) * (rng.random(shape[:-2] + (1, shape[-1] // 4)) > 0.0625), 4, axis=-1).astype(np.float32)
    return mx_ref.flush(v.astype(BF))
T, V, M, CAPP, R, O = 512, 192, 288, 32, 3, 2
START = np.repeat(np.arange(N), V)
def loose(rng, at, to, who, but=-1):
    to = to.copy(); n = np.zeros((N, N), int); np.add.at(n, (at, to), 1)
    for i in rng.permutation(who):
        q = rng.integers(0, N)
        if q != but and n[:, q].sum() < M and (q == at[i] or n[at[i], q] < CAPP): n[at[i], to[i]] -= 1; n[at[i], q] += 1; to[i] = q
    return to
def turn(rng, at):
    to = at.copy(); far = 1 + rng.permutation(N - 1)
    for s in range(N):
        k = rng.permutation(np.flatnonzero(at == s))
        for i in range(min(N - 1, len(k) // CAPP)): to[k[CAPP * i:CAPP * i + CAPP]] = (s + far[i]) % N
    return to
def collect(rng, at, e):
    to = at.copy(); k = rng.permutation(np.flatnonzero(at == e))[M - (N - 1) * CAPP:]
    to[k] = (e + 1 + np.arange(len(k)) % (N - 1)) % N
    for s in range(N):
        if s != e: to[rng.permutation(np.flatnonzero(at == s))[:CAPP]] = e
    return to
def spill(rng, at, to, who, ranks):
    to = to.copy(); n = np.zeros((N, N), int); others = np.setdiff1d(np.arange(N * V), who); np.add.at(n, (at[others], to[others]), 1)
    for i in rng.permutation(who):
        q = ranks[np.argmin(np.where(n[at[i], ranks] < CAPP, n[:, ranks].sum(axis=0), N * V))]
        n[at[i], q] += 1; to[i] = q
    return to
def lists(rng, a, share=0.25):
    nx = rng.integers(0, N * T, (N, 2 * T)); free = [list(rng.permutation(2 * T)) for r in range(N)]
    way = np.zeros((R - 1, N * V), int)
    for k in range(R - 2, -1, -1):
        goal = a[k + 1] if k == R - 2 else a[k + 1] * T + way[k + 1] // 2
        known = {}
        for i in rng.permutation(N * V):
            s = int(a[k][i]); L = known.setdefault((s, int(goal[i])), [])
            if not L or rng.random() >= share:
                L.append(free[s].pop()); way[k, i] = L[-1]
            else: way[k, i] = L[rng.integers(0, len(L))]
        if k < R - 2: nx[a[k], way[k]] = goal
    nx[a[R - 2], way[R - 2]] = a[R - 1] * T + rng.integers(0, T, N * V)
    st = (way[0] // 2).reshape(N, V); bt = sum((way[k] % 2) << k for k in range(R - 1)).reshape(N, V)
    return {"nx": np.stack([table(e) for e in nx]), "st": np.stack([table(e) for e in st]), "bt": np.stack([table(e) for e in bt])}
def setup_inputs(rng):
    a = [START]
    for k in range(R - 1): a.append(loose(rng, a[k], a[k], np.arange(N * V)))
    return {"x": f(rng, N, 128, 4 * T), "w": f(rng, N, 128, R * O * 512), **lists(rng, a)}
def setup_inputs_through(rng):
    h = rng.integers(1, N); a = [START, START.copy(), (START + h) % N]
    for s in range(N):
        for g, k in enumerate(np.array_split(V * s + rng.permutation(V), -(-V // CAPP))): a[1][k] = (s + g) % N
    return {**setup_inputs(rng), **lists(rng, a)}
def setup_inputs_far(rng):
    a = [START]
    for k in range(R - 1): a.append(turn(rng, a[k]))
    a[R - 1] = loose(rng, a[R - 2], a[R - 1], np.flatnonzero(a[R - 1] == a[R - 2]))
    return {**setup_inputs(rng), **lists(rng, a)}
def setup_inputs_gather(rng):
    p = rng.permutation(N); home, end, bare = p[:3]; a = [START, START.copy()]
    for j, s in enumerate(p[2:]): a[1][rng.permutation(np.flatnonzero(START == s))[:min(CAPP, max(0, M - V - j * CAPP))]] = home
    to = collect(rng, a[1], end)
    to = spill(rng, a[1], to, np.flatnonzero(((a[1] == end) & (to != end)) | (to == bare)), np.append(p[3:], home))
    a.append(loose(rng, a[1], to, np.flatnonzero((to == a[1]) & (a[1] != end)), but=bare))
    return {**setup_inputs(rng), **lists(rng, a, share=0.75)}
def setup_inputs_stay(rng):
    p = rng.integers(0, N); a = [START, collect(rng, START, p)]
    a.append(loose(rng, a[1], a[1], np.flatnonzero(a[1] != p)))
    return {**setup_inputs(rng), **lists(rng, a)}
def setup_inputs_spread(rng):
    d = setup_inputs(rng); d["x"] = wide(rng, N, 128, 4 * T, cols=8); return d
def follow(nx, st, bt):
    n = np.concatenate([entries(t) for t in nx]); bits = np.concatenate([entries(t) for t in bt])
    at = [np.concatenate([entries(st[r]) + r * T for r in range(N)])]
    for k in range(R - 1): at.append(n[2 * at[k] + (bits >> k & 1)])
    return at
def check_inputs(d):
    b = []
    for name, top in (("nx", N * T), ("st", T), ("bt", 2 ** (R - 1))):
        if d[name].min() < 0 or d[name].max() >= top: b.append(name)
    if b: return b
    at = [t // T for t in follow(d["nx"], d["st"], d["bt"])]
    for k in range(R):
        if np.bincount(at[k], minlength=N).max() > M: b.append("walkers on a rank at step " + str(k))
    for k in range(R - 1):
        n = np.zeros((N, N), int); np.add.at(n, (at[k], at[k + 1]), 1); np.fill_diagonal(n, 0)
        if n.max() > CAPP: b.append("walkers from a rank to another from step " + str(k))
    return b
def reference(x, w, nx, st, bt):
    nodes = np.concatenate([x[r] for r in range(N)], axis=1)
    at = follow(nx, st, bt)
    y = np.zeros((N, 128, O * M), np.float32); ids = np.full((N, 2, M), -1, np.float32)
    for e in range(N):
        m = np.flatnonzero(at[R - 1] // T == e)
        ids[e, 0, :len(m)] = m // V; ids[e, 1, :len(m)] = m % V
        for k in range(R):
            c = np.full(M, -1); c[:len(m)] = at[k][m]
            q = mx_ref.quantize(cols(nodes, c))
            for o in range(O): y[e][:, M * o:M * o + M] += mx_ref.matmul(mx_ref.quantize(np.ascontiguousarray(cut(w[e], k * O + o))), q)
    return {"y": y, "id": ids}

@@ -1,0 +1,429 @@
+from concourse.bass import DstId, RemoteDMATransfer
+from concourse.mybir import dt, AluOpType as A, AxisListType, ActivationFunctionType as F
+
+N = 8
+TN, V, M, KEYS = 512, 192, 288, 1536
+CAP = 32
+ARR = (N - 1) * CAP
+CAND = V + ARR
+CX = CAND + CAP
+ALL = CAND + ARR
+TAIL = CAND + N * CAP
+SPREAD = 2 * ARR - 16
+YZ = CAND + SPREAD
+KW = 1544
+X4 = "float8_e4m3fn_x4"
+
+
+def _sb(n, d="float32"):
+    return ("sbuf", [128, n], d)
+
+
+SCRATCH = {
+    "stw": _sb(12, "int32"), "btw": _sb(12, "int32"), "nxrow": _sb(1024, "int32"), "nxw": _sb(64, "int32"), "nxf": _sb(64),
+    "nxt": _sb(64), "nxlin": _sb(1024), "nxl": _sb(1032), "xt": _sb(2048, "bfloat16"), "wt": _sb(3072, "bfloat16"),
+    "ic": _sb(160), "ict": _sb(160), "cf": _sb(16), "ioL": _sb(KW), "kL": _sb(208), "wab": _sb(40, "int32"), "cw0": _sb(40),
+    "wac": _sb(40, "uint16"), "cw": _sb(40), "dw": _sb(40), "yx": _sb(ALL), "sT": _sb(KW), "iT": _sb(KW),
+    "o1": _sb(64, "int32"), "off1": _sb(12, "uint16"), "b1u": _sb(12, "uint16"), "stu": _sb(12, "uint16"),
+    "n1r": _sb(V), "n1L": _sb(V), "b1L": _sb(V), "kb": _sb(V), "a1": _sb(V), "aL": _sb(208),
+    "ga": _sb(V), "gb": _sb(V), "c1L": _sb(V), "sg0": _sb(V), "sg1": _sb(V), "sg2": _sb(CX), "sg3": _sb(CX),
+    "cnt1": _sb(2), "nb": _sb(2), "sub0": _sb(208), "ab1": _sb(208), "vv": _sb(2), "pk": _sb(2),
+    "x1": _sb(64), "x1t": _sb(64), "w1": _sb(16), "w1i": _sb(16, "int32"), "w1k": _sb(16, "int32"),
+    "s1off": _sb(16, "uint16"), "land1": _sb(14),
+    "own": _sb(V), "ownt": _sb(V), "ow": _sb(96, "int32"), "noff": _sb(26, "uint16"), "c1u": _sb(26, "uint16"),
+    "n2L": _sb(CAND), "g2a": _sb(CAND), "g2b": _sb(CAND), "c2L": _sb(CX), "l1": _sb(64, "int32"),
+    "cnt2": _sb(8), "x2": _sb(64), "x2t": _sb(64), "w2": _sb(16), "o2off": _sb(32, "uint16"), "w2u": _sb(16, "uint16"),
+    "ku1": _sb(14, "uint16"), "keyL": _sb(CAND), "inf0": _sb(CAND), "infoL": _sb(CX),
+    "ig": _sb(256), "ig2": _sb(256), "igt": _sb(256), "l2s": _sb(16), "land2": _sb(14),
+    "n2g": _sb(CAND), "n2t": _sb(CAND), "n2w": _sb(80, "int32"), "c2u": _sb(26, "uint16"), "fw": _sb(120), "xx": _sb(60),
+    "ko": _sb(26), "kou": _sb(40, "uint16"), "pwa": _sb(40, "uint16"), "ones": _sb(CAND), "bm": _sb(KEYS + TAIL), "pp": _sb(KEYS + TAIL),
+    "l2i": _sb(64, "int32"), "c2ua": _sb(28, "uint16"), "ku2": _sb(28, "uint16"), "sW": _sb(YZ + 8), "iW": _sb(YZ + 8),
+    "pg": _sb(ALL), "pt": _sb(ALL), "plu": _sb(40, "uint16"), "inv": _sb(M + TAIL),
+    "ivg": _sb(M), "ivt": _sb(M), "ylu": _sb(18, "uint16"), "ids": _sb(M), "idi": _sb(M),
+    "xq": _sb(TN, X4), "xs": _sb(TN, "uint8"), "wq": _sb(768, X4), "ws": _sb(768, "uint8"),
+    "stq": _sb(V, X4), "sts": _sb(V, "uint8"), "p1q": _sb(256, X4), "p1s": _sb(256, "uint8"),
+    "cq": _sb(2 * CAND, X4), "cs": _sb(2 * CAND, "uint8"), "n2q": _sb(CAND, X4), "n2s": _sb(CAND, "uint8"),
+    "p2q": _sb(512, X4), "p2s": _sb(512, "uint8"), "eq": _sb(2 * ARR, X4), "es": _sb(2 * ARR, "uint8"),
+    "fq": _sb(SPREAD, X4), "fs": _sb(SPREAD, "uint8"),
+    "yb0": _sb(YZ + 8), "yb1": _sb(YZ + 8), "yo0": _sb(M), "yo1": _sb(M),
+    "ps": ("psum", [128, 2048], "float32"),
+}
+SEMAPHORES = ["cv", "cs_", "ct", "cg", "dst", "dbt", "dnx", "dnw", "dnl", "dx", "dw_", "dcq", "dc1", "dc2", "dy0", "dy1", "did",
+              "did2", "sent", "al1", "aq1", "as1", "al2", "aq2", "as2"]
+
+
+def _split(core, others, topo):
+    own = topo.cores_of(core)
+    far = [c for c in others if c not in own]
+    near = [c for c in others if c in own]
+    out, taken = {}, []
+    for part in (far, near):
+        if not part:
+            continue
+        free = [e for e in topo.engines(core, part[0]) if e not in taken]
+        k = 1
+        while 2 * k * len(part) <= len(free):
+            k *= 2
+        for j, c in enumerate(part):
+            out[c] = free[j * k:(j + 1) * k]
+            taken += out[c]
+    return out
+
+
+def rank_program(g, core, T, topo):
+    r = T.rank_of(core)
+    if r is None:
+        return
+    sem = T.sem
+    queues = {"v": (g.vector, "cv"), "s": (g.scalar, "cs_"), "t": (g.tensor, "ct"), "g": (g, "cg"), "y": (g.sync, None)}
+    total, seen = {}, {q: {} for q in queues}
+    wrote, read = {}, {}
+
+    def await_(q, toks):
+        eng, need = queues[q][0], {}
+        for s, val in toks:
+            val = total[s] if val is None else val
+            need[s] = max(need.get(s, 0), val)
+        for s in need:
+            if seen[q].get(s, 0) < need[s]:
+                eng.wait_ge(sem[s], need[s])
+                seen[q][s] = need[s]
+
+    def deps(q, r_, w_, own=None):
+        mine = (queues[q][1], own)
+        toks = []
+        for k in r_:
+            toks += wrote.get(k, [])
+        for k in w_:
+            toks += [t for t in wrote.get(k, []) + read.get(k, []) if t[0] not in mine]
+        await_(q, toks)
+
+    def note(tok, r_, w_):
+        for k in r_:
+            read.setdefault(k, []).append(tok)
+        for k in w_:
+            wrote.setdefault(k, []).append(tok)
+
+    def op(q, r_, w_, fn):
+        r_, w_ = r_.split(), w_.split()
+        deps(q, r_, w_)
+        s = queues[q][1]
+        total[s] = total.get(s, 0) + 1
+        fn(queues[q][0]).then_inc(sem[s], 1)
+        note((s, total[s]), r_, w_)
+
+    def dma(q, s, r_, w_, out, in_):
+        r_, w_ = r_.split(), w_.split()
+        deps(q, r_, w_, s)
+        total[s] = total.get(s, 0) + 16
+        queues[q][0].dma_start(out, in_).then_inc(sem[s], 16)
+        note((s, None), r_, w_)
+
+    def copy(r_, w_, out, in_, q="v", scale=1.0):
+        if q == "s":
+            op("s", r_, w_, (lambda e: e.activation(out, in_, F.Copy)) if scale == 1.0 else
+               (lambda e: e.activation(out, in_, F.Copy, scale=scale)))
+        else:
+            op(q, r_, w_, lambda e: e.tensor_copy(out, in_))
+
+    def ts(r_, w_, out, in0, s1, o0, s2=None, o1=None):
+        if o1 is None:
+            op("v", r_, w_, lambda e: e.tensor_scalar(out, in0, s1, None, o0))
+        else:
+            op("v", r_, w_, lambda e: e.tensor_scalar(out, in0, s1, s2, o0, o1))
+
+    def tt(r_, w_, out, a, b, o):
+        op("v", r_, w_, lambda e: e.tensor_tensor(out, a, b, o))
+
+    def fill(w_, ap, c):
+        op("v", "", w_, lambda e: e.memset(ap, c))
+
+    def turn(r_, w_, out, in_):
+        op("v", r_, w_, lambda e: e.transpose(out, in_))
+
+    def iota(w_, ap, pat, base, mult=0):
+        op("g", "", w_, lambda e: e.iota(ap, pat, base, mult, allow_small_or_imprecise_dtypes=True))
+
+    def count(r_, w_, out, in_, bias, acc):
+        op("s", r_, w_, lambda e: e.activation(out, in_, F.Sign, bias=bias, accum_out=acc))
+
+    def scan(r_, w_, out, a, b, init, o1):
+        op("v", r_, w_, lambda e: e.tensor_tensor_scan(out, a, b, init, A.add, o1))
+
+    def pick(deps_q, deps_s, w_q, w_s, oq, os_, iq, is_, off, off_key):
+        copy(deps_q + " " + off_key, w_q, oq.bitcast(dt.uint32), iq.bitcast(dt.uint32).indirect(off))
+        copy(deps_s + " " + off_key, w_s, os_, is_.indirect(off), q="s")
+
+    others = [c for c in T.cores if c != core]
+    engines = _split(core, others, topo)
+
+    def arrivals(s):
+        n = sum(len(_split(c, [b for b in T.cores if b != c], topo)[core]) for c in others)
+        total[s] = n
+        return (s, n)
+
+    def send(r_, s, src, dst):
+        deps("g", r_.split(), [])
+        tr = []
+        for c in others:
+            d = T.rank_of(c)
+            rid, pid = topo.addr(c)[:2]
+            m = 0
+            for e in engines[c]:
+                m |= 1 << e
+            tr.append(RemoteDMATransfer(dst_ids=[DstId(rid=rid, pnc=pid)], dma_engine_mask=m, remote_sem=sem[s],
+                                        src=src(d), dst=dst(r - (r > d))))
+            total["sent"] = total.get("sent", 0) + len(engines[c])
+        g.remote_dma_fused(tr, local_sem=sem.sent)
+
+    fill("nxrow", T.nxrow[:], 0)
+    for k in range(8):
+        dma("s", "dst", "", "stw", T.stw[16 * k:16 * k + 16, :], T.st[:])
+        dma("y", "dbt", "", "btw", T.btw[16 * k:16 * k + 16, :], T.bt[:])
+    for k in range(2):
+        dma("s", "dnw", "", "nxw", T.nxw[16 * k:16 * k + 16, :], T.nx[:])
+    dma("y", "dnx", "", "nxrow", T.nxrow[0:1, :], T.nx[:])
+    dma("y", "dx", "", "xt", T.xt[:], T.x[:])
+
+    ic, ict, cf, fw = T.ic, T.ict, T.cf, T.fw
+    iota("ic", ic[:, 0:32], [[0, 2], [512, 8], [0, 2]], 0)
+    iota("ic", ic[:, 32:64], [[8, 2], [0, 8], [128, 2]], 4, 1)
+    iota("ic", ic[:, 64:96], [[1, 2], [0, 16]], 0)
+    iota("ic", ic[:, 96:128], [[0, 2], [1, 16]], 0)
+    iota("ic", ic[:, 128:160], [[1, 32]], 0)
+    iota("kL", T.kL[:], [[16384, 208]], 0)
+    iota("ioL0", T.ioL[:, 0:256], [[1, 256]], 0)
+    iota("wab", T.wab[:], [[32, 20], [0, 2]], 0)
+    iota("cw0", T.cw0[:], [[16, 40]], 0)
+    turn("ic", "ict", ict[:], ic[:])
+    f = lambda j: cf[:, j:j + 1]
+    lo, odd, q15, q31 = (ict[:, j:j + 1] for j in (0, 64, 96, 128))
+    ts("ict", "hi", f(1), lo, 512.0, A.add)
+    ts("ict", "sb", f(2), ict[:, 32:33], -0.125, A.mult)
+    ts("ict", "sb", f(3), ict[:, 32:33], -0.125, A.mult, -2.0, A.add)
+    ts("ict", "nbc", f(4), lo, -2.0, A.mult, -16384.0 * 96, A.add)
+
+    o1 = T.o1
+    ts("btw", "b0", o1[:, 0:12], T.btw[:], 1, A.bitwise_and)
+    ts("stw", "e0", o1[:, 24:36], T.stw[:], 2, A.mult)
+    tt("e0 b0", "e1", o1[:, 36:48], o1[:, 24:36], o1[:, 0:12], A.add)
+    ts("e1", "e2", o1[:, 48:60], o1[:, 36:48], 1025, A.mult)
+    ts("e2", "e3", o1[:, 24:36], o1[:, 48:60], 4, A.arith_shift_right, 1023, A.bitwise_and)
+    copy("e3", "off1", T.off1[:], o1[:, 24:36])
+    copy("nxrow off1", "n1r", T.n1r[:], T.nxrow[:].indirect(T.off1[:]))
+    op("g", "n1r", "n1L", lambda e: e.partition_broadcast(T.n1L[:], T.n1r[0:1, :], 128))
+    copy("nxw", "nxf", T.nxf[0:32, :], T.nxw[0:32, :])
+    turn("nxf", "nxt", T.nxt[0:32, :], T.nxf[0:32, :])
+    for b in range(2):
+        dma("y", "dnl", "nxt", "nxlin", T.nxlin[0:1, 512 * b:512 * b + 512], T.nxt[0:32, 32 * b:32 * b + 16])
+    op("g", "nxlin", "nxl", lambda e: e.partition_broadcast(T.nxl[:, 0:1024], T.nxlin[0:1, :], 128))
+    iota("nxl", T.nxl[:, 1024:1032], [[0, 8]], N * TN)
+    ts("btw", "b1", o1[:, 12:24], T.btw[:], 1, A.arith_shift_right)
+    copy("b1", "b1u", T.b1u[:], o1[:, 12:24])
+    copy("ioL0 b1u", "b1L", T.b1L[:], T.ioL[:, 0:8].indirect(T.b1u[:]))
+    tt("b1L kL", "kb", T.kb[:], T.b1L[:], T.kL[:, 0:V], A.add)
+    ts("n1L ict", "ga", T.ga[:], T.n1L[:], lo, A.is_ge)
+    ts("n1L hi", "gb", T.gb[:], T.n1L[:], f(1), A.is_ge)
+    scan("ga gb", "c1L", T.c1L[:], T.ga[:], T.gb[:], 0.0, A.subtract)
+    copy("n1L", "a1", T.a1[:], T.n1L[:], q="s", scale=2.0)
+    for k in range(2):
+        count("c1L sb", "cnt1 sgx%d" % k, T["sg%d" % k][:], T.c1L[:], f(2 + k), T.cnt1[:, k:k + 1])
+    tt("a1 kb", "aL", T.aL[:, 0:V], T.a1[:], T.kb[:], A.add)
+    ts("ict", "nsc", f(5), lo, 2.0, A.mult, 1024.0, A.add)
+    ts("kL nsc", "aL", T.aL[:, V:208], T.kL[:, V:208], f(5), A.add)
+    ts("cnt1 nbc", "nb", T.nb[:], T.cnt1[:], 8192.0, A.mult, f(4), A.add)
+    op("s", "aL nb", "ab1", lambda e: e.activation(T.ab1[:], T.aL[:], F.Abs, bias=T.nb[:, 1:2]))
+    ts("aL nb", "sub0", T.sub0[:], T.aL[:], T.nb[:, 0:1], A.add)
+    ts("cnt1", "pk", T.pk[:], T.cnt1[:], -1024.0, A.mult, 2048.0 * (96 + V * r), A.add)
+    op("v", "sub0", "vv", lambda e: e.tensor_reduce(T.vv[:, 0:1], T.sub0[:], AxisListType.X, A.min, apply_absolute_value=True))
+    fill("x1", T.x1[:], 0.0)
+    op("v", "ab1", "vv", lambda e: e.tensor_reduce(T.vv[:, 1:2], T.ab1[:], AxisListType.X, A.min))
+    tt("pk vv", "x1", T.x1[:, 0:64:32], T.pk[:], T.vv[:], A.add)
+    turn("x1", "x1t", T.x1t[:], T.x1[:])
+    for k in range(8):
+        dma("y" if k % 2 else "s", "dc1", "x1t", "w1", T.w1[16 * k:16 * k + 16, :], T.x1t[0:128:32, :])
+    send("w1", "al1", lambda d: T.w1[:, 2 * d:2 * d + 2], lambda j: T.land1[:, 2 * j:2 * j + 2])
+
+    ts("wab ict", "wac", T.wac[:], T.wab[:], q31, A.add)
+    copy("n1L wac", "own", T.own[:], T.n1L[:].indirect(T.wac[:, 0:12]), q="s")
+    ts("cw0 ict", "cw", T.cw[:], T.cw0[:], q15, A.add)
+    ts("ict", "even", f(6), odd, -1.0, A.mult, 1.0, A.add)
+    ts("cw", "dw", T.dw[:], T.cw[:], float(KEYS), A.add)
+    ts("cw", "kw", fw[:, 0:12], T.cw[:, 0:12], float(V * r), A.add)
+    copy("stw", "stu", T.stu[:], T.stw[:])
+    op("v", "xt", "xq xs", lambda e: e.quantize_mx(T.xq[:], T.xs[:], T.xt[:]))
+    pick("xq", "xs", "stq", "sts", T.stq[:], T.sts[:], T.xq[:], T.xs[:], T.stu[:], "stu")
+    turn("own", "ownt", T.ownt[:], T.own[:])
+    copy("w1", "w1i", T.w1i[:], T.w1[:])
+    ts("w1i", "w1k", T.w1k[:], T.w1i[:], 11, A.arith_shift_right)
+    ts("w1k", "s1off", T.s1off[:], T.w1k[:], -V * r, A.add, V - 1, A.min)
+    pick("stq", "sts", "p1q", "p1s", T.p1q[:], T.p1s[:], T.stq[:], T.sts[:], T.s1off[:], "s1off")
+    send("p1q", "aq1", lambda d: T.p1q[:, CAP * d:CAP * d + CAP].bitcast(dt.uint8),
+         lambda j: T.cq[:, V + CAP * j:V + CAP * j + CAP].bitcast(dt.uint8))
+    send("p1s", "as1", lambda d: T.p1s[:, CAP * d:CAP * d + CAP], lambda j: T.cs[:, V + CAP * j:V + CAP * j + CAP])
+    dma("y", "dcq", "stq", "cq0", T.cq[:, 0:V].bitcast(dt.uint8), T.stq[:].bitcast(dt.uint8))
+    dma("y", "dcq", "sts", "cs0", T.cs[:, 0:V], T.sts[:])
+    dma("y", "dw_", "", "wt", T.wt[:], T.w[:])
+    iota("keyL", T.keyL[:, 0:V], [[1, V]], V * r)
+    iota("infoX", T.infoL[:, CAND:CX], [[1, CAP]], KEYS + CAND + CAP * r)
+    iota("ioL", T.ioL[:, 256:KW], [[1, KW - 256]], 256)
+    iota("ones", T.ones[:], [[0, CAND]], 1)
+    iota("sT", T.sT[:, 0:KEYS], [[1, 8], [0, V]], 0)
+    iota("sT", T.sT[:, KEYS:KW], [[0, 8]], 0)
+    iota("iT", T.iT[:, KEYS:KW], [[0, 8]], 0)
+    ow = T.ow
+    copy("ownt", "n1w", ow[:, 0:12], T.ownt[:, 0:V:16])
+    ts("n1w", "oc", ow[:, 12:24], ow[:, 0:12], 511, A.bitwise_and)
+    ts("n1w", "oa", ow[:, 24:36], ow[:, 0:12], 9, A.arith_shift_right)
+    ts("oc", "od", ow[:, 36:48], ow[:, 12:24], 2, A.mult)
+    ts("oa", "of", ow[:, 48:60], ow[:, 24:36], r, A.not_equal, 2048, A.mult)
+    tt("od b1", "oe", ow[:, 60:72], ow[:, 36:48], o1[:, 12:24], A.add)
+    copy("oc", "c1u0", T.c1u[:, 0:12], ow[:, 12:24])
+    tt("oe of", "og", ow[:, 72:84], ow[:, 60:72], ow[:, 48:60], A.add)
+    ts("og", "noff0", T.noff[:, 0:12], ow[:, 72:84], 1024, A.min)
+    copy("nxl noff0", "n2L0", T.n2L[:, 0:V], T.nxl[:].indirect(T.noff[:, 0:12]))
+    ts("n2L0 ict", "g2a0", T.g2a[:, 0:V], T.n2L[:, 0:V], lo, A.is_ge)
+    ts("n2L0 hi", "g2b0", T.g2b[:, 0:V], T.n2L[:, 0:V], f(1), A.is_ge)
+    scan("g2a0 g2b0", "c2L0", T.c2L[:, 0:V], T.g2a[:, 0:V], T.g2b[:, 0:V], 0.0, A.subtract)
+    for k in range(2):
+        count("c2L0 sb", "cnt2o sgy%d" % k, T["sg%d" % (2 + k)][:, 0:V], T.c2L[:, 0:V], f(2 + k), T.cnt2[:, k:k + 1])
+    copy("n2L0", "inf00", T.inf0[:, 0:V], T.n2L[:, 0:V], q="s", scale=4096.0)
+    fill("x2", T.x2[:], 0.0)
+
+    wrote["land1"] = [arrivals("al1")]
+    wrote["cqa"] = [arrivals("aq1")]
+    wrote["csa"] = [arrivals("as1")]
+    l1 = T.l1
+    copy("land1", "l1", l1[:, 0:14], T.land1[:])
+    ts("l1", "la", l1[:, 14:28], l1[:, 0:14], 2047, A.bitwise_and)
+    copy("la", "noff1", T.noff[:, 12:26], l1[:, 14:28])
+    copy("nxl noff1", "n2L1", T.n2L[:, V:CAND], T.nxl[:].indirect(T.noff[:, 12:26]))
+    ts("n2L1 ict", "g2a1", T.g2a[:, V:CAND], T.n2L[:, V:CAND], lo, A.is_ge)
+    ts("n2L1 hi", "g2b1", T.g2b[:, V:CAND], T.n2L[:, V:CAND], f(1), A.is_ge)
+    scan("g2a1 g2b1 c2L0", "c2L1", T.c2L[:, V:CAND], T.g2a[:, V:CAND], T.g2b[:, V:CAND], T.c2L[:, V - 1:V], A.subtract)
+    ts("ioL0 c2L1", "c2L2", T.c2L[:, CAND:CX], T.ioL[:, 1:1 + CAP], T.c2L[:, CAND - 1:CAND], A.add)
+    for k in range(2):
+        count("c2L1 c2L2 sb", "cnt2a sgz%d" % k, T["sg%d" % (2 + k)][:, V:CX], T.c2L[:, V:CX], f(2 + k), T.cnt2[:, 4 + k:5 + k])
+    ts("cnt2o", "cnt2h", T.cnt2[:, 2:4], T.cnt2[:, 0:2], -0.5, A.mult, CX / 2.0, A.add)
+    ts("l1", "lk", l1[:, 28:42], l1[:, 0:14], 11, A.arith_shift_right)
+    ts("l1", "le", l1[:, 42:56], l1[:, 0:14], 1, A.arith_shift_right, 511, A.bitwise_and)
+    copy("lk", "ku1", T.ku1[:], l1[:, 28:42])
+    ts("cnt2a", "cnt2b", T.cnt2[:, 6:8], T.cnt2[:, 4:6], -0.5, A.mult)
+    tt("cnt2b cnt2h", "x2", T.x2[:, 0:64:32], T.cnt2[:, 6:8], T.cnt2[:, 2:4], A.add)
+    turn("x2", "x2t", T.x2t[:], T.x2[:])
+    for k in range(8):
+        dma("y" if k % 2 else "s", "dc2", "x2t", "w2", T.w2[16 * k:16 * k + 16, :], T.x2t[0:128:32, :])
+    copy("n2L1", "inf01", T.inf0[:, V:CAND], T.n2L[:, V:CAND], q="s", scale=4096.0)
+    copy("ioL0 ioL ku1", "keyL1", T.keyL[:, V:CAND], T.ioL[:].indirect(T.ku1[:]), q="s")
+    tt("inf00 keyL", "info0", T.infoL[:, 0:V], T.inf0[:, 0:V], T.keyL[:, 0:V], A.add)
+    copy("le", "c1u1", T.c1u[:, 12:26], l1[:, 42:56])
+    tt("inf01 keyL1", "info1", T.infoL[:, V:CAND], T.inf0[:, V:CAND], T.keyL[:, V:CAND], A.add)
+    pick("xq", "xs", "cq1", "cs1", T.cq[:, CAND:2 * CAND], T.cs[:, CAND:2 * CAND], T.xq[:], T.xs[:], T.c1u[:], "c1u0 c1u1")
+    copy("w2", "w2u", T.w2u[:], T.w2[:])
+    copy("info0 info1 infoX w2u", "ig", T.ig[:], T.infoL[:].indirect(T.w2u[:]))
+    copy("ig wac", "ig2", T.ig2[:], T.ig[:].indirect(T.wac[:, 0:16]))
+    turn("ig2", "igt", T.igt[:], T.ig2[:])
+    copy("igt", "l2s", T.l2s[:], T.igt[:, 0:256:16])
+    send("l2s", "al2", lambda d: T.l2s[:, 2 * d:2 * d + 2], lambda j: T.land2[:, 2 * j:2 * j + 2])
+    ts("w2", "o2off", T.o2off[:, 0:32:2], T.w2[:], CAND - 1.0, A.min)
+    ts("w2", "o2off", T.o2off[:, 1:32:2], T.w2[:], CAND - 1.0, A.min, float(CAND), A.add)
+    pick("cq0 cq1 cqa", "cs0 cs1 csa", "p2q", "p2s", T.p2q[:], T.p2s[:], T.cq[:], T.cs[:], T.o2off[:], "o2off")
+    send("p2q", "aq2", lambda d: T.p2q[:, 64 * d:64 * d + 64].bitcast(dt.uint8),
+         lambda j: T.eq[:, 64 * j:64 * j + 64].bitcast(dt.uint8))
+    send("p2s", "as2", lambda d: T.p2s[:, 64 * d:64 * d + 64], lambda j: T.es[:, 64 * j:64 * j + 64])
+    iota("pp", T.pp[:, KEYS:KEYS + TAIL], [[1, TAIL]], M + 1)
+    iota("yx", T.yx[:, 0:CAND], [[1, CAND]], 0)
+    iota("yx", T.yx[:, CAND:ALL], [[32, 14], [1, 16]], CAND)
+    iota("inv", T.inv[:, 0:M], [[0, M]], YZ)
+    iota("iT", T.iT[:, 0:KEYS], [[0, 8], [1, V]], 0)
+    for o in range(2):
+        iota("ybz%d" % o, T["yb%d" % o][:, YZ:YZ + 8], [[0, 8]], 0)
+    iota("sW", T.sW[:, 0:V], [[0, V]], r)
+    iota("iW", T.iW[:, 0:V], [[1, V]], 0)
+    iota("sW", T.sW[:, YZ:YZ + 8], [[0, 8]], -1)
+    iota("iW", T.iW[:, YZ:YZ + 8], [[0, 8]], -1)
+
+    n2w, xx = T.n2w, T.xx
+    copy("n2L0 n2L1 wac", "n2g", T.n2g[:], T.n2L[:].indirect(T.wac[:, 0:26]), q="s")
+    copy("ioL0 ioL", "bm", T.bm[:, 0:KEYS], T.ioL[:, 0:KEYS], q="s", scale=0.0)
+    copy("lk", "kw", fw[:, 12:26], l1[:, 28:42])
+    turn("n2g", "n2t", T.n2t[:], T.n2g[:])
+    copy("n2t", "n2w", n2w[:, 0:26], T.n2t[:, 0:CAND:16])
+    ts("n2w", "n2e", n2w[:, 52:78], n2w[:, 0:26], 9, A.arith_shift_right)
+    ts("n2w", "n2c", n2w[:, 26:52], n2w[:, 0:26], 511, A.bitwise_and)
+    ts("n2e", "bad", fw[:, 26:52], n2w[:, 52:78], r, A.not_equal)
+    copy("n2c", "c2u", T.c2u[:], n2w[:, 26:52])
+    tt("bad dw", "badd", fw[:, 52:78], fw[:, 26:52], T.dw[:, 0:26], A.mult)
+    pick("xq", "xs", "n2q", "n2s", T.n2q[:], T.n2s[:], T.xq[:], T.xs[:], T.c2u[:], "c2u")
+    tt("kw badd", "ko", T.ko[:], fw[:, 0:26], fw[:, 52:78], A.max)
+    op("v", "wt", "wq0 ws0", lambda e: e.quantize_mx(T.wq[:, 0:384], T.ws[:, 0:384], T.wt[:, 0:1536]))
+    copy("ko", "kou0", T.kou[:, 0:26], T.ko[:])
+    op("v", "wt", "wq1 ws1", lambda e: e.quantize_mx(T.wq[:, 384:768], T.ws[:, 384:768], T.wt[:, 1536:3072]))
+    op("v", "kou0 ones", "bm", lambda e: e.tensor_copy(T.bm[:].indirect(T.kou[:, 0:26]), T.ones[:]))
+    ts("ko even", "qa", xx[:, 0:13], T.ko[:, 0:26:2], f(6), A.mult)
+    ts("ko ict", "qb", xx[:, 13:26], T.ko[:, 1:26:2], odd, A.mult)
+    tt("qa qb", "qc", xx[:, 26:39], xx[:, 0:13], xx[:, 13:26], A.add)
+    copy("qc", "pwa", T.pwa[:, 0:26:2], xx[:, 26:39])
+    copy("qc", "pwa", T.pwa[:, 1:26:2], xx[:, 26:39])
+
+    W = lambda k, o: (T.wq[:, 128 * (2 * k + o):128 * (2 * k + o) + 128], T.ws[:, 128 * (2 * k + o):128 * (2 * k + o) + 128])
+
+    def mm(r_, w_, bank, n, k, o, q, s, a, b):
+        wq, ws = W(k, o)
+        op("t", r_ + " wq0 ws0 wq1 ws1", w_, lambda e: e.matmul_mx(T.ps[:, 512 * bank:512 * bank + n], wq, ws, q, s, a, b))
+
+    for o in range(2):
+        mm("cq0 cqa cs0 csa", "psS%d" % o, o, CAND, 0, o, T.cq[:, 0:CAND], T.cs[:, 0:CAND], True, False)
+        mm("cq1 cs1", "psS%d" % o, o, CAND, 1, o, T.cq[:, CAND:2 * CAND], T.cs[:, CAND:2 * CAND], False, False)
+        mm("n2q n2s", "psS%d" % o, o, CAND, 2, o, T.n2q[:], T.n2s[:], False, True)
+
+    wrote["land2"] = [arrivals("al2")]
+    wrote["eqa"] = [arrivals("aq2")]
+    wrote["esa"] = [arrivals("as2")]
+    l2 = T.l2i
+    copy("land2", "m0", l2[:, 0:14], T.land2[:])
+    ts("m0", "m1", l2[:, 14:28], l2[:, 0:14], 4095, A.bitwise_and)
+    copy("m1", "kou1", T.kou[:, 26:40], l2[:, 14:28])
+    op("v", "kou1 ones", "bm", lambda e: e.tensor_copy(T.bm[:].indirect(T.kou[:, 26:40]), T.ones[:, 0:ARR]))
+    ts("m0", "m2", l2[:, 28:42], l2[:, 0:14], 12, A.arith_shift_right, 511, A.bitwise_and)
+    ts("m1 even", "qd", xx[:, 39:46], l2[:, 14:28:2], f(6), A.mult)
+    ts("m1 ict", "qe", xx[:, 46:53], l2[:, 15:28:2], odd, A.mult)
+    scan("bm", "pp", T.pp[:, 0:KEYS], T.bm[:, 0:KEYS], T.bm[:, 0:KEYS], 0.0, A.max)
+    tt("qd qe", "qf", xx[:, 53:60], xx[:, 39:46], xx[:, 46:53], A.add)
+    copy("m2", "c2ua", T.c2ua[:, 0:28:2], l2[:, 28:42])
+    copy("qf", "pwb", T.pwa[:, 26:40:2], xx[:, 53:60])
+    copy("qf", "pwb", T.pwa[:, 27:40:2], xx[:, 53:60])
+    copy("m2", "c2ua", T.c2ua[:, 1:28:2], l2[:, 28:42])
+    copy("pp pwa", "pg0", T.pg[:, 0:320], T.pp[:].indirect(T.pwa[:, 0:20]))
+    copy("pp pwa pwb", "pg1", T.pg[:, 320:ALL], T.pp[:].indirect(T.pwa[:, 20:40]), q="s")
+    turn("pg0", "pt0", T.pt[:, 0:320], T.pg[:, 0:320])
+    ts("m1", "ku2", T.ku2[:, 0:28:2], l2[:, 14:28], KEYS - 1, A.min)
+    ts("m1", "ku2", T.ku2[:, 1:28:2], l2[:, 14:28], KEYS - 1, A.min)
+    turn("pg1", "pt1", T.pt[:, 320:ALL], T.pg[:, 320:ALL])
+    ts("pt0 pt1", "plu", T.plu[:], T.pt[:, 0:ALL:16], -1.0, A.add)
+    pick("xq", "xs", "fq", "fs", T.fq[:], T.fs[:], T.xq[:], T.xs[:], T.c2ua[:, 0:27], "c2ua")
+    op("v", "plu yx", "inv", lambda e: e.tensor_copy(T.inv[:].indirect(T.plu[:]), T.yx[:]))
+    copy("inv wac", "ivg", T.ivg[:], T.inv[:, 0:M].indirect(T.wac[:, 0:18]))
+    turn("ivg", "ivt", T.ivt[:], T.ivg[:])
+    copy("ivt", "ylu", T.ylu[:], T.ivt[:, 0:M:16])
+    for o in range(2):
+        mm("fq fs", "psA%d" % o, 2 + o, SPREAD, 2, o, T.fq[:], T.fs[:], True, False)
+    for o in range(2):
+        copy("psS%d" % o, "yb%d" % o, T["yb%d" % o][:, 0:CAND], T.ps[:, 512 * o:512 * o + CAND], q="s")
+    for t_, w_ in (("sT", "sW"), ("iT", "iW")):
+        copy(t_ + " ku1", w_, T[w_][:, V:CAND], T[t_][:].indirect(T.ku1[:]), q="s")
+        copy(t_ + " ku2", w_, T[w_][:, CAND:YZ], T[t_][:].indirect(T.ku2[:, 0:27]), q="s")
+    for o in range(2):
+        mm("eqa esa", "psA%d" % o, 2 + o, SPREAD, 0, o, T.eq[:, 0:SPREAD], T.es[:, 0:SPREAD], False, False)
+        mm("eqa esa", "psA%d" % o, 2 + o, SPREAD, 1, o, T.eq[:, 16:16 + SPREAD], T.es[:, 16:16 + SPREAD], False, True)
+    copy("psA0", "yb0", T.yb0[:, CAND:YZ], T.ps[:, 1024:1024 + SPREAD], q="s")
+    copy("psA1", "yb1", T.yb1[:, CAND:YZ], T.ps[:, 1536:1536 + SPREAD], q="s")
+    copy("yb0 ybz0 ylu", "yo0", T.yo0[:], T.yb0[:].indirect(T.ylu[:]))
+    dma("y", "dy0", "yo0", "y0", T.y[:, 0:M], T.yo0[:])
+    copy("yb1 ybz1 ylu", "yo1", T.yo1[:], T.yb1[:].indirect(T.ylu[:]), q="s")
+    dma("s", "dy1", "yo1", "y1", T.y[:, M:2 * M], T.yo1[:])
+    copy("sW ylu", "ids", T.ids[:], T.sW[:].indirect(T.ylu[:]))
+    dma("y", "did", "ids", "id0", T["id"][0:1, :], T.ids[0:1, :])
+    copy("iW ylu", "idi", T.idi[:], T.iW[:].indirect(T.ylu[:]), q="s")
+    dma("s", "did2", "idi", "id1", T["id"][1:2, :], T.idi[0:1, :])
+    await_("g", [(s, None) for s in total])

@@ -2,16 +2,10 @@ from concourse.bass import DstId, RemoteDMATransfer
 from concourse.mybir import dt, AluOpType as A, AxisListType, ActivationFunctionType as F
 
 N = 8
-TN, V, M, KEYS = 512, 192, 288, 1536
-CAP = 32
-ARR = (N - 1) * CAP
-CAND = V + ARR
-CX = CAND + CAP
-ALL = CAND + ARR
-TAIL = CAND + N * CAP
-SPREAD = 2 * ARR - 16
-YZ = CAND + SPREAD
-KW = 1544
+TN, V, M, CAP = 512, 192, 288, 32
+A2, XB, A1, SB, QW = 16, 528, 1072, 1328, 1520
+RB = 224
+ML = 25
 X4 = "float8_e4m3fn_x4"
 
 
@@ -20,54 +14,58 @@ def _sb(n, d="float32"):
 
 
 SCRATCH = {
-    "stw": _sb(12, "int32"), "btw": _sb(12, "int32"), "nxrow": _sb(1024, "int32"), "nxw": _sb(64, "int32"), "nxf": _sb(64),
-    "nxt": _sb(64), "nxlin": _sb(1024), "nxl": _sb(1032), "xt": _sb(2048, "bfloat16"), "wt": _sb(3072, "bfloat16"),
-    "ic": _sb(160), "ict": _sb(160), "cf": _sb(16), "ioL": _sb(KW), "kL": _sb(208), "wab": _sb(40, "int32"), "cw0": _sb(40),
-    "wac": _sb(40, "uint16"), "cw": _sb(40), "dw": _sb(40), "yx": _sb(ALL), "sT": _sb(KW), "iT": _sb(KW),
-    "o1": _sb(64, "int32"), "off1": _sb(12, "uint16"), "b1u": _sb(12, "uint16"), "stu": _sb(12, "uint16"),
-    "n1r": _sb(V), "n1L": _sb(V), "b1L": _sb(V), "kb": _sb(V), "a1": _sb(V), "aL": _sb(208),
-    "ga": _sb(V), "gb": _sb(V), "c1L": _sb(V), "sg0": _sb(V), "sg1": _sb(V), "sg2": _sb(CX), "sg3": _sb(CX),
-    "cnt1": _sb(2), "nb": _sb(2), "sub0": _sb(208), "ab1": _sb(208), "vv": _sb(2), "pk": _sb(2),
-    "x1": _sb(64), "x1t": _sb(64), "w1": _sb(16), "w1i": _sb(16, "int32"), "w1k": _sb(16, "int32"),
-    "s1off": _sb(16, "uint16"), "land1": _sb(14),
-    "own": _sb(V), "ownt": _sb(V), "ow": _sb(96, "int32"), "noff": _sb(26, "uint16"), "c1u": _sb(26, "uint16"),
-    "n2L": _sb(CAND), "g2a": _sb(CAND), "g2b": _sb(CAND), "c2L": _sb(CX), "l1": _sb(64, "int32"),
-    "cnt2": _sb(8), "x2": _sb(64), "x2t": _sb(64), "w2": _sb(16), "o2off": _sb(32, "uint16"), "w2u": _sb(16, "uint16"),
-    "ku1": _sb(14, "uint16"), "keyL": _sb(CAND), "inf0": _sb(CAND), "infoL": _sb(CX),
-    "ig": _sb(256), "ig2": _sb(256), "igt": _sb(256), "l2s": _sb(16), "land2": _sb(14),
-    "n2g": _sb(CAND), "n2t": _sb(CAND), "n2w": _sb(80, "int32"), "c2u": _sb(26, "uint16"), "fw": _sb(120), "xx": _sb(60),
-    "ko": _sb(26), "kou": _sb(40, "uint16"), "pwa": _sb(40, "uint16"), "ones": _sb(CAND), "bm": _sb(KEYS + TAIL), "pp": _sb(KEYS + TAIL),
-    "l2i": _sb(64, "int32"), "c2ua": _sb(28, "uint16"), "ku2": _sb(28, "uint16"), "sW": _sb(YZ + 8), "iW": _sb(YZ + 8),
-    "pg": _sb(ALL), "pt": _sb(ALL), "plu": _sb(40, "uint16"), "inv": _sb(M + TAIL),
-    "ivg": _sb(M), "ivt": _sb(M), "ylu": _sb(18, "uint16"), "ids": _sb(M), "idi": _sb(M),
-    "xq": _sb(TN, X4), "xs": _sb(TN, "uint8"), "wq": _sb(768, X4), "ws": _sb(768, "uint8"),
+    "stw": _sb(12, "int32"), "btw": _sb(12, "int32"), "nxrow": _sb(1024, "int32"), "nxw": _sb(32, "int32"), "nxf": _sb(32),
+    "nxt": _sb(32), "nxl": _sb(1040), "xt": _sb(2080, "bfloat16"), "wt": _sb(3072, "bfloat16"),
+    "ic": _sb(320), "ict": _sb(320), "cf": _sb(16), "ioL": _sb(1536), "wa": _sb(QW), "cl": _sb(32, "uint16"), "rl": _sb(12),
+    "cdest": _sb(V), "keep": _sb(V), "ci": _sb(V), "iw": _sb(64), "iw2": _sb(32), "ie": _sb(48), "mk": _sb(32),
+    "o1": _sb(64, "int32"), "off1": _sb(12, "uint16"), "stu": _sb(12, "uint16"), "b1s": _sb(16),
+    "n1r": _sb(V), "n1t": _sb(V), "jf": _sb(6), "m1": _sb(6, "uint16"), "land1": _sb(48, "uint16"), "di": _sb(8, "int32"),
+    "f1": _sb(V, "bfloat16"), "f1t": _sb(V, "bfloat16"), "c1L": _sb(V, "bfloat16"), "sg": _sb(2 * V, "bfloat16"), "cnt1": _sb(2),
+    "x1": _sb(64), "x1t": _sb(64), "w1": _sb(16), "s1off": _sb(16, "uint16"),
+    "zf": _sb(48), "off2": _sb(16, "uint16"), "c1u": _sb(12, "uint16"), "n2r": _sb(V), "n2t": _sb(V), "xo": _sb(12, "uint16"),
+    "fl": _sb(V), "junk": _sb(V), "tot": _sb(2), "px": _sb(96), "pxt": _sb(96), "init": _sb(1), "cnt": _sb(V), "val": _sb(V),
+    "vt": _sb(V), "seg": _sb(V), "c0u": _sb(12, "uint16"), "t1": _sb(V), "vals": _sb(V), "m2": _sb(26, "uint16"),
+    "land2": _sb(N * ML, "uint16"), "tab2": _sb(RB + 272), "y2": _sb(544), "g2": _sb(64), "r2": _sb(64), "p2off": _sb(32, "uint16"),
+    "mi": _sb(32, "int32"), "kk": _sb(96), "z2": _sb(N * ML), "zz": _sb(176), "bsum": _sb(1), "xe": _sb(12, "uint16"),
+    "fe": _sb(V), "pe": _sb(V), "pt": _sb(V), "po": _sb(12, "uint16"), "d0u": _sb(12, "uint16"), "d1u": _sb(12, "uint16"),
+    "x3": _sb(V), "x3t": _sb(V), "t3": _sb(V), "v3": _sb(V), "v4": _sb(V), "tab3": _sb(RB + M + 16), "y3": _sb(608),
+    "g3": _sb(160), "r3": _sb(160), "fo": _sb(54, "uint16"), "ki": _sb(64, "int32"), "x5": _sb(64), "x5t": _sb(64),
+    "q0": _sb(TN + 8, X4), "s0": _sb(TN + 8, "uint8"), "wq": _sb(768, X4), "ws": _sb(768, "uint8"),
     "stq": _sb(V, X4), "sts": _sb(V, "uint8"), "p1q": _sb(256, X4), "p1s": _sb(256, "uint8"),
-    "cq": _sb(2 * CAND, X4), "cs": _sb(2 * CAND, "uint8"), "n2q": _sb(CAND, X4), "n2s": _sb(CAND, "uint8"),
-    "p2q": _sb(512, X4), "p2s": _sb(512, "uint8"), "eq": _sb(2 * ARR, X4), "es": _sb(2 * ARR, "uint8"),
-    "fq": _sb(SPREAD, X4), "fs": _sb(SPREAD, "uint8"),
-    "yb0": _sb(YZ + 8), "yb1": _sb(YZ + 8), "yo0": _sb(M), "yo1": _sb(M),
-    "ps": ("psum", [128, 2048], "float32"),
+    "q1": _sb(QW, X4), "s1": _sb(QW, "uint8"), "p2q": _sb(512, X4), "p2s": _sb(512, "uint8"),
+    "q2": _sb(QW, X4), "s2": _sb(QW, "uint8"), "fq": _sb(3 * M, X4), "fs": _sb(3 * M, "uint8"),
+    "yo0": _sb(M), "yo1": _sb(M), "ps": ("psum", [128, 1024], "float32"),
 }
-SEMAPHORES = ["cv", "cs_", "ct", "cg", "dst", "dbt", "dnx", "dnw", "dnl", "dx", "dw_", "dcq", "dc1", "dc2", "dy0", "dy1", "did",
-              "did2", "sent", "al1", "aq1", "as1", "al2", "aq2", "as2"]
+SEMAPHORES = ["cv", "cs_", "ct", "cg", "dst", "dbt", "dnx", "dnw", "dnl", "dx", "dw0", "dw1", "dc1", "dm1", "dm2", "dq1", "dq2", "dq3",
+              "dy0", "dy1", "did", "sent", "al1", "aq1", "as1", "al2", "aq2", "as2"]
 
 
-def _split(core, others, topo):
+def _parts(core, others, topo):
     own = topo.cores_of(core)
     far = [c for c in others if c not in own]
     near = [c for c in others if c in own]
-    out, taken = {}, []
+    out, taken = [], []
     for part in (far, near):
-        if not part:
-            continue
-        free = [e for e in topo.engines(core, part[0]) if e not in taken]
+        if part:
+            free = [e for e in topo.engines(core, part[0]) if e not in taken]
+            out.append((part, free))
+            taken += free
+    return out
+
+
+def _split(core, others, topo):
+    out = {}
+    for part, free in _parts(core, others, topo):
         k = 1
         while 2 * k * len(part) <= len(free):
             k *= 2
         for j, c in enumerate(part):
             out[c] = free[j * k:(j + 1) * k]
-            taken += out[c]
     return out
+
+
+def _mask(engines):
+    return sum(1 << e for e in engines)
 
 
 def rank_program(g, core, T, topo):
@@ -93,7 +91,7 @@ def rank_program(g, core, T, topo):
         mine = (queues[q][1], own)
         toks = []
         for k in r_:
-            toks += wrote.get(k, [])
+            toks += wrote[k]
         for k in w_:
             toks += [t for t in wrote.get(k, []) + read.get(k, []) if t[0] not in mine]
         await_(q, toks)
@@ -119,12 +117,11 @@ def rank_program(g, core, T, topo):
         queues[q][0].dma_start(out, in_).then_inc(sem[s], 16)
         note((s, None), r_, w_)
 
-    def copy(r_, w_, out, in_, q="v", scale=1.0):
-        if q == "s":
-            op("s", r_, w_, (lambda e: e.activation(out, in_, F.Copy)) if scale == 1.0 else
-               (lambda e: e.activation(out, in_, F.Copy, scale=scale)))
-        else:
-            op(q, r_, w_, lambda e: e.tensor_copy(out, in_))
+    def copy(r_, w_, out, in_):
+        op("v", r_, w_, lambda e: e.tensor_copy(out, in_))
+
+    def act(r_, w_, out, in_, fn=F.Copy, **k):
+        op("s", r_, w_, lambda e: e.activation(out, in_, fn, **k))
 
     def ts(r_, w_, out, in0, s1, o0, s2=None, o1=None):
         if o1 is None:
@@ -141,289 +138,277 @@ def rank_program(g, core, T, topo):
     def turn(r_, w_, out, in_):
         op("v", r_, w_, lambda e: e.transpose(out, in_))
 
-    def iota(w_, ap, pat, base, mult=0):
-        op("g", "", w_, lambda e: e.iota(ap, pat, base, mult, allow_small_or_imprecise_dtypes=True))
+    def iota(w_, ap, pat, base, mult=0, after=""):
+        op("g", after, w_, lambda e: e.iota(ap, pat, base, mult, allow_small_or_imprecise_dtypes=True))
 
-    def count(r_, w_, out, in_, bias, acc):
-        op("s", r_, w_, lambda e: e.activation(out, in_, F.Sign, bias=bias, accum_out=acc))
+    def scan(r_, w_, out, a, b, init, o0, o1):
+        op("v", r_, w_, lambda e: e.tensor_tensor_scan(out, a, b, init, o0, o1))
 
-    def scan(r_, w_, out, a, b, init, o1):
-        op("v", r_, w_, lambda e: e.tensor_tensor_scan(out, a, b, init, A.add, o1))
+    def summed(r_, w_, out, in_):
+        op("v", r_, w_, lambda e: e.tensor_reduce(out, in_, AxisListType.X, A.add))
+
+    def quant(r_, w_, q, s, in_):
+        op("v", r_, w_, lambda e: e.quantize_mx(q, s, in_))
 
     def pick(deps_q, deps_s, w_q, w_s, oq, os_, iq, is_, off, off_key):
         copy(deps_q + " " + off_key, w_q, oq.bitcast(dt.uint32), iq.bitcast(dt.uint32).indirect(off))
-        copy(deps_s + " " + off_key, w_s, os_, is_.indirect(off), q="s")
+        act(deps_s + " " + off_key, w_s, os_, is_.indirect(off))
+
+    def move(q, s, r_q, r_s, w_, dq, ds, a, sq, ss, b, n):
+        dma(q, s, r_q, w_, dq[:, a:a + n].bitcast(dt.uint8), sq[:, b:b + n].bitcast(dt.uint8))
+        dma(q, s, r_s, w_, ds[:, a:a + n], ss[:, b:b + n])
 
     others = [c for c in T.cores if c != core]
-    engines = _split(core, others, topo)
+    rest = lambda c: [b for b in T.cores if b != c]
+    place = lambda c: DstId(rid=topo.addr(c)[0], pnc=topo.addr(c)[1])
 
-    def arrivals(s):
-        n = sum(len(_split(c, [b for b in T.cores if b != c], topo)[core]) for c in others)
-        total[s] = n
-        return (s, n)
-
-    def send(r_, s, src, dst):
+    def send(r_, s, w_, src, dst):
         deps("g", r_.split(), [])
-        tr = []
-        for c in others:
-            d = T.rank_of(c)
-            rid, pid = topo.addr(c)[:2]
-            m = 0
-            for e in engines[c]:
-                m |= 1 << e
-            tr.append(RemoteDMATransfer(dst_ids=[DstId(rid=rid, pnc=pid)], dma_engine_mask=m, remote_sem=sem[s],
-                                        src=src(d), dst=dst(r - (r > d))))
-            total["sent"] = total.get("sent", 0) + len(engines[c])
-        g.remote_dma_fused(tr, local_sem=sem.sent)
+        engines = _split(core, others, topo)
+        g.remote_dma_fused([RemoteDMATransfer(dst_ids=[place(c)], dma_engine_mask=_mask(engines[c]), remote_sem=sem[s],
+                                              src=src(T.rank_of(c)), dst=dst) for c in others], local_sem=sem.sent)
+        total["sent"] = total.get("sent", 0) + sum(len(engines[c]) for c in others)
+        total[s] = sum(len(_split(c, rest(c), topo)[core]) for c in others)
+        wrote.setdefault(w_, []).append((s, total[s]))
+
+    def spread(r_, s, w_, src, dst):
+        deps("g", r_.split(), [])
+        parts = _parts(core, others, topo)
+        g.remote_dma_fused([RemoteDMATransfer(dst_ids=[place(c) for c in part], dma_engine_mask=_mask(free), remote_sem=sem[s],
+                                              srcs=[src], dsts=[dst] * len(part)) for part, free in parts], local_sem=sem.sent)
+        total["sent"] = total.get("sent", 0) + sum(len(free) for part, free in parts)
+        total[s] = sum(len(free) for c in others for part, free in _parts(c, rest(c), topo) if core in part)
+        wrote.setdefault(w_, []).append((s, total[s]))
 
     fill("nxrow", T.nxrow[:], 0)
     for k in range(8):
         dma("s", "dst", "", "stw", T.stw[16 * k:16 * k + 16, :], T.st[:])
         dma("y", "dbt", "", "btw", T.btw[16 * k:16 * k + 16, :], T.bt[:])
-    for k in range(2):
-        dma("s", "dnw", "", "nxw", T.nxw[16 * k:16 * k + 16, :], T.nx[:])
-    dma("y", "dnx", "", "nxrow", T.nxrow[0:1, :], T.nx[:])
-    dma("y", "dx", "", "xt", T.xt[:], T.x[:])
+    for k in range(4):
+        dma("s", "dnw", "", "nxw", T.nxw[16 * k:16 * k + 16, :], T.nx[:, 32 * (k // 2):32 * (k // 2) + 32])
+        dma("y", "dnx", "", "nxrow", T.nxrow[32 * k:32 * k + 1, :], T.nx[:])
+    dma("y", "dx", "", "xt", T.xt[:, 32:2080], T.x[:])
 
-    ic, ict, cf, fw = T.ic, T.ict, T.cf, T.fw
-    iota("ic", ic[:, 0:32], [[0, 2], [512, 8], [0, 2]], 0)
+    ic, ict, cf, cl, ioL = T.ic, T.ict, T.cf, T.cl, T.ioL
+    iota("ioL0", ioL[:, 0:256], [[1, 256]], 0)
+    iota("ic", ic[:, 0:32], [[1, 2], [2, 16]], 0)
     iota("ic", ic[:, 32:64], [[8, 2], [0, 8], [128, 2]], 4, 1)
-    iota("ic", ic[:, 64:96], [[1, 2], [0, 16]], 0)
+    iota("ic", ic[:, 64:96], [[0, 2], [8, 8], [48, 2]], 0, 3)
     iota("ic", ic[:, 96:128], [[0, 2], [1, 16]], 0)
-    iota("ic", ic[:, 128:160], [[1, 32]], 0)
-    iota("kL", T.kL[:], [[16384, 208]], 0)
-    iota("ioL0", T.ioL[:, 0:256], [[1, 256]], 0)
-    iota("wab", T.wab[:], [[32, 20], [0, 2]], 0)
-    iota("cw0", T.cw0[:], [[16, 40]], 0)
-    turn("ic", "ict", ict[:], ic[:])
+    iota("ic", ic[:, 128:160], [[1, 2], [0, 16]], 0)
+    iota("rl", T.rl[:], [[1, 6], [0, 2]], 0)
+    iota("ic1", ic[:, 160:192], [[0, 2], [32, 16]], RB - 1)
+    iota("cdest", T.cdest[:], [[0, 12], [1, 8], [0, 2]], 0)
+    iota("ic2", ic[:, 168:192:16], [[16, 2]], 0, after="ic1")
+    iota("ic2", ic[:, 169:192:16], [[32, 2]], A1 - 1, 2)
+    iota("ic2", ic[:, 192:208], [[32, 4], [-1, 2], [288, 2]], 1)
+    iota("ic2", ic[:, 208:224], [[32, 4], [-1, 2], [-256, 2]], 257)
+    iota("ic2", ic[:, 170:192:16], [[0, 2]], 0)
+    iota("ic2", ic[:, 224:256], [[1, 32]], 0, 1)
+    fill("di", T.di[:], 0)
+    fill("xz", T.xt[:, 0:32], 0.0)
+    fill("x1", T.x1[:], 0.0)
+    fill("tot0", T.tot[0:32, 1:2], 0.0)
+    fill("pxc", T.px[:, 32:48], 0.0)
+    fill("x5", T.x5[0:32, :], 0.0)
+    turn("ic", "ict", ict[:, 0:160], ic[:, 0:160])
     f = lambda j: cf[:, j:j + 1]
-    lo, odd, q15, q31 = (ict[:, j:j + 1] for j in (0, 64, 96, 128))
-    ts("ict", "hi", f(1), lo, 512.0, A.add)
-    ts("ict", "sb", f(2), ict[:, 32:33], -0.125, A.mult)
-    ts("ict", "sb", f(3), ict[:, 32:33], -0.125, A.mult, -2.0, A.add)
-    ts("ict", "nbc", f(4), lo, -2.0, A.mult, -16384.0 * 96, A.add)
+    q15, odd = ict[:, 96:97], ict[:, 128:129]
+    ts("ict", "bl", cl[:, 0:1], ict[:, 0:1], 11.0, A.min)
+    for k in range(1, 6):
+        act("ioL0", "ioL", ioL[:, 256 * k:256 * k + 256], ioL[:, 0:256], F.Identity, bias=256.0 * k)
+    act("ioL0 ioL", "nxl", T.nxl[:], ioL[:, 0:1040], F.Identity, bias=2.0 * N * TN, scale=0.0)
 
     o1 = T.o1
     ts("btw", "b0", o1[:, 0:12], T.btw[:], 1, A.bitwise_and)
     ts("stw", "e0", o1[:, 24:36], T.stw[:], 2, A.mult)
     tt("e0 b0", "e1", o1[:, 36:48], o1[:, 24:36], o1[:, 0:12], A.add)
+    ts("btw bl", "b1s", T.b1s[:], T.btw[:].indirect(cl[:, 0:1]), 2.0, A.is_ge)
     ts("e1", "e2", o1[:, 48:60], o1[:, 36:48], 1025, A.mult)
-    ts("e2", "e3", o1[:, 24:36], o1[:, 48:60], 4, A.arith_shift_right, 1023, A.bitwise_and)
-    copy("e3", "off1", T.off1[:], o1[:, 24:36])
-    copy("nxrow off1", "n1r", T.n1r[:], T.nxrow[:].indirect(T.off1[:]))
-    op("g", "n1r", "n1L", lambda e: e.partition_broadcast(T.n1L[:], T.n1r[0:1, :], 128))
-    copy("nxw", "nxf", T.nxf[0:32, :], T.nxw[0:32, :])
-    turn("nxf", "nxt", T.nxt[0:32, :], T.nxf[0:32, :])
-    for b in range(2):
-        dma("y", "dnl", "nxt", "nxlin", T.nxlin[0:1, 512 * b:512 * b + 512], T.nxt[0:32, 32 * b:32 * b + 16])
-    op("g", "nxlin", "nxl", lambda e: e.partition_broadcast(T.nxl[:, 0:1024], T.nxlin[0:1, :], 128))
-    iota("nxl", T.nxl[:, 1024:1032], [[0, 8]], N * TN)
-    ts("btw", "b1", o1[:, 12:24], T.btw[:], 1, A.arith_shift_right)
-    copy("b1", "b1u", T.b1u[:], o1[:, 12:24])
-    copy("ioL0 b1u", "b1L", T.b1L[:], T.ioL[:, 0:8].indirect(T.b1u[:]))
-    tt("b1L kL", "kb", T.kb[:], T.b1L[:], T.kL[:, 0:V], A.add)
-    ts("n1L ict", "ga", T.ga[:], T.n1L[:], lo, A.is_ge)
-    ts("n1L hi", "gb", T.gb[:], T.n1L[:], f(1), A.is_ge)
-    scan("ga gb", "c1L", T.c1L[:], T.ga[:], T.gb[:], 0.0, A.subtract)
-    copy("n1L", "a1", T.a1[:], T.n1L[:], q="s", scale=2.0)
+    copy("nxw", "nxf", T.nxf[0:64, :], T.nxw[0:64, :])
+    ts("e2", "e3", o1[:, 12:24], o1[:, 48:60], 4, A.arith_shift_right, 1023, A.bitwise_and)
+    turn("nxf", "nxt", T.nxt[0:64, :], T.nxf[0:64, :])
+    copy("e3", "off1", T.off1[:], o1[:, 12:24])
+    copy("rl", "rlu", cl[:, 2:14], T.rl[:])
+    ts("nxrow off1", "n1r", T.n1r[:], T.nxrow[:].indirect(T.off1[:]), 2.0, A.mult)
+    turn("n1r", "n1t", T.n1t[:], T.n1r[:])
+    tt("n1t b1s", "jf", T.jf[:], T.n1t[:, 0:V:32], T.b1s[:, 0:6], A.add)
+    ts("n1t", "di", T.di[:, 0:6], T.n1t[:, 0:V:32], 1.0 / 1024, A.mult, -0.4995, A.add)
+    copy("jf", "m1", T.m1[:], T.jf[:])
+    spread("m1", "al1", "land1", T.m1[:], T.land1[:, 6 * r:6 * r + 6])
+    dma("s", "dm1", "m1", "land1o", T.land1[:, 6 * r:6 * r + 6], T.m1[:])
+    for k in range(8):
+        dma("y", "dnl", "nxt", "nxl", T.nxl[16 * k:16 * k + 1, 8:1032], T.nxt[0:64, 0:16])
+    dma("y", "dw1", "", "wt1", T.wt[:, 1536:3072], T.w[:, 1536:3072])
+    iota("keep", T.keep[:], [[0, 12], [4096, 16]], 0)
+    iota("ic3", ic[:, 256:272], [[32, 2], [320, 2], [1, 4]], 0)
+    iota("ic3", ic[:, 272:288], [[32, 2], [-288, 2], [1, 4]], 288)
+    iota("ic3", ic[:, 288:320], [[256, 2], [1, 16]], 257, 16)
+
+    iw, iw2, ie = T.iw, T.iw2, T.ie
+    tt("di rlu cdest", "f1", T.f1[:], T.di[:].indirect(cl[:, 2:14]), T.cdest[:], A.is_equal)
+    ts("ict", "sb", f(0), ict[:, 32:33], -0.125, A.mult)
+    ts("ict", "sb", f(1), ict[:, 32:33], -0.125, A.mult, -2.0, A.add)
+    turn("f1", "f1t", T.f1t[:], T.f1[:])
+    ts("ioL0 ict", "iw2", iw2[:], ioL[:, 0:32], q15, A.is_equal)
+    scan("f1t", "c1L", T.c1L[:], T.f1t[:], T.f1t[:], 0.0, A.add, A.max)
     for k in range(2):
-        count("c1L sb", "cnt1 sgx%d" % k, T["sg%d" % k][:], T.c1L[:], f(2 + k), T.cnt1[:, k:k + 1])
-    tt("a1 kb", "aL", T.aL[:, 0:V], T.a1[:], T.kb[:], A.add)
-    ts("ict", "nsc", f(5), lo, 2.0, A.mult, 1024.0, A.add)
-    ts("kL nsc", "aL", T.aL[:, V:208], T.kL[:, V:208], f(5), A.add)
-    ts("cnt1 nbc", "nb", T.nb[:], T.cnt1[:], 8192.0, A.mult, f(4), A.add)
-    op("s", "aL nb", "ab1", lambda e: e.activation(T.ab1[:], T.aL[:], F.Abs, bias=T.nb[:, 1:2]))
-    ts("aL nb", "sub0", T.sub0[:], T.aL[:], T.nb[:, 0:1], A.add)
-    ts("cnt1", "pk", T.pk[:], T.cnt1[:], -1024.0, A.mult, 2048.0 * (96 + V * r), A.add)
-    op("v", "sub0", "vv", lambda e: e.tensor_reduce(T.vv[:, 0:1], T.sub0[:], AxisListType.X, A.min, apply_absolute_value=True))
-    fill("x1", T.x1[:], 0.0)
-    op("v", "ab1", "vv", lambda e: e.tensor_reduce(T.vv[:, 1:2], T.ab1[:], AxisListType.X, A.min))
-    tt("pk vv", "x1", T.x1[:, 0:64:32], T.pk[:], T.vv[:], A.add)
+        act("c1L sb", "cnt1 sg", T.sg[:, V * k:V * k + V], T.c1L[:], F.Sign, bias=f(k), accum_out=T.cnt1[:, k:k + 1])
+    ts("stw", "stu", T.stu[:], T.stw[:], 8.0, A.add)
+    turn("ic2", "ict2", ict[:, 160:256], ic[:, 160:256])
+    ts("ict", "even", f(2), odd, -1.0, A.mult, 1.0, A.add)
+    ts("ict", "q31", f(3), odd, 16.0, A.mult, q15, A.add)
+    ts("ict2", "m9", f(4), ict[:, 224:225], 16.0 * r + 9, A.is_equal)
+    ts("ict", "dg", cl[:, 14:15], ict[:, 64:65], 0.125, A.mult, 47.0, A.min)
+    ts("cnt1", "x1", T.x1[:, 0:64:32], T.cnt1[:], -0.5, A.mult, V / 2.0, A.add)
+    ts("ic q31", "iwf", iw[:, 32:64], ic[:, 96:128], f(3), A.is_equal)
     turn("x1", "x1t", T.x1t[:], T.x1[:])
     for k in range(8):
         dma("y" if k % 2 else "s", "dc1", "x1t", "w1", T.w1[16 * k:16 * k + 16, :], T.x1t[0:128:32, :])
-    send("w1", "al1", lambda d: T.w1[:, 2 * d:2 * d + 2], lambda j: T.land1[:, 2 * j:2 * j + 2])
-
-    ts("wab ict", "wac", T.wac[:], T.wab[:], q31, A.add)
-    copy("n1L wac", "own", T.own[:], T.n1L[:].indirect(T.wac[:, 0:12]), q="s")
-    ts("cw0 ict", "cw", T.cw[:], T.cw0[:], q15, A.add)
-    ts("ict", "even", f(6), odd, -1.0, A.mult, 1.0, A.add)
-    ts("cw", "dw", T.dw[:], T.cw[:], float(KEYS), A.add)
-    ts("cw", "kw", fw[:, 0:12], T.cw[:, 0:12], float(V * r), A.add)
-    copy("stw", "stu", T.stu[:], T.stw[:])
-    op("v", "xt", "xq xs", lambda e: e.quantize_mx(T.xq[:], T.xs[:], T.xt[:]))
-    pick("xq", "xs", "stq", "sts", T.stq[:], T.sts[:], T.xq[:], T.xs[:], T.stu[:], "stu")
-    turn("own", "ownt", T.ownt[:], T.own[:])
-    copy("w1", "w1i", T.w1i[:], T.w1[:])
-    ts("w1i", "w1k", T.w1k[:], T.w1i[:], 11, A.arith_shift_right)
-    ts("w1k", "s1off", T.s1off[:], T.w1k[:], -V * r, A.add, V - 1, A.min)
+    ts("ict even iwf", "iwf", iw[:, 41:64:16], ict[:, 96:98], 8.0, A.is_lt, f(2), A.mult)
+    fill("iwf", iw[:, 32 + r:64:16], 0.0)
+    fill("iwf", iw[:, 40:64:16], 1.0)
+    ts("ic ict", "mk", T.mk[:], ic[:, 96:128], q15, A.is_equal)
+    ts("ioL0 q31 ict2", "pxc", T.px[:, 64:96], ioL[:, 0:32], f(3), A.is_equal, ict[:, 160:161], A.mult)
+    turn("iwf", "iw", iw[:, 0:32], iw[:, 32:64])
+    ts("ioL0 ict2", "la", cl[:, 16:18], ioL[:, 0:129:128], ict[:, 192:193], A.add)
+    for k in range(2):
+        quant("xt xz", "q0 s0", T.q0[:, 260 * k:260 * k + 260], T.s0[:, 260 * k:260 * k + 260], T.xt[:, 1040 * k:1040 * k + 1040])
+    pick("q0", "s0", "stq", "sts", T.stq[:], T.sts[:], T.q0[:], T.s0[:], T.stu[:], "stu")
+    move("y", "dq1", "stq", "sts", "q1s", T.q1, T.s1, SB, T.stq, T.sts, 0, V)
+    act("ioL m9", "ci", T.ci[:], ioL[:, SB:SB + V], F.Identity, scale=f(4))
+    quant("xt", "q1x", T.q1[:, XB:XB + TN], T.s1[:, XB:XB + TN], T.xt[:, 32:2080])
+    ts("w1", "s1off", T.s1off[:], T.w1[:], V - 1.0, A.min)
     pick("stq", "sts", "p1q", "p1s", T.p1q[:], T.p1s[:], T.stq[:], T.sts[:], T.s1off[:], "s1off")
-    send("p1q", "aq1", lambda d: T.p1q[:, CAP * d:CAP * d + CAP].bitcast(dt.uint8),
-         lambda j: T.cq[:, V + CAP * j:V + CAP * j + CAP].bitcast(dt.uint8))
-    send("p1s", "as1", lambda d: T.p1s[:, CAP * d:CAP * d + CAP], lambda j: T.cs[:, V + CAP * j:V + CAP * j + CAP])
-    dma("y", "dcq", "stq", "cq0", T.cq[:, 0:V].bitcast(dt.uint8), T.stq[:].bitcast(dt.uint8))
-    dma("y", "dcq", "sts", "cs0", T.cs[:, 0:V], T.sts[:])
-    dma("y", "dw_", "", "wt", T.wt[:], T.w[:])
-    iota("keyL", T.keyL[:, 0:V], [[1, V]], V * r)
-    iota("infoX", T.infoL[:, CAND:CX], [[1, CAP]], KEYS + CAND + CAP * r)
-    iota("ioL", T.ioL[:, 256:KW], [[1, KW - 256]], 256)
-    iota("ones", T.ones[:], [[0, CAND]], 1)
-    iota("sT", T.sT[:, 0:KEYS], [[1, 8], [0, V]], 0)
-    iota("sT", T.sT[:, KEYS:KW], [[0, 8]], 0)
-    iota("iT", T.iT[:, KEYS:KW], [[0, 8]], 0)
-    ow = T.ow
-    copy("ownt", "n1w", ow[:, 0:12], T.ownt[:, 0:V:16])
-    ts("n1w", "oc", ow[:, 12:24], ow[:, 0:12], 511, A.bitwise_and)
-    ts("n1w", "oa", ow[:, 24:36], ow[:, 0:12], 9, A.arith_shift_right)
-    ts("oc", "od", ow[:, 36:48], ow[:, 12:24], 2, A.mult)
-    ts("oa", "of", ow[:, 48:60], ow[:, 24:36], r, A.not_equal, 2048, A.mult)
-    tt("od b1", "oe", ow[:, 60:72], ow[:, 36:48], o1[:, 12:24], A.add)
-    copy("oc", "c1u0", T.c1u[:, 0:12], ow[:, 12:24])
-    tt("oe of", "og", ow[:, 72:84], ow[:, 60:72], ow[:, 48:60], A.add)
-    ts("og", "noff0", T.noff[:, 0:12], ow[:, 72:84], 1024, A.min)
-    copy("nxl noff0", "n2L0", T.n2L[:, 0:V], T.nxl[:].indirect(T.noff[:, 0:12]))
-    ts("n2L0 ict", "g2a0", T.g2a[:, 0:V], T.n2L[:, 0:V], lo, A.is_ge)
-    ts("n2L0 hi", "g2b0", T.g2b[:, 0:V], T.n2L[:, 0:V], f(1), A.is_ge)
-    scan("g2a0 g2b0", "c2L0", T.c2L[:, 0:V], T.g2a[:, 0:V], T.g2b[:, 0:V], 0.0, A.subtract)
-    for k in range(2):
-        count("c2L0 sb", "cnt2o sgy%d" % k, T["sg%d" % (2 + k)][:, 0:V], T.c2L[:, 0:V], f(2 + k), T.cnt2[:, k:k + 1])
-    copy("n2L0", "inf00", T.inf0[:, 0:V], T.n2L[:, 0:V], q="s", scale=4096.0)
-    fill("x2", T.x2[:], 0.0)
+    at1 = A1 + CAP * r
+    send("p1q", "aq1", "q1a", lambda d: T.p1q[:, CAP * d:CAP * d + CAP].bitcast(dt.uint8), T.q1[:, at1:at1 + CAP].bitcast(dt.uint8))
+    send("p1s", "as1", "s1a", lambda d: T.p1s[:, CAP * d:CAP * d + CAP], T.s1[:, at1:at1 + CAP])
+    quant("wt1", "wq1", T.wq[:, 384:768], T.ws[:, 384:768], T.wt[:, 1536:3072])
+    for a, b in ((A1, at1), (at1 + CAP, A1 + N * CAP)):
+        if b > a:
+            move("y", "dq2", "q1a", "s1a", "q2o", T.q2, T.s2, a, T.q1, T.s1, a, b - a)
+    move("y", "dq2", "stq", "sts", "q2o", T.q2, T.s2, SB, T.stq, T.sts, 0, V)
+    move("y", "dq2", "q0", "s0", "q2o", T.q2, T.s2, 0, T.q0, T.s0, 0, 8)
 
-    wrote["land1"] = [arrivals("al1")]
-    wrote["cqa"] = [arrivals("aq1")]
-    wrote["csa"] = [arrivals("as1")]
-    l1 = T.l1
-    copy("land1", "l1", l1[:, 0:14], T.land1[:])
-    ts("l1", "la", l1[:, 14:28], l1[:, 0:14], 2047, A.bitwise_and)
-    copy("la", "noff1", T.noff[:, 12:26], l1[:, 14:28])
-    copy("nxl noff1", "n2L1", T.n2L[:, V:CAND], T.nxl[:].indirect(T.noff[:, 12:26]))
-    ts("n2L1 ict", "g2a1", T.g2a[:, V:CAND], T.n2L[:, V:CAND], lo, A.is_ge)
-    ts("n2L1 hi", "g2b1", T.g2b[:, V:CAND], T.n2L[:, V:CAND], f(1), A.is_ge)
-    scan("g2a1 g2b1 c2L0", "c2L1", T.c2L[:, V:CAND], T.g2a[:, V:CAND], T.g2b[:, V:CAND], T.c2L[:, V - 1:V], A.subtract)
-    ts("ioL0 c2L1", "c2L2", T.c2L[:, CAND:CX], T.ioL[:, 1:1 + CAP], T.c2L[:, CAND - 1:CAND], A.add)
-    for k in range(2):
-        count("c2L1 c2L2 sb", "cnt2a sgz%d" % k, T["sg%d" % (2 + k)][:, V:CX], T.c2L[:, V:CX], f(2 + k), T.cnt2[:, 4 + k:5 + k])
-    ts("cnt2o", "cnt2h", T.cnt2[:, 2:4], T.cnt2[:, 0:2], -0.5, A.mult, CX / 2.0, A.add)
-    ts("l1", "lk", l1[:, 28:42], l1[:, 0:14], 11, A.arith_shift_right)
-    ts("l1", "le", l1[:, 42:56], l1[:, 0:14], 1, A.arith_shift_right, 511, A.bitwise_and)
-    copy("lk", "ku1", T.ku1[:], l1[:, 28:42])
-    ts("cnt2a", "cnt2b", T.cnt2[:, 6:8], T.cnt2[:, 4:6], -0.5, A.mult)
-    tt("cnt2b cnt2h", "x2", T.x2[:, 0:64:32], T.cnt2[:, 6:8], T.cnt2[:, 2:4], A.add)
-    turn("x2", "x2t", T.x2t[:], T.x2[:])
-    for k in range(8):
-        dma("y" if k % 2 else "s", "dc2", "x2t", "w2", T.w2[16 * k:16 * k + 16, :], T.x2t[0:128:32, :])
-    copy("n2L1", "inf01", T.inf0[:, V:CAND], T.n2L[:, V:CAND], q="s", scale=4096.0)
-    copy("ioL0 ioL ku1", "keyL1", T.keyL[:, V:CAND], T.ioL[:].indirect(T.ku1[:]), q="s")
-    tt("inf00 keyL", "info0", T.infoL[:, 0:V], T.inf0[:, 0:V], T.keyL[:, 0:V], A.add)
-    copy("le", "c1u1", T.c1u[:, 12:26], l1[:, 42:56])
-    tt("inf01 keyL1", "info1", T.infoL[:, V:CAND], T.inf0[:, V:CAND], T.keyL[:, V:CAND], A.add)
-    pick("xq", "xs", "cq1", "cs1", T.cq[:, CAND:2 * CAND], T.cs[:, CAND:2 * CAND], T.xq[:], T.xs[:], T.c1u[:], "c1u0 c1u1")
-    copy("w2", "w2u", T.w2u[:], T.w2[:])
-    copy("info0 info1 infoX w2u", "ig", T.ig[:], T.infoL[:].indirect(T.w2u[:]))
-    copy("ig wac", "ig2", T.ig2[:], T.ig[:].indirect(T.wac[:, 0:16]))
-    turn("ig2", "igt", T.igt[:], T.ig2[:])
-    copy("igt", "l2s", T.l2s[:], T.igt[:, 0:256:16])
-    send("l2s", "al2", lambda d: T.l2s[:, 2 * d:2 * d + 2], lambda j: T.land2[:, 2 * j:2 * j + 2])
-    ts("w2", "o2off", T.o2off[:, 0:32:2], T.w2[:], CAND - 1.0, A.min)
-    ts("w2", "o2off", T.o2off[:, 1:32:2], T.w2[:], CAND - 1.0, A.min, float(CAND), A.add)
-    pick("cq0 cq1 cqa", "cs0 cs1 csa", "p2q", "p2s", T.p2q[:], T.p2s[:], T.cq[:], T.cs[:], T.o2off[:], "o2off")
-    send("p2q", "aq2", lambda d: T.p2q[:, 64 * d:64 * d + 64].bitcast(dt.uint8),
-         lambda j: T.eq[:, 64 * j:64 * j + 64].bitcast(dt.uint8))
-    send("p2s", "as2", lambda d: T.p2s[:, 64 * d:64 * d + 64], lambda j: T.es[:, 64 * j:64 * j + 64])
-    iota("pp", T.pp[:, KEYS:KEYS + TAIL], [[1, TAIL]], M + 1)
-    iota("yx", T.yx[:, 0:CAND], [[1, CAND]], 0)
-    iota("yx", T.yx[:, CAND:ALL], [[32, 14], [1, 16]], CAND)
-    iota("inv", T.inv[:, 0:M], [[0, M]], YZ)
-    iota("iT", T.iT[:, 0:KEYS], [[0, 8], [1, V]], 0)
-    for o in range(2):
-        iota("ybz%d" % o, T["yb%d" % o][:, YZ:YZ + 8], [[0, 8]], 0)
-    iota("sW", T.sW[:, 0:V], [[0, V]], r)
-    iota("iW", T.iW[:, 0:V], [[1, V]], 0)
-    iota("sW", T.sW[:, YZ:YZ + 8], [[0, 8]], -1)
-    iota("iW", T.iW[:, YZ:YZ + 8], [[0, 8]], -1)
+    m2, tot, px, mi, kk = T.m2, T.tot, T.px, T.mi, T.kk
+    copy("land1 land1o", "zf", T.zf[:], T.land1[:])
+    ts("zf dg", "off2", T.off2[:], T.zf[:].indirect(cl[:, 14:15]), 8.0 - 1024 * r, A.add, 1032.0, A.min)
+    copy("nxl off2", "n2r", T.n2r[:], T.nxl[:].indirect(T.off2[:, 0:12]))
+    ts("off2", "c1u", T.c1u[:], T.off2[:, 0:12], 0.5, A.mult, XB - 4.25, A.add)
+    turn("n2r", "n2t", T.n2t[:], T.n2r[:])
+    ts("n2t", "xo", T.xo[:], T.n2t[:, 0:V:16], 1.0 / TN, A.mult, -0.499, A.add)
+    act("iw2 xo", "tot junk", T.junk[:], iw2[:].indirect(T.xo[:]), F.Identity, accum_out=tot[:, 0:1])
+    act("ioL0 ioL c1u iw2", "t1", T.t1[:], ioL[:].indirect(T.c1u[:]), F.Identity, scale=iw2[:, 1:2])
+    act("ioL0 ioL iw2", "wa", T.wa[:], ioL[:, 0:QW], F.Identity, scale=iw2[:, 0:1])
+    act("ioL0 ioL", "tab2", T.tab2[:], ioL[:, 0:RB + 272], F.Identity, scale=0.0)
+    act("ioL0 ioL", "tab3", T.tab3[:], ioL[:, 0:RB + M + 16], F.Identity, scale=0.0)
+    act("ioL0", "x3", T.x3[:], ioL[:, 0:V], F.Identity, scale=0.0)
+    copy("iw xo", "fl", T.fl[:], iw[:, 0:32].indirect(T.xo[:]))
+    ts("n2t", "m2a", m2[:, 0:12], T.n2t[:, 0:V:16], -1.0, A.mult, float(N * TN), A.add)
+    tt("tot", "u2", tot[64:96, 1:2], tot[0:32, 0:1], tot[32:64, 0:1], A.add)
+    copy("tot", "u1", tot[32:64, 1:2], tot[0:32, 0:1])
+    ts("iw2 tot even", "pxb", px[:, 48:64], iw2[:, 0:16], tot[:, 0:1], A.mult, f(2), A.mult)
+    tt("tot u2", "u3", tot[96:128, 1:2], tot[64:96, 1:2], tot[64:96, 0:1], A.add)
+    ts("zf dg", "mi", mi[:, 0:16], T.zf[:].indirect(cl[:, 14:15]), 1.0 / 1024, A.mult, -0.4995, A.add)
+    ts("mk tot0 u1 u2 u3", "pxa", px[:, 0:32], T.mk[:, 0:32], tot[:, 1:2], A.mult)
+    ts("off2", "c1i", mi[:, 16:28], T.off2[:, 0:12], 0.5, A.mult, XB + 32 - 4.25, A.add)
+    turn("pxa pxb pxc", "pxt", T.pxt[:], px[:])
+    ts("mi", "cba", kk[:, 0:12], mi[:, 0:12], 64.0, A.mult, float(A2 + 32 - RB - CAP * r), A.add)
+    summed("pxt", "init", T.init[:], T.pxt[:])
+    scan("fl ci init", "cnt", T.cnt[:], T.fl[:], T.ci[:], T.init[:], A.add, A.max)
+    copy("init", "m2c", m2[:, 24:25], T.init[:])
+    tt("cnt fl", "val", T.val[:], T.cnt[:], T.fl[:], A.mult)
+    turn("val", "vt", T.vt[:], T.val[:])
+    scan("keep vt", "seg", T.seg[:], T.keep[:], T.vt[:], 0.0, A.min, A.max)
+    copy("vt", "c0u", T.c0u[:], T.vt[:, 9:V:16])
+    copy("seg", "m2b", m2[:, 12:24], T.seg[:, 8:V:16])
+    spread("m2a m2b m2c", "al2", "land2", m2[:, 0:ML], T.land2[:, ML * r:ML * r + ML])
+    dma("s", "dm2", "m2a m2b m2c", "land2o", T.land2[:, ML * r:ML * r + ML], m2[:, 0:ML])
+    move("y", "dq3", "q0 land2", "s0", "q2x", T.q2, T.s2, XB, T.q0, T.s0, 8, TN)
+    dma("y", "dw0", "", "wt0", T.wt[:, 0:1536], T.w[:, 0:1536])
+    tt("wa c0u t1", "vals", T.vals[:], T.wa[:].indirect(T.c0u[:]), T.t1[:], A.add)
+    op("v", "vals m2b tab2", "tab2s", lambda e: e.tensor_copy(T.tab2[:].indirect(m2[:, 12:24]), T.vals[:]))
 
-    n2w, xx = T.n2w, T.xx
-    copy("n2L0 n2L1 wac", "n2g", T.n2g[:], T.n2L[:].indirect(T.wac[:, 0:26]), q="s")
-    copy("ioL0 ioL", "bm", T.bm[:, 0:KEYS], T.ioL[:, 0:KEYS], q="s", scale=0.0)
-    copy("lk", "kw", fw[:, 12:26], l1[:, 28:42])
-    turn("n2g", "n2t", T.n2t[:], T.n2g[:])
-    copy("n2t", "n2w", n2w[:, 0:26], T.n2t[:, 0:CAND:16])
-    ts("n2w", "n2e", n2w[:, 52:78], n2w[:, 0:26], 9, A.arith_shift_right)
-    ts("n2w", "n2c", n2w[:, 26:52], n2w[:, 0:26], 511, A.bitwise_and)
-    ts("n2e", "bad", fw[:, 26:52], n2w[:, 52:78], r, A.not_equal)
-    copy("n2c", "c2u", T.c2u[:], n2w[:, 26:52])
-    tt("bad dw", "badd", fw[:, 52:78], fw[:, 26:52], T.dw[:, 0:26], A.mult)
-    pick("xq", "xs", "n2q", "n2s", T.n2q[:], T.n2s[:], T.xq[:], T.xs[:], T.c2u[:], "c2u")
-    tt("kw badd", "ko", T.ko[:], fw[:, 0:26], fw[:, 52:78], A.max)
-    op("v", "wt", "wq0 ws0", lambda e: e.quantize_mx(T.wq[:, 0:384], T.ws[:, 0:384], T.wt[:, 0:1536]))
-    copy("ko", "kou0", T.kou[:, 0:26], T.ko[:])
-    op("v", "wt", "wq1 ws1", lambda e: e.quantize_mx(T.wq[:, 384:768], T.ws[:, 384:768], T.wt[:, 1536:3072]))
-    op("v", "kou0 ones", "bm", lambda e: e.tensor_copy(T.bm[:].indirect(T.kou[:, 0:26]), T.ones[:]))
-    ts("ko even", "qa", xx[:, 0:13], T.ko[:, 0:26:2], f(6), A.mult)
-    ts("ko ict", "qb", xx[:, 13:26], T.ko[:, 1:26:2], odd, A.mult)
-    tt("qa qb", "qc", xx[:, 26:39], xx[:, 0:13], xx[:, 13:26], A.add)
-    copy("qc", "pwa", T.pwa[:, 0:26:2], xx[:, 26:39])
-    copy("qc", "pwa", T.pwa[:, 1:26:2], xx[:, 26:39])
+    def collect(tag, tab, y, n, lst, gg, rr, w):
+        turn("tab%ss" % tag, "ya" + tag, y[:, 0:n], tab[:, RB:RB + n])
+        turn("tab%ss" % tag, "yb" + tag, y[:, n:2 * n + 32], tab[:, RB - 16:RB + n + 16])
+        ys = "ya%s yb%s l%s" % (tag, tag, "a" if tag == "2" else "e")
+        copy(ys, "ga" + tag, gg[:, 0:w], y[:, 0:2 * n + 16].indirect(lst))
+        tt(ys + " ga" + tag, "gb" + tag, gg[:, w:2 * w], y[:, 16:2 * n + 32].indirect(lst), gg[:, 0:w], A.add)
+        tt("gb" + tag, "ra" + tag, rr[0:64, 0:w], gg[0:64, w:2 * w], gg[64:128, w:2 * w], A.add)
+        tt("ra" + tag, "rb" + tag, rr[0:32, w:2 * w], rr[0:32, 0:w], rr[32:64, 0:w], A.add)
 
-    W = lambda k, o: (T.wq[:, 128 * (2 * k + o):128 * (2 * k + o) + 128], T.ws[:, 128 * (2 * k + o):128 * (2 * k + o) + 128])
+    big = 8192.0
+    turn("ic3", "ict3", ict[:, 256:320], ic[:, 256:320])
+    act("iw2", "al", f(11), iw2[:, 10:11], F.Identity, scale=-big)
+    act("iw2", "al", f(12), iw2[:, 10:11], F.Identity, scale=big + RB - 2 - N * (RB - 1 + CAP * r), bias=1.0)
+    act("ioL0", "oh", ie[:, 16:32], ioL[:, 0:16], F.Abs, bias=-float(r))
+    act("oh", "oh2", ie[:, 32:48], ie[:, 16:32], F.Relu, scale=-1.0, bias=1.0)
+    act("oh2 al", "ie", ie[:, 0:16], ie[:, 32:48], F.Identity, scale=f(12), bias=f(11))
+    act("ioL0 ict3", "x3", T.x3[:, 3:V:16], ioL[:, 0:V:16], F.Identity, bias=ict[:, 288:289])
+    collect("2", T.tab2, T.y2, 256, cl[:, 16:18], T.g2, T.r2, 32)
+    for k in range(4):
+        ts("rb2", "p2off", T.p2off[32 * k:32 * k + 32, :], T.r2[0:32, 32:64], float(XB), A.max)
+    pick("q1x q1s q1a", "q1x q1s s1a", "p2q", "p2s", T.p2q[:], T.p2s[:], T.q1[:], T.s1[:], T.p2off[:], "p2off")
+    at2 = A2 + 2 * CAP * r
+    send("p2q", "aq2", "q2a", lambda d: T.p2q[:, 64 * d:64 * d + 64].bitcast(dt.uint8), T.q2[:, at2:at2 + 64].bitcast(dt.uint8))
+    send("p2s", "as2", "s2a", lambda d: T.p2s[:, 64 * d:64 * d + 64], T.s2[:, at2:at2 + 64])
 
-    def mm(r_, w_, bank, n, k, o, q, s, a, b):
-        wq, ws = W(k, o)
-        op("t", r_ + " wq0 ws0 wq1 ws1", w_, lambda e: e.matmul_mx(T.ps[:, 512 * bank:512 * bank + n], wq, ws, q, s, a, b))
+    z2, zz = T.z2, T.zz
+    copy("land2 land2o", "z2", z2[:], T.land2[:])
+    tt("c1i vt", "c1m", kk[:, 12:24], mi[:, 16:28], T.vt[:, 9:V:16], A.min)
+    tt("z2", "za", zz[:, 0:100], z2[:, 0:100], z2[:, 100:200], A.max)
+    summed("z2", "bsum", T.bsum[:], z2[:, 24:200:ML])
+    tt("za", "zb", zz[:, 100:150], zz[:, 0:50], zz[:, 50:100], A.max)
+    tt("zb", "zc", zz[:, 150:175], zz[:, 100:125], zz[:, 125:150], A.max)
+    an, bn = zz[:, 150:162], zz[:, 162:174]
+    ts("zc", "xe", T.xe[:], an, -1.0 / TN, A.mult, N - 0.499, A.add)
+    tt("zc cba", "bc", kk[:, 24:36], bn, kk[:, 0:12], A.add)
+    copy("ie xe", "fe", T.fe[:], ie[:, 0:16].indirect(T.xe[:]))
+    tt("bc c1m", "d1", kk[:, 36:48], kk[:, 24:36], kk[:, 12:24], A.max)
+    scan("fe bsum", "pe", T.pe[:], T.fe[:], T.fe[:], T.bsum[:], A.add, A.max)
+    ts("d1", "d1u", T.d1u[:], kk[:, 36:48], -32.0, A.add)
+    act("ioL0 ioL d1u iw2", "t3", T.t3[:], ioL[:].indirect(T.d1u[:]), F.Identity, scale=iw2[:, 1:2])
+    turn("pe", "pt", T.pt[:], T.pe[:])
+    ts("zc", "x3", T.x3[:, 2:V:16], an, -1.0, A.mult, float(8 + TN * (N - r)), A.add)
+    tt("pt", "pa", kk[:, 60:72], T.pt[:, r:V:16], T.pt[:, 10:V:16], A.add)
+    tt("bc vt", "d0", kk[:, 48:60], kk[:, 24:36], T.vt[:, 9:V:16], A.max)
+    turn("x3", "x3t", T.x3t[:], T.x3[:])
+    copy("d0", "d0u", T.d0u[:], kk[:, 48:60])
+    tt("pa vt", "pb", kk[:, 72:84], kk[:, 60:72], T.vt[:, 8:V:16], A.max)
+    tt("wa d0u x3t", "v3", T.v3[:], T.wa[:].indirect(T.d0u[:]), T.x3t[:], A.add)
+    copy("pb", "po", T.po[:], kk[:, 72:84])
+    ts("ioL0 ioL ict3", "le", cl[:, 18:23], ioL[:, 0:257:64], ict[:, 256:257], A.add, 590.0, A.min)
+    tt("v3 t3", "v4", T.v4[:], T.v3[:], T.t3[:], A.add)
+    op("v", "v4 po tab3", "tab3s", lambda e: e.tensor_copy(T.tab3[:].indirect(T.po[:]), T.v4[:]))
+    collect("3", T.tab3, T.y3, M, cl[:, 18:23], T.g3, T.r3, 80)
+    for k in range(3):
+        copy("rb3", "fo0", T.fo[0:32, 18 * k:18 * k + 18], T.r3[0:32, 80 + k:152:4])
+    for k in range(1, 4):
+        copy("fo0", "fo", T.fo[32 * k:32 * k + 32, :], T.fo[0:32, :])
 
-    for o in range(2):
-        mm("cq0 cqa cs0 csa", "psS%d" % o, o, CAND, 0, o, T.cq[:, 0:CAND], T.cs[:, 0:CAND], True, False)
-        mm("cq1 cs1", "psS%d" % o, o, CAND, 1, o, T.cq[:, CAND:2 * CAND], T.cs[:, CAND:2 * CAND], False, False)
-        mm("n2q n2s", "psS%d" % o, o, CAND, 2, o, T.n2q[:], T.n2s[:], False, True)
-
-    wrote["land2"] = [arrivals("al2")]
-    wrote["eqa"] = [arrivals("aq2")]
-    wrote["esa"] = [arrivals("as2")]
-    l2 = T.l2i
-    copy("land2", "m0", l2[:, 0:14], T.land2[:])
-    ts("m0", "m1", l2[:, 14:28], l2[:, 0:14], 4095, A.bitwise_and)
-    copy("m1", "kou1", T.kou[:, 26:40], l2[:, 14:28])
-    op("v", "kou1 ones", "bm", lambda e: e.tensor_copy(T.bm[:].indirect(T.kou[:, 26:40]), T.ones[:, 0:ARR]))
-    ts("m0", "m2", l2[:, 28:42], l2[:, 0:14], 12, A.arith_shift_right, 511, A.bitwise_and)
-    ts("m1 even", "qd", xx[:, 39:46], l2[:, 14:28:2], f(6), A.mult)
-    ts("m1 ict", "qe", xx[:, 46:53], l2[:, 15:28:2], odd, A.mult)
-    scan("bm", "pp", T.pp[:, 0:KEYS], T.bm[:, 0:KEYS], T.bm[:, 0:KEYS], 0.0, A.max)
-    tt("qd qe", "qf", xx[:, 53:60], xx[:, 39:46], xx[:, 46:53], A.add)
-    copy("m2", "c2ua", T.c2ua[:, 0:28:2], l2[:, 28:42])
-    copy("qf", "pwb", T.pwa[:, 26:40:2], xx[:, 53:60])
-    copy("qf", "pwb", T.pwa[:, 27:40:2], xx[:, 53:60])
-    copy("m2", "c2ua", T.c2ua[:, 1:28:2], l2[:, 28:42])
-    copy("pp pwa", "pg0", T.pg[:, 0:320], T.pp[:].indirect(T.pwa[:, 0:20]))
-    copy("pp pwa pwb", "pg1", T.pg[:, 320:ALL], T.pp[:].indirect(T.pwa[:, 20:40]), q="s")
-    turn("pg0", "pt0", T.pt[:, 0:320], T.pg[:, 0:320])
-    ts("m1", "ku2", T.ku2[:, 0:28:2], l2[:, 14:28], KEYS - 1, A.min)
-    ts("m1", "ku2", T.ku2[:, 1:28:2], l2[:, 14:28], KEYS - 1, A.min)
-    turn("pg1", "pt1", T.pt[:, 320:ALL], T.pg[:, 320:ALL])
-    ts("pt0 pt1", "plu", T.plu[:], T.pt[:, 0:ALL:16], -1.0, A.add)
-    pick("xq", "xs", "fq", "fs", T.fq[:], T.fs[:], T.xq[:], T.xs[:], T.c2ua[:, 0:27], "c2ua")
-    op("v", "plu yx", "inv", lambda e: e.tensor_copy(T.inv[:].indirect(T.plu[:]), T.yx[:]))
-    copy("inv wac", "ivg", T.ivg[:], T.inv[:, 0:M].indirect(T.wac[:, 0:18]))
-    turn("ivg", "ivt", T.ivt[:], T.ivg[:])
-    copy("ivt", "ylu", T.ylu[:], T.ivt[:, 0:M:16])
-    for o in range(2):
-        mm("fq fs", "psA%d" % o, 2 + o, SPREAD, 2, o, T.fq[:], T.fs[:], True, False)
-    for o in range(2):
-        copy("psS%d" % o, "yb%d" % o, T["yb%d" % o][:, 0:CAND], T.ps[:, 512 * o:512 * o + CAND], q="s")
-    for t_, w_ in (("sT", "sW"), ("iT", "iW")):
-        copy(t_ + " ku1", w_, T[w_][:, V:CAND], T[t_][:].indirect(T.ku1[:]), q="s")
-        copy(t_ + " ku2", w_, T[w_][:, CAND:YZ], T[t_][:].indirect(T.ku2[:, 0:27]), q="s")
-    for o in range(2):
-        mm("eqa esa", "psA%d" % o, 2 + o, SPREAD, 0, o, T.eq[:, 0:SPREAD], T.es[:, 0:SPREAD], False, False)
-        mm("eqa esa", "psA%d" % o, 2 + o, SPREAD, 1, o, T.eq[:, 16:16 + SPREAD], T.es[:, 16:16 + SPREAD], False, True)
-    copy("psA0", "yb0", T.yb0[:, CAND:YZ], T.ps[:, 1024:1024 + SPREAD], q="s")
-    copy("psA1", "yb1", T.yb1[:, CAND:YZ], T.ps[:, 1536:1536 + SPREAD], q="s")
-    copy("yb0 ybz0 ylu", "yo0", T.yo0[:], T.yb0[:].indirect(T.ylu[:]))
+    for k in (2, 1, 0):
+        src = ("q0", "s0", T.q0[:], T.s0[:]) if k == 2 else ("q2o q2x q2a", "q2o q2x s2a", T.q2[:], T.s2[:])
+        pick(src[0], src[1], "fq%d" % k, "fs%d" % k, T.fq[:, M * k:M * k + M], T.fs[:, M * k:M * k + M],
+             src[2], src[3], T.fo[:, 18 * k:18 * k + 18], "fo0 fo")
+        if k == 2:
+            quant("wt0", "wq0", T.wq[:, 0:384], T.ws[:, 0:384], T.wt[:, 0:1536])
+        for o in range(2):
+            c = 128 * (2 * k + o)
+            op("t", "fq%d fs%d wq%d" % (k, k, c // 384), "ps%d" % o, lambda e: e.matmul_mx(
+                T.ps[:, 512 * o:512 * o + M], T.wq[:, c:c + 128], T.ws[:, c:c + 128], T.fq[:, M * k:M * k + M],
+                T.fs[:, M * k:M * k + M], k == 2, k == 0))
+    ki = T.ki
+    copy("rb3", "k0", ki[0:32, 0:18], T.r3[0:32, 83:152:4])
+    ts("k0", "k1", ki[0:32, 18:36], ki[0:32, 0:18], 8, A.arith_shift_right)
+    ts("k0", "k2", ki[0:32, 36:54], ki[0:32, 0:18], 255, A.bitwise_and)
+    copy("ps0", "yo0", T.yo0[:], T.ps[:, 0:M])
     dma("y", "dy0", "yo0", "y0", T.y[:, 0:M], T.yo0[:])
-    copy("yb1 ybz1 ylu", "yo1", T.yo1[:], T.yb1[:].indirect(T.ylu[:]), q="s")
+    act("ps1", "yo1", T.yo1[:], T.ps[:, 512:512 + M])
     dma("s", "dy1", "yo1", "y1", T.y[:, M:2 * M], T.yo1[:])
-    copy("sW ylu", "ids", T.ids[:], T.sW[:].indirect(T.ylu[:]))
-    dma("y", "did", "ids", "id0", T["id"][0:1, :], T.ids[0:1, :])
-    copy("iW ylu", "idi", T.idi[:], T.iW[:].indirect(T.ylu[:]), q="s")
-    dma("s", "did2", "idi", "id1", T["id"][1:2, :], T.idi[0:1, :])
+    for k in range(2):
+        ts("k1 k2", "x5", T.x5[0:32, 32 * k:32 * k + 18], ki[0:32, 18 + 18 * k:36 + 18 * k], -1.0, A.add)
+    turn("x5", "x5t", T.x5t[0:32, :], T.x5[0:32, :])
+    for k in range(2):
+        dma("y", "did", "x5t", "id%d" % k, T["id"][k:k + 1, :], T.x5t[0:18, 32 * k:32 * k + 16])
     await_("g", [(s, None) for s in total])

@@ -3,9 +3,10 @@ from concourse.mybir import dt, AluOpType as A, AxisListType, ActivationFunction
 
 N = 8
 TN, V, M, CAP = 512, 192, 288, 32
-A2, XB, A1, SB, QW = 16, 528, 1072, 1328, 1520
+XB, A2, A1, SB, QW = 16, 528, 1040, 1296, 1488
 RB = 224
 ML = 25
+BIG = 8192.0
 X4 = "float8_e4m3fn_x4"
 
 
@@ -15,29 +16,29 @@ def _sb(n, d="float32"):
 
 SCRATCH = {
     "stw": _sb(12, "int32"), "btw": _sb(12, "int32"), "nxrow": _sb(1024, "int32"), "nxw": _sb(32, "int32"), "nxf": _sb(32),
-    "nxt": _sb(32), "nxl": _sb(1040), "xt": _sb(2080, "bfloat16"), "wt": _sb(3072, "bfloat16"),
-    "ic": _sb(320), "ict": _sb(320), "cf": _sb(16), "ioL": _sb(1536), "wa": _sb(QW), "cl": _sb(32, "uint16"), "rl": _sb(12),
-    "cdest": _sb(V), "keep": _sb(V), "ci": _sb(V), "iw": _sb(64), "iw2": _sb(32), "ie": _sb(48), "mk": _sb(32),
+    "nxt": _sb(32), "nxl": _sb(1040), "xt": _sb(4 * A2, "bfloat16"), "wt": _sb(3072, "bfloat16"),
+    "ic": _sb(320), "ict": _sb(320), "cf": _sb(16), "ioL": _sb(1536), "cl": _sb(32, "uint16"), "rl": _sb(12),
+    "cdest": _sb(V), "ci": _sb(V), "iw": _sb(64), "iw2": _sb(32), "ie": _sb(48), "mk": _sb(32),
     "o1": _sb(64, "int32"), "off1": _sb(12, "uint16"), "stu": _sb(12, "uint16"), "b1s": _sb(16),
     "n1r": _sb(V), "n1t": _sb(V), "jf": _sb(6), "m1": _sb(6, "uint16"), "land1": _sb(48, "uint16"), "di": _sb(8, "int32"),
     "f1": _sb(V, "bfloat16"), "f1t": _sb(V, "bfloat16"), "c1L": _sb(V, "bfloat16"), "sg": _sb(2 * V, "bfloat16"), "cnt1": _sb(2),
     "x1": _sb(64), "x1t": _sb(64), "w1": _sb(16), "s1off": _sb(16, "uint16"),
-    "zf": _sb(48), "off2": _sb(16, "uint16"), "c1u": _sb(12, "uint16"), "n2r": _sb(V), "n2t": _sb(V), "xo": _sb(12, "uint16"),
-    "fl": _sb(V), "junk": _sb(V), "tot": _sb(2), "px": _sb(96), "pxt": _sb(96), "init": _sb(1), "cnt": _sb(V), "val": _sb(V),
-    "vt": _sb(V), "seg": _sb(V), "c0u": _sb(12, "uint16"), "t1": _sb(V), "vals": _sb(V), "m2": _sb(26, "uint16"),
+    "zf": _sb(48), "off2": _sb(16, "uint16"), "n2r": _sb(V), "n2t": _sb(V), "xo": _sb(12, "uint16"),
+    "fl": _sb(V), "junk": _sb(V), "tot": _sb(2), "px": _sb(96), "pxt": _sb(96), "init": _sb(1), "cnt": _sb(V), "fb": _sb(V),
+    "fbt": _sb(V), "vt": _sb(V), "seg": _sb(V), "c0u": _sb(12, "uint16"), "vals": _sb(V), "m2": _sb(26, "uint16"),
     "land2": _sb(N * ML, "uint16"), "tab2": _sb(RB + 272), "y2": _sb(544), "g2": _sb(64), "r2": _sb(64), "p2off": _sb(32, "uint16"),
-    "mi": _sb(32, "int32"), "kk": _sb(96), "z2": _sb(N * ML), "zz": _sb(176), "bsum": _sb(1), "xe": _sb(12, "uint16"),
-    "fe": _sb(V), "pe": _sb(V), "pt": _sb(V), "po": _sb(12, "uint16"), "d0u": _sb(12, "uint16"), "d1u": _sb(12, "uint16"),
-    "x3": _sb(V), "x3t": _sb(V), "t3": _sb(V), "v3": _sb(V), "v4": _sb(V), "tab3": _sb(RB + M + 16), "y3": _sb(608),
-    "g3": _sb(160), "r3": _sb(160), "fo": _sb(54, "uint16"), "ki": _sb(64, "int32"), "x5": _sb(64), "x5t": _sb(64),
-    "q0": _sb(TN + 8, X4), "s0": _sb(TN + 8, "uint8"), "wq": _sb(768, X4), "ws": _sb(768, "uint8"),
+    "mi": _sb(32, "int32"), "kk": _sb(112), "z2": _sb(N * ML), "zz": _sb(176), "bsum": _sb(1), "xe": _sb(12, "uint16"),
+    "fe": _sb(V), "de": _sb(V), "pe": _sb(V), "pt": _sb(V), "po": _sb(12, "uint16"), "d0u": _sb(12, "uint16"),
+    "d1u": _sb(12, "uint16"), "x3": _sb(V), "x3t": _sb(V), "t3": _sb(V), "v3": _sb(V), "v4": _sb(V), "tab3": _sb(RB + M + 16),
+    "y3": _sb(608), "g3": _sb(160), "r3": _sb(160), "fo": _sb(54, "uint16"), "ki": _sb(64, "int32"), "x5": _sb(64), "x5t": _sb(64),
+    "q0": _sb(A2, X4), "s0": _sb(A2, "uint8"), "wq": _sb(768, X4), "ws": _sb(768, "uint8"),
     "stq": _sb(V, X4), "sts": _sb(V, "uint8"), "p1q": _sb(256, X4), "p1s": _sb(256, "uint8"),
     "q1": _sb(QW, X4), "s1": _sb(QW, "uint8"), "p2q": _sb(512, X4), "p2s": _sb(512, "uint8"),
     "q2": _sb(QW, X4), "s2": _sb(QW, "uint8"), "fq": _sb(3 * M, X4), "fs": _sb(3 * M, "uint8"),
     "yo0": _sb(M), "yo1": _sb(M), "ps": ("psum", [128, 1024], "float32"),
 }
-SEMAPHORES = ["cv", "cs_", "ct", "cg", "dst", "dbt", "dnx", "dnw", "dnl", "dx", "dw0", "dw1", "dc1", "dm1", "dm2", "dq1", "dq2", "dq3",
-              "dy0", "dy1", "did", "sent", "al1", "aq1", "as1", "al2", "aq2", "as2"]
+SEMAPHORES = ["cv", "cs_", "ct", "cg", "dst", "ds2", "dbt", "dnx", "dnw", "dn0", "dnl", "dx", "dw0", "dw1", "dc1", "dm1", "dm2",
+              "dq1", "dq2", "dy0", "dy1", "did", "sent", "sent1", "sent2", "al1", "aq1", "as1", "al2", "aq2", "as2", "aq3", "as3"]
 
 
 def _parts(core, others, topo):
@@ -162,171 +163,197 @@ def rank_program(g, core, T, topo):
     rest = lambda c: [b for b in T.cores if b != c]
     place = lambda c: DstId(rid=topo.addr(c)[0], pnc=topo.addr(c)[1])
 
-    def send(r_, s, w_, src, dst):
+    def send(r_, s, w_, src, dst, left="sent", only=lambda a, b: True):
         deps("g", r_.split(), [])
         engines = _split(core, others, topo)
         g.remote_dma_fused([RemoteDMATransfer(dst_ids=[place(c)], dma_engine_mask=_mask(engines[c]), remote_sem=sem[s],
-                                              src=src(T.rank_of(c)), dst=dst) for c in others], local_sem=sem.sent)
-        total["sent"] = total.get("sent", 0) + sum(len(engines[c]) for c in others)
-        total[s] = sum(len(_split(c, rest(c), topo)[core]) for c in others)
+                                              src=src(T.rank_of(c)), dst=dst) for c in others if only(core, c)], local_sem=sem[left])
+        total[left] = total.get(left, 0) + sum(len(engines[c]) for c in others if only(core, c))
+        wrote[left] = [(left, None)]
+        total[s] = sum(len(_split(c, rest(c), topo)[core]) for c in others if only(c, core))
         wrote.setdefault(w_, []).append((s, total[s]))
 
-    def spread(r_, s, w_, src, dst):
+    def spread(r_, s, w_, src, dst, left):
         deps("g", r_.split(), [])
         parts = _parts(core, others, topo)
         g.remote_dma_fused([RemoteDMATransfer(dst_ids=[place(c) for c in part], dma_engine_mask=_mask(free), remote_sem=sem[s],
-                                              srcs=[src], dsts=[dst] * len(part)) for part, free in parts], local_sem=sem.sent)
-        total["sent"] = total.get("sent", 0) + sum(len(free) for part, free in parts)
+                                              srcs=[src], dsts=[dst] * len(part)) for part, free in parts], local_sem=sem[left])
+        total[left] = total.get(left, 0) + sum(len(free) for part, free in parts)
+        wrote[left] = [(left, None)]
         total[s] = sum(len(free) for c in others for part, free in _parts(c, rest(c), topo) if core in part)
         wrote.setdefault(w_, []).append((s, total[s]))
 
     fill("nxrow", T.nxrow[:], 0)
-    for k in range(8):
+    for k in range(2):
         dma("s", "dst", "", "stw", T.stw[16 * k:16 * k + 16, :], T.st[:])
         dma("y", "dbt", "", "btw", T.btw[16 * k:16 * k + 16, :], T.bt[:])
     for k in range(4):
         dma("s", "dnw", "", "nxw", T.nxw[16 * k:16 * k + 16, :], T.nx[:, 32 * (k // 2):32 * (k // 2) + 32])
-        dma("y", "dnx", "", "nxrow", T.nxrow[32 * k:32 * k + 1, :], T.nx[:])
-    dma("y", "dx", "", "xt", T.xt[:, 32:2080], T.x[:])
+    for k in range(2, 8):
+        dma("y", "ds2", "", "stw2", T.stw[16 * k:16 * k + 16, :], T.st[:])
+    dma("y", "dnx", "", "nxrow", T.nxrow[0:1, :], T.nx[:])
+    dma("y", "dx", "", "xt", T.xt[:, 4 * XB:4 * A2], T.x[:])
+    dma("y", "dw1", "", "wt1", T.wt[:, 1536:3072], T.w[:, 1536:3072])
 
-    ic, ict, cf, cl, ioL = T.ic, T.ict, T.cf, T.cl, T.ioL
-    iota("ioL0", ioL[:, 0:256], [[1, 256]], 0)
+    ic, ict, cf, cl, ioL, iw, iw2, ie = T.ic, T.ict, T.cf, T.cl, T.ioL, T.iw, T.iw2, T.ie
     iota("ic", ic[:, 0:32], [[1, 2], [2, 16]], 0)
+    iota("ioL0", ioL[:, 0:256], [[1, 256]], 0)
     iota("ic", ic[:, 32:64], [[8, 2], [0, 8], [128, 2]], 4, 1)
     iota("ic", ic[:, 64:96], [[0, 2], [8, 8], [48, 2]], 0, 3)
     iota("ic", ic[:, 96:128], [[0, 2], [1, 16]], 0)
     iota("ic", ic[:, 128:160], [[1, 2], [0, 16]], 0)
     iota("rl", T.rl[:], [[1, 6], [0, 2]], 0)
-    iota("ic1", ic[:, 160:192], [[0, 2], [32, 16]], RB - 1)
-    iota("cdest", T.cdest[:], [[0, 12], [1, 8], [0, 2]], 0)
-    iota("ic2", ic[:, 168:192:16], [[16, 2]], 0, after="ic1")
+    iota("ic1", ic[:, 160:192], [[0, 2], [32, 16]], RB - 33)
+    iota("ic2", ic[:, 192:208], [[32, 4], [1, 2], [288, 2]], 1)
+    iota("ic2", ic[:, 208:224], [[32, 4], [1, 2], [-256, 2]], 257)
+    iota("ic2", ic[:, 160:192:16], [[16, 2]], 0, after="ic1")
     iota("ic2", ic[:, 169:192:16], [[32, 2]], A1 - 1, 2)
-    iota("ic2", ic[:, 192:208], [[32, 4], [-1, 2], [288, 2]], 1)
-    iota("ic2", ic[:, 208:224], [[32, 4], [-1, 2], [-256, 2]], 257)
     iota("ic2", ic[:, 170:192:16], [[0, 2]], 0)
     iota("ic2", ic[:, 224:256], [[1, 32]], 0, 1)
-    fill("di", T.di[:], 0)
-    fill("xz", T.xt[:, 0:32], 0.0)
+    iota("cdest", T.cdest[:], [[0, 12], [1, 8], [0, 2]], 0)
+    for a, b in ((32, 64), (64, 128)):
+        fill("btz", T.btw[a:b, :], 0)
+        fill("offz", T.off1[a:b, :], 0)
+    fill("m1z", T.m1[:], 0)
+    fill("diz", T.di[:, 6:8], 0)
+    fill("xz", T.xt[:, 0:4 * XB], 0.0)
     fill("x1", T.x1[:], 0.0)
     fill("tot0", T.tot[0:32, 1:2], 0.0)
     fill("pxc", T.px[:, 32:48], 0.0)
     fill("x5", T.x5[0:32, :], 0.0)
-    turn("ic", "ict", ict[:, 0:160], ic[:, 0:160])
     f = lambda j: cf[:, j:j + 1]
     q15, odd = ict[:, 96:97], ict[:, 128:129]
-    ts("ict", "bl", cl[:, 0:1], ict[:, 0:1], 11.0, A.min)
     for k in range(1, 6):
         act("ioL0", "ioL", ioL[:, 256 * k:256 * k + 256], ioL[:, 0:256], F.Identity, bias=256.0 * k)
-    act("ioL0 ioL", "nxl", T.nxl[:], ioL[:, 0:1040], F.Identity, bias=2.0 * N * TN, scale=0.0)
 
     o1 = T.o1
-    ts("btw", "b0", o1[:, 0:12], T.btw[:], 1, A.bitwise_and)
-    ts("stw", "e0", o1[:, 24:36], T.stw[:], 2, A.mult)
-    tt("e0 b0", "e1", o1[:, 36:48], o1[:, 24:36], o1[:, 0:12], A.add)
-    ts("btw bl", "b1s", T.b1s[:], T.btw[:].indirect(cl[:, 0:1]), 2.0, A.is_ge)
-    ts("e1", "e2", o1[:, 48:60], o1[:, 36:48], 1025, A.mult)
+    ts("btw", "b0", o1[0:32, 0:12], T.btw[0:32, :], 1, A.bitwise_and)
+    ts("stw", "e0", o1[0:32, 24:36], T.stw[0:32, :], 2, A.mult)
+    turn("ic", "ict", ict[:, 0:160], ic[:, 0:160])
+    tt("e0 b0", "e1", o1[0:32, 36:48], o1[0:32, 24:36], o1[0:32, 0:12], A.add)
     copy("nxw", "nxf", T.nxf[0:64, :], T.nxw[0:64, :])
-    ts("e2", "e3", o1[:, 12:24], o1[:, 48:60], 4, A.arith_shift_right, 1023, A.bitwise_and)
+    ts("ict", "bl", cl[:, 0:1], ict[:, 0:1], 11.0, A.min)
+    ts("e1", "e2", o1[0:32, 48:60], o1[0:32, 36:48], 1025, A.mult)
     turn("nxf", "nxt", T.nxt[0:64, :], T.nxf[0:64, :])
-    copy("e3", "off1", T.off1[:], o1[:, 12:24])
+    ts("ioL0 ict", "iw2", iw2[:], ioL[:, 0:32], q15, A.is_equal)
+    ts("e2", "e3", o1[0:32, 12:24], o1[0:32, 48:60], 4, A.arith_shift_right, 1023, A.bitwise_and)
     copy("rl", "rlu", cl[:, 2:14], T.rl[:])
-    ts("nxrow off1", "n1r", T.n1r[:], T.nxrow[:].indirect(T.off1[:]), 2.0, A.mult)
-    turn("n1r", "n1t", T.n1t[:], T.n1r[:])
-    tt("n1t b1s", "jf", T.jf[:], T.n1t[:, 0:V:32], T.b1s[:, 0:6], A.add)
-    ts("n1t", "di", T.di[:, 0:6], T.n1t[:, 0:V:32], 1.0 / 1024, A.mult, -0.4995, A.add)
-    copy("jf", "m1", T.m1[:], T.jf[:])
-    spread("m1", "al1", "land1", T.m1[:], T.land1[:, 6 * r:6 * r + 6])
+    ts("btw btz bl", "b1s", T.b1s[:], T.btw[:].indirect(cl[:, 0:1]), 2.0, A.is_ge)
+    copy("e3", "off1", T.off1[0:32, :], o1[0:32, 12:24])
+    ts("ict", "even", f(2), odd, -1.0, A.mult, 1.0, A.add)
+    ts("ict", "q31", f(3), odd, 16.0, A.mult, q15, A.add)
+    ts("nxrow off1 offz", "n1r", T.n1r[:], T.nxrow[:].indirect(T.off1[:]), 2.0, A.mult)
+    ts("ict", "sb", f(0), ict[:, 32:33], -0.125, A.mult)
+    ts("ict", "sb", f(1), ict[:, 32:33], -0.125, A.mult, -2.0, A.add)
+    turn("n1r", "n1t", T.n1t[0:32, :], T.n1r[0:32, :])
+    ts("ic q31", "iwf", iw[:, 32:64], ic[:, 96:128], f(3), A.is_equal)
+    ts("ic ict", "mk", T.mk[:], ic[:, 96:128], q15, A.is_equal)
+    tt("n1t b1s", "jf", T.jf[0:32, :], T.n1t[0:32, 0:V:32], T.b1s[0:32, 0:6], A.add)
+    for k in range(4):
+        ts("n1t", "di", T.di[32 * k:32 * k + 32, 0:6], T.n1t[0:32, 0:V:32], 1.0 / 1024, A.mult, -0.4995, A.add)
+        if k == 1:
+            copy("jf m1z", "m1", T.m1[32 * (r // 2):32 * (r // 2) + 32, :], T.jf[0:32, :])
+    spread("m1", "al1", "land1", T.m1[:], T.land1[:, 6 * r:6 * r + 6], "sent1")
+    act("iw2", "m1c", f(8), iw2[:, 1:2], F.Identity, scale=XB - 4 - BIG, bias=BIG)
+    for k in range(2):
+        act("ioL0 ioL iw2 m1c", "nxl", T.nxl[:, k:1040:2], ioL[:, 0:520], F.Identity, bias=f(8), scale=iw2[:, 1:2])
     dma("s", "dm1", "m1", "land1o", T.land1[:, 6 * r:6 * r + 6], T.m1[:])
-    for k in range(8):
-        dma("y", "dnl", "nxt", "nxl", T.nxl[16 * k:16 * k + 1, 8:1032], T.nxt[0:64, 0:16])
-    dma("y", "dw1", "", "wt1", T.wt[:, 1536:3072], T.w[:, 1536:3072])
-    iota("keep", T.keep[:], [[0, 12], [4096, 16]], 0)
+    dma("y", "dn0", "nxt", "nxl0 nxl", T.nxl[0:1, 8:1032], T.nxt[0:64, 0:16])
+    dma("y", "dw0", "", "wt0", T.wt[:, 0:1536], T.w[:, 0:1536])
+    for k in range(1, 8):
+        dma("y", "dnl", "nxl0", "nxl1", T.nxl[16 * k:16 * k + 1, 8:1032], T.nxl[0:1, 8:1032])
     iota("ic3", ic[:, 256:272], [[32, 2], [320, 2], [1, 4]], 0)
     iota("ic3", ic[:, 272:288], [[32, 2], [-288, 2], [1, 4]], 288)
     iota("ic3", ic[:, 288:320], [[256, 2], [1, 16]], 257, 16)
 
-    iw, iw2, ie = T.iw, T.iw2, T.ie
-    tt("di rlu cdest", "f1", T.f1[:], T.di[:].indirect(cl[:, 2:14]), T.cdest[:], A.is_equal)
-    ts("ict", "sb", f(0), ict[:, 32:33], -0.125, A.mult)
-    ts("ict", "sb", f(1), ict[:, 32:33], -0.125, A.mult, -2.0, A.add)
+    def quant_x(w_, q, s, k):
+        h = A2 // 4
+        quant("xt xz", w_, q[:, h * k:h * k + h], s[:, h * k:h * k + h], T.xt[:, 4 * h * k:4 * h * k + 4 * h])
+
+    def quant_w(k):
+        quant("wt%d" % (k // 3), "wq%d" % k, T.wq[:, 128 * k:128 * k + 128], T.ws[:, 128 * k:128 * k + 128], T.wt[:, 512 * k:512 * k + 512])
+
+    ts("stw stw2", "stu", T.stu[:], T.stw[:], float(XB), A.add)
+    tt("di diz rlu cdest", "f1", T.f1[:], T.di[:].indirect(cl[:, 2:14]), T.cdest[:], A.is_equal)
+    quant_x("q0 s0", T.q0, T.s0, 0)
     turn("f1", "f1t", T.f1t[:], T.f1[:])
-    ts("ioL0 ict", "iw2", iw2[:], ioL[:, 0:32], q15, A.is_equal)
+    quant_x("q0 s0", T.q0, T.s0, 1)
     scan("f1t", "c1L", T.c1L[:], T.f1t[:], T.f1t[:], 0.0, A.add, A.max)
     for k in range(2):
         act("c1L sb", "cnt1 sg", T.sg[:, V * k:V * k + V], T.c1L[:], F.Sign, bias=f(k), accum_out=T.cnt1[:, k:k + 1])
-    ts("stw", "stu", T.stu[:], T.stw[:], 8.0, A.add)
+    quant_x("q0 s0", T.q0, T.s0, 2)
+    quant_x("q0 s0", T.q0, T.s0, 3)
     turn("ic2", "ict2", ict[:, 160:256], ic[:, 160:256])
-    ts("ict", "even", f(2), odd, -1.0, A.mult, 1.0, A.add)
-    ts("ict", "q31", f(3), odd, 16.0, A.mult, q15, A.add)
+    ts("ict even iwf", "iwf", iw[:, 41:64:16], ict[:, 96:98], 9.0, A.is_lt, f(2), A.mult)
+    fill("iwf", iw[:, 32:64:16], 1.0)
     ts("ict2", "m9", f(4), ict[:, 224:225], 16.0 * r + 9, A.is_equal)
-    ts("ict", "dg", cl[:, 14:15], ict[:, 64:65], 0.125, A.mult, 47.0, A.min)
     ts("cnt1", "x1", T.x1[:, 0:64:32], T.cnt1[:], -0.5, A.mult, V / 2.0, A.add)
-    ts("ic q31", "iwf", iw[:, 32:64], ic[:, 96:128], f(3), A.is_equal)
+    ts("ict", "dg", cl[:, 14:15], ict[:, 64:65], 0.125, A.mult, 47.0, A.min)
+    turn("iwf", "iw", iw[:, 0:32], iw[:, 32:64])
     turn("x1", "x1t", T.x1t[:], T.x1[:])
     for k in range(8):
         dma("y" if k % 2 else "s", "dc1", "x1t", "w1", T.w1[16 * k:16 * k + 16, :], T.x1t[0:128:32, :])
-    ts("ict even iwf", "iwf", iw[:, 41:64:16], ict[:, 96:98], 8.0, A.is_lt, f(2), A.mult)
-    fill("iwf", iw[:, 32 + r:64:16], 0.0)
-    fill("iwf", iw[:, 40:64:16], 1.0)
-    ts("ic ict", "mk", T.mk[:], ic[:, 96:128], q15, A.is_equal)
-    ts("ioL0 q31 ict2", "pxc", T.px[:, 64:96], ioL[:, 0:32], f(3), A.is_equal, ict[:, 160:161], A.mult)
-    turn("iwf", "iw", iw[:, 0:32], iw[:, 32:64])
-    ts("ioL0 ict2", "la", cl[:, 16:18], ioL[:, 0:129:128], ict[:, 192:193], A.add)
-    for k in range(2):
-        quant("xt xz", "q0 s0", T.q0[:, 260 * k:260 * k + 260], T.s0[:, 260 * k:260 * k + 260], T.xt[:, 1040 * k:1040 * k + 1040])
     pick("q0", "s0", "stq", "sts", T.stq[:], T.sts[:], T.q0[:], T.s0[:], T.stu[:], "stu")
     move("y", "dq1", "stq", "sts", "q1s", T.q1, T.s1, SB, T.stq, T.sts, 0, V)
     act("ioL m9", "ci", T.ci[:], ioL[:, SB:SB + V], F.Identity, scale=f(4))
-    quant("xt", "q1x", T.q1[:, XB:XB + TN], T.s1[:, XB:XB + TN], T.xt[:, 32:2080])
+    act("iw2", "nb", f(5), iw2[:, r + 1:r + 2], F.Identity, scale=-BIG, bias=BIG)
+    act("ioL0 ioL", "tab2", T.tab2[:], ioL[:, 0:RB + 272], F.Identity, scale=0.0)
+    ts("ioL0 q31 ict2", "pxc", T.px[:, 64:96], ioL[:, 0:32], f(3), A.is_equal, ict[:, 160:161], A.mult)
+    ts("ioL0 ict2", "la", cl[:, 16:18], ioL[:, 0:129:128], ict[:, 192:193], A.add)
+    quant("xt", "q1x", T.q1[:, XB:A2], T.s1[:, XB:A2], T.xt[:, 4 * XB:4 * A2])
+    turn("ic3", "ict3", ict[:, 256:320], ic[:, 256:320])
+    for k in range(4):
+        quant_x("q2x", T.q2, T.s2, k)
     ts("w1", "s1off", T.s1off[:], T.w1[:], V - 1.0, A.min)
+    ts("ioL0 ioL ict3", "le", cl[:, 18:23], ioL[:, 0:257:64], ict[:, 256:257], A.add, 590.0, A.min)
     pick("stq", "sts", "p1q", "p1s", T.p1q[:], T.p1s[:], T.stq[:], T.sts[:], T.s1off[:], "s1off")
     at1 = A1 + CAP * r
-    send("p1q", "aq1", "q1a", lambda d: T.p1q[:, CAP * d:CAP * d + CAP].bitcast(dt.uint8), T.q1[:, at1:at1 + CAP].bitcast(dt.uint8))
-    send("p1s", "as1", "s1a", lambda d: T.p1s[:, CAP * d:CAP * d + CAP], T.s1[:, at1:at1 + CAP])
-    quant("wt1", "wq1", T.wq[:, 384:768], T.ws[:, 384:768], T.wt[:, 1536:3072])
-    for a, b in ((A1, at1), (at1 + CAP, A1 + N * CAP)):
-        if b > a:
-            move("y", "dq2", "q1a", "s1a", "q2o", T.q2, T.s2, a, T.q1, T.s1, a, b - a)
-    move("y", "dq2", "stq", "sts", "q2o", T.q2, T.s2, SB, T.stq, T.sts, 0, V)
-    move("y", "dq2", "q0", "s0", "q2o", T.q2, T.s2, 0, T.q0, T.s0, 0, 8)
+    send("p1q", "aq1", "q1a", lambda d: T.p1q[:, CAP * d:CAP * d + CAP].bitcast(dt.uint8), T.q1[:, at1:at1 + CAP].bitcast(dt.uint8), "sent1")
+    send("p1s", "as1", "s1a", lambda d: T.p1s[:, CAP * d:CAP * d + CAP], T.s1[:, at1:at1 + CAP], "sent1")
 
-    m2, tot, px, mi, kk = T.m2, T.tot, T.px, T.mi, T.kk
+    m2, tot, px, mi, kk, vt = T.m2, T.tot, T.px, T.mi, T.kk, T.vt
+    cba, c1m, bc, d1, d0, pa, c0m, cbb = (kk[:, 12 * k:12 * k + 12] for k in range(8))
     copy("land1 land1o", "zf", T.zf[:], T.land1[:])
+    quant_w(5)
     ts("zf dg", "off2", T.off2[:], T.zf[:].indirect(cl[:, 14:15]), 8.0 - 1024 * r, A.add, 1032.0, A.min)
-    copy("nxl off2", "n2r", T.n2r[:], T.nxl[:].indirect(T.off2[:, 0:12]))
-    ts("off2", "c1u", T.c1u[:], T.off2[:, 0:12], 0.5, A.mult, XB - 4.25, A.add)
-    turn("n2r", "n2t", T.n2t[:], T.n2r[:])
-    ts("n2t", "xo", T.xo[:], T.n2t[:, 0:V:16], 1.0 / TN, A.mult, -0.499, A.add)
-    act("iw2 xo", "tot junk", T.junk[:], iw2[:].indirect(T.xo[:]), F.Identity, accum_out=tot[:, 0:1])
-    act("ioL0 ioL c1u iw2", "t1", T.t1[:], ioL[:].indirect(T.c1u[:]), F.Identity, scale=iw2[:, 1:2])
-    act("ioL0 ioL iw2", "wa", T.wa[:], ioL[:, 0:QW], F.Identity, scale=iw2[:, 0:1])
-    act("ioL0 ioL", "tab2", T.tab2[:], ioL[:, 0:RB + 272], F.Identity, scale=0.0)
-    act("ioL0 ioL", "tab3", T.tab3[:], ioL[:, 0:RB + M + 16], F.Identity, scale=0.0)
-    act("ioL0", "x3", T.x3[:], ioL[:, 0:V], F.Identity, scale=0.0)
-    copy("iw xo", "fl", T.fl[:], iw[:, 0:32].indirect(T.xo[:]))
-    ts("n2t", "m2a", m2[:, 0:12], T.n2t[:, 0:V:16], -1.0, A.mult, float(N * TN), A.add)
-    tt("tot", "u2", tot[64:96, 1:2], tot[0:32, 0:1], tot[32:64, 0:1], A.add)
-    copy("tot", "u1", tot[32:64, 1:2], tot[0:32, 0:1])
-    ts("iw2 tot even", "pxb", px[:, 48:64], iw2[:, 0:16], tot[:, 0:1], A.mult, f(2), A.mult)
-    tt("tot u2", "u3", tot[96:128, 1:2], tot[64:96, 1:2], tot[64:96, 0:1], A.add)
     ts("zf dg", "mi", mi[:, 0:16], T.zf[:].indirect(cl[:, 14:15]), 1.0 / 1024, A.mult, -0.4995, A.add)
-    ts("mk tot0 u1 u2 u3", "pxa", px[:, 0:32], T.mk[:, 0:32], tot[:, 1:2], A.mult)
+    copy("nxl nxl1 off2", "n2r", T.n2r[:], T.nxl[:].indirect(T.off2[:, 0:12]))
+    quant_w(4)
+    turn("n2r", "n2t", T.n2t[:], T.n2r[:])
+    quant_w(3)
+    ts("n2t", "xo", T.xo[:], T.n2t[:, 0:V:16], 1.0 / TN, A.mult, 0.501, A.add)
+    ts("n2t", "m2a", m2[:, 0:12], T.n2t[:, 0:V:16], -1.0, A.mult, float(N * TN), A.add)
+    ts("mi", "cba", cba, mi[:, 0:12], 64.0, A.mult, float(A2 + 32 - RB - CAP * r), A.add)
+    act("iw2 xo", "tot junk", T.junk[:], iw2[:].indirect(T.xo[:]), F.Identity, accum_out=tot[:, 0:1])
+    copy("iw xo", "fl", T.fl[:], iw[:, 0:32].indirect(T.xo[:]))
+    act("fl nb", "fb", T.fb[:], T.fl[:], F.Identity, scale=f(5))
+    act("ioL0 ioL", "tab3", T.tab3[:], ioL[:, 0:RB + M + 16], F.Identity, scale=0.0)
+    act("ioL0", "x3z", T.x3[:], ioL[:, 0:V], F.Identity, scale=0.0, bias=BIG)
+    quant_w(2)
+    copy("tot", "u1", tot[32:64, 1:2], tot[0:32, 0:1])
+    ts("tot", "u2", tot[64:96, 1:2], tot[0:32, 0:1], tot[32:64, 0:1], A.add)
+    ts("tot", "u3", tot[96:128, 1:2], tot[0:32, 0:1], tot[32:64, 0:1], A.add, tot[64:96, 0:1], A.add)
+    ts("iw2 tot even", "pxb", px[:, 48:64], iw2[:, 0:16], tot[:, 0:1], A.mult, f(2), A.mult)
     ts("off2", "c1i", mi[:, 16:28], T.off2[:, 0:12], 0.5, A.mult, XB + 32 - 4.25, A.add)
+    ts("mk tot0 u1 u2 u3", "pxa", px[:, 0:32], T.mk[:], tot[:, 1:2], A.mult)
+    turn("fb", "fbt", T.fbt[:], T.fb[:])
     turn("pxa pxb pxc", "pxt", T.pxt[:], px[:])
-    ts("mi", "cba", kk[:, 0:12], mi[:, 0:12], 64.0, A.mult, float(A2 + 32 - RB - CAP * r), A.add)
+    quant_w(1)
     summed("pxt", "init", T.init[:], T.pxt[:])
+    quant_w(0)
     scan("fl ci init", "cnt", T.cnt[:], T.fl[:], T.ci[:], T.init[:], A.add, A.max)
     copy("init", "m2c", m2[:, 24:25], T.init[:])
-    tt("cnt fl", "val", T.val[:], T.cnt[:], T.fl[:], A.mult)
-    turn("val", "vt", T.vt[:], T.val[:])
-    scan("keep vt", "seg", T.seg[:], T.keep[:], T.vt[:], 0.0, A.min, A.max)
-    copy("vt", "c0u", T.c0u[:], T.vt[:, 9:V:16])
+    turn("cnt", "vt", vt[:], T.cnt[:])
+    copy("vt", "c0u", T.c0u[:], vt[:, 9:V:16])
+    scan("fbt vt", "seg", T.seg[:], T.fbt[:], vt[:], 0.0, A.max, A.min)
+    tt("ioL0 ioL c0u n2r", "vals", T.vals[:], ioL[:].indirect(T.c0u[:]), T.n2r[:], A.min)
     copy("seg", "m2b", m2[:, 12:24], T.seg[:, 8:V:16])
-    spread("m2a m2b m2c", "al2", "land2", m2[:, 0:ML], T.land2[:, ML * r:ML * r + ML])
+    spread("m2a m2b m2c", "al2", "land2", m2[:, 0:ML], T.land2[:, ML * r:ML * r + ML], "sent2")
     dma("s", "dm2", "m2a m2b m2c", "land2o", T.land2[:, ML * r:ML * r + ML], m2[:, 0:ML])
-    move("y", "dq3", "q0 land2", "s0", "q2x", T.q2, T.s2, XB, T.q0, T.s0, 8, TN)
-    dma("y", "dw0", "", "wt0", T.wt[:, 0:1536], T.w[:, 0:1536])
-    tt("wa c0u t1", "vals", T.vals[:], T.wa[:].indirect(T.c0u[:]), T.t1[:], A.add)
+    for a, b in ((A1, at1), (at1 + CAP, QW)):
+        if b > a:
+            move("y", "dq2", "q1a q1s sent2", "s1a q1s", "q2o", T.q2, T.s2, a, T.q1, T.s1, a, b - a)
+    tt("vt fbt", "c0m", c0m, vt[:, 9:V:16], T.fbt[:, 9:V:16], A.min)
     op("v", "vals m2b tab2", "tab2s", lambda e: e.tensor_copy(T.tab2[:].indirect(m2[:, 12:24]), T.vals[:]))
 
     def collect(tag, tab, y, n, lst, gg, rr, w):
@@ -338,77 +365,87 @@ def rank_program(g, core, T, topo):
         tt("gb" + tag, "ra" + tag, rr[0:64, 0:w], gg[0:64, w:2 * w], gg[64:128, w:2 * w], A.add)
         tt("ra" + tag, "rb" + tag, rr[0:32, w:2 * w], rr[0:32, 0:w], rr[32:64, 0:w], A.add)
 
-    big = 8192.0
-    turn("ic3", "ict3", ict[:, 256:320], ic[:, 256:320])
-    act("iw2", "al", f(11), iw2[:, 10:11], F.Identity, scale=-big)
-    act("iw2", "al", f(12), iw2[:, 10:11], F.Identity, scale=big + RB - 2 - N * (RB - 1 + CAP * r), bias=1.0)
+    low, lift = 2.0 ** 30, N * (RB - 1 + CAP * r) - (RB - 1)
+    act("iw2", "al", f(11), iw2[:, 10:11], F.Identity, scale=-low)
+    act("iw2", "al", f(12), iw2[:, 10:11], F.Identity, scale=low + BIG, bias=1.0)
+    act("ict", "db", f(15), odd, F.Identity, scale=16.0, bias=1.0 + lift)
     act("ioL0", "oh", ie[:, 16:32], ioL[:, 0:16], F.Abs, bias=-float(r))
+    act("ict3", "k8", f(13), ict[:, 288:289], F.Identity, scale=0.125)
+    act("iw2", "b3", f(14), iw2[:, 1:2], F.Identity, scale=-BIG, bias=BIG)
     act("oh", "oh2", ie[:, 32:48], ie[:, 16:32], F.Relu, scale=-1.0, bias=1.0)
+    act("ioL0 k8 x3z", "x3", T.x3[:, 3:V:16], ioL[:, 0:V:16], F.Identity, scale=0.125, bias=f(13))
+    act("ioL0 db", "de", T.de[:], ioL[:, 0:V], F.Identity, bias=f(15))
     act("oh2 al", "ie", ie[:, 0:16], ie[:, 32:48], F.Identity, scale=f(12), bias=f(11))
-    act("ioL0 ict3", "x3", T.x3[:, 3:V:16], ioL[:, 0:V:16], F.Identity, bias=ict[:, 288:289])
+    tt("cba c0m", "cbb", cbb, cba, c0m, A.subtract)
+    tt("c1i c0m", "c1m", c1m, mi[:, 16:28], c0m, A.min)
     collect("2", T.tab2, T.y2, 256, cl[:, 16:18], T.g2, T.r2, 32)
     for k in range(4):
         ts("rb2", "p2off", T.p2off[32 * k:32 * k + 32, :], T.r2[0:32, 32:64], float(XB), A.max)
-    pick("q1x q1s q1a", "q1x q1s s1a", "p2q", "p2s", T.p2q[:], T.p2s[:], T.q1[:], T.s1[:], T.p2off[:], "p2off")
     at2 = A2 + 2 * CAP * r
-    send("p2q", "aq2", "q2a", lambda d: T.p2q[:, 64 * d:64 * d + 64].bitcast(dt.uint8), T.q2[:, at2:at2 + 64].bitcast(dt.uint8))
-    send("p2s", "as2", "s2a", lambda d: T.p2s[:, 64 * d:64 * d + 64], T.s2[:, at2:at2 + 64])
+
+    def leave(k):
+        part = _parts(core, others, topo)[k][0]
+        a, b = min(T.rank_of(c) for c in part), max(T.rank_of(c) for c in part) + 1
+        only = lambda c, d: (d in topo.cores_of(c)) == (k == 1)
+        pick("q1x q1s q1a", "q1x q1s s1a", "p2q%d" % k, "p2s%d" % k, T.p2q[:, 64 * a:64 * b], T.p2s[:, 64 * a:64 * b],
+             T.q1[:], T.s1[:], T.p2off[:, 4 * a:4 * b], "p2off")
+        send("p2q%d" % k, "aq%d" % (2 + k), "q2a", lambda d: T.p2q[:, 64 * d:64 * d + 64].bitcast(dt.uint8),
+             T.q2[:, at2:at2 + 64].bitcast(dt.uint8), only=only)
+        send("p2s%d" % k, "as%d" % (2 + k), "s2a", lambda d: T.p2s[:, 64 * d:64 * d + 64], T.s2[:, at2:at2 + 64], only=only)
+
+    leave(0)
 
     z2, zz = T.z2, T.zz
     copy("land2 land2o", "z2", z2[:], T.land2[:])
-    tt("c1i vt", "c1m", kk[:, 12:24], mi[:, 16:28], T.vt[:, 9:V:16], A.min)
+    leave(1)
     tt("z2", "za", zz[:, 0:100], z2[:, 0:100], z2[:, 100:200], A.max)
     summed("z2", "bsum", T.bsum[:], z2[:, 24:200:ML])
     tt("za", "zb", zz[:, 100:150], zz[:, 0:50], zz[:, 50:100], A.max)
     tt("zb", "zc", zz[:, 150:175], zz[:, 100:125], zz[:, 125:150], A.max)
     an, bn = zz[:, 150:162], zz[:, 162:174]
     ts("zc", "xe", T.xe[:], an, -1.0 / TN, A.mult, N - 0.499, A.add)
-    tt("zc cba", "bc", kk[:, 24:36], bn, kk[:, 0:12], A.add)
-    copy("ie xe", "fe", T.fe[:], ie[:, 0:16].indirect(T.xe[:]))
-    tt("bc c1m", "d1", kk[:, 36:48], kk[:, 24:36], kk[:, 12:24], A.max)
-    scan("fe bsum", "pe", T.pe[:], T.fe[:], T.fe[:], T.bsum[:], A.add, A.max)
-    ts("d1", "d1u", T.d1u[:], kk[:, 36:48], -32.0, A.add)
-    act("ioL0 ioL d1u iw2", "t3", T.t3[:], ioL[:].indirect(T.d1u[:]), F.Identity, scale=iw2[:, 1:2])
-    turn("pe", "pt", T.pt[:], T.pe[:])
-    ts("zc", "x3", T.x3[:, 2:V:16], an, -1.0, A.mult, float(8 + TN * (N - r)), A.add)
-    tt("pt", "pa", kk[:, 60:72], T.pt[:, r:V:16], T.pt[:, 10:V:16], A.add)
-    tt("bc vt", "d0", kk[:, 48:60], kk[:, 24:36], T.vt[:, 9:V:16], A.max)
+    act("ie xe", "fe", T.fe[:], ie[:, 0:16].indirect(T.xe[:]))
+    tt("zc cbb", "bc", bc, bn, cbb, A.add)
+    ts("zc x3z", "x3", T.x3[:, 2:V:16], an, -1.0, A.mult, float(XB + TN * (N - r)), A.add)
+    tt("bc c1m", "d1", d1, bc, c1m, A.max)
+    tt("bc c0m", "d0", d0, bc, c0m, A.max)
     turn("x3", "x3t", T.x3t[:], T.x3[:])
-    copy("d0", "d0u", T.d0u[:], kk[:, 48:60])
-    tt("pa vt", "pb", kk[:, 72:84], kk[:, 60:72], T.vt[:, 8:V:16], A.max)
-    tt("wa d0u x3t", "v3", T.v3[:], T.wa[:].indirect(T.d0u[:]), T.x3t[:], A.add)
-    copy("pb", "po", T.po[:], kk[:, 72:84])
-    ts("ioL0 ioL ict3", "le", cl[:, 18:23], ioL[:, 0:257:64], ict[:, 256:257], A.add, 590.0, A.min)
-    tt("v3 t3", "v4", T.v4[:], T.v3[:], T.t3[:], A.add)
+    ts("d1", "d1u", T.d1u[:], d1, -32.0, A.add)
+    act("ioL0 ioL d1u b3", "t3", T.t3[:], ioL[:].indirect(T.d1u[:]), F.Identity, scale=iw2[:, 1:2], bias=f(14))
+    copy("d0", "d0u", T.d0u[:], d0)
+    scan("fe de bsum", "pe", T.pe[:], T.fe[:], T.de[:], T.bsum[:], A.add, A.max)
+    tt("ioL0 ioL d0u x3t", "v3", T.v3[:], ioL[:].indirect(T.d0u[:]), T.x3t[:], A.min)
+    turn("pe", "pt", T.pt[:], T.pe[:])
+    tt("v3 t3", "v4", T.v4[:], T.v3[:], T.t3[:], A.min)
+    tt("pt", "pa", pa, T.pt[:, r + 1:V:16], T.pt[:, 10:V:16], A.min)
+    ts("pa", "po", T.po[:], pa, -float(lift), A.add)
     op("v", "v4 po tab3", "tab3s", lambda e: e.tensor_copy(T.tab3[:].indirect(T.po[:]), T.v4[:]))
     collect("3", T.tab3, T.y3, M, cl[:, 18:23], T.g3, T.r3, 80)
     for k in range(3):
         copy("rb3", "fo0", T.fo[0:32, 18 * k:18 * k + 18], T.r3[0:32, 80 + k:152:4])
+    ki = T.ki
+    ts("rb3", "k0", ki[0:32, 0:18], T.r3[0:32, 83:152:4], 8.0, A.mult)
     for k in range(1, 4):
         copy("fo0", "fo", T.fo[32 * k:32 * k + 32, :], T.fo[0:32, :])
+    ts("k0", "k1", ki[0:32, 18:36], ki[0:32, 0:18], 8, A.arith_shift_right)
+    ts("k0", "k2", ki[0:32, 36:54], ki[0:32, 0:18], 255, A.bitwise_and)
 
     for k in (2, 1, 0):
         src = ("q0", "s0", T.q0[:], T.s0[:]) if k == 2 else ("q2o q2x q2a", "q2o q2x s2a", T.q2[:], T.s2[:])
-        pick(src[0], src[1], "fq%d" % k, "fs%d" % k, T.fq[:, M * k:M * k + M], T.fs[:, M * k:M * k + M],
-             src[2], src[3], T.fo[:, 18 * k:18 * k + 18], "fo0 fo")
-        if k == 2:
-            quant("wt0", "wq0", T.wq[:, 0:384], T.ws[:, 0:384], T.wt[:, 0:1536])
+        pick(src[0], src[1], "fq%d" % k, "fs%d" % k, T.fq[:, M * k:M * k + M], T.fs[:, M * k:M * k + M], src[2], src[3],
+             T.fo[:, 18 * k:18 * k + 18], "fo0 fo")
         for o in range(2):
             c = 128 * (2 * k + o)
-            op("t", "fq%d fs%d wq%d" % (k, k, c // 384), "ps%d" % o, lambda e: e.matmul_mx(
+            op("t", "fq%d fs%d wq%d" % (k, k, c // 128), "ps%d" % o, lambda e: e.matmul_mx(
                 T.ps[:, 512 * o:512 * o + M], T.wq[:, c:c + 128], T.ws[:, c:c + 128], T.fq[:, M * k:M * k + M],
                 T.fs[:, M * k:M * k + M], k == 2, k == 0))
-    ki = T.ki
-    copy("rb3", "k0", ki[0:32, 0:18], T.r3[0:32, 83:152:4])
-    ts("k0", "k1", ki[0:32, 18:36], ki[0:32, 0:18], 8, A.arith_shift_right)
-    ts("k0", "k2", ki[0:32, 36:54], ki[0:32, 0:18], 255, A.bitwise_and)
+    for k in range(2):
+        ts("k1 k2", "x5", T.x5[0:32, 32 * k:32 * k + 18], ki[0:32, 18 + 18 * k:36 + 18 * k], -1.0, A.add)
+    turn("x5", "x5t", T.x5t[0:32, :], T.x5[0:32, :])
     copy("ps0", "yo0", T.yo0[:], T.ps[:, 0:M])
     dma("y", "dy0", "yo0", "y0", T.y[:, 0:M], T.yo0[:])
     act("ps1", "yo1", T.yo1[:], T.ps[:, 512:512 + M])
     dma("s", "dy1", "yo1", "y1", T.y[:, M:2 * M], T.yo1[:])
-    for k in range(2):
-        ts("k1 k2", "x5", T.x5[0:32, 32 * k:32 * k + 18], ki[0:32, 18 + 18 * k:36 + 18 * k], -1.0, A.add)
-    turn("x5", "x5t", T.x5t[0:32, :], T.x5[0:32, :])
     for k in range(2):
         dma("y", "did", "x5t", "id%d" % k, T["id"][k:k + 1, :], T.x5t[0:18, 32 * k:32 * k + 16])
     await_("g", [(s, None) for s in total])

@@ -3,10 +3,11 @@ from concourse.mybir import dt, AluOpType as A, AxisListType, ActivationFunction
 
 N = 8
 TN, V, M, CAP = 512, 192, 288, 32
-XB, A2, A1, SB, QW = 16, 528, 1040, 1296, 1488
+XB, A1, SB, A2, QW = 16, 528, 784, 976, 1488
 RB = 224
 ML = 25
 BIG = 8192.0
+LIFT = 2048
 X4 = "float8_e4m3fn_x4"
 
 
@@ -16,29 +17,29 @@ def _sb(n, d="float32"):
 
 SCRATCH = {
     "stw": _sb(12, "int32"), "btw": _sb(12, "int32"), "nxrow": _sb(1024, "int32"), "nxw": _sb(32, "int32"), "nxf": _sb(32),
-    "nxt": _sb(32), "nxl": _sb(1040), "xt": _sb(4 * A2, "bfloat16"), "wt": _sb(3072, "bfloat16"),
-    "ic": _sb(320), "ict": _sb(320), "cf": _sb(16), "ioL": _sb(1536), "cl": _sb(32, "uint16"), "rl": _sb(12),
-    "cdest": _sb(V), "ci": _sb(V), "iw": _sb(64), "iw2": _sb(32), "ie": _sb(48), "mk": _sb(32),
+    "nxt": _sb(32), "nxl": _sb(1040), "xt": _sb(4 * A1, "bfloat16"), "wt": _sb(3072, "bfloat16"),
+    "ic": _sb(320), "ict": _sb(320), "cf": _sb(16), "ioL": _sb(1024), "wa": _sb(A2 - A1), "wb": _sb(768), "cl": _sb(32, "uint16"),
+    "rl": _sb(12), "cdest": _sb(V), "ci": _sb(V), "iw": _sb(64), "iw2": _sb(32), "ie": _sb(48), "mk": _sb(32),
     "o1": _sb(64, "int32"), "off1": _sb(12, "uint16"), "stu": _sb(12, "uint16"), "b1s": _sb(16),
     "n1r": _sb(V), "n1t": _sb(V), "jf": _sb(6), "m1": _sb(6, "uint16"), "land1": _sb(48, "uint16"), "di": _sb(8, "int32"),
     "f1": _sb(V, "bfloat16"), "f1t": _sb(V, "bfloat16"), "c1L": _sb(V, "bfloat16"), "sg": _sb(2 * V, "bfloat16"), "cnt1": _sb(2),
     "x1": _sb(64), "x1t": _sb(64), "w1": _sb(16), "s1off": _sb(16, "uint16"),
     "zf": _sb(48), "off2": _sb(16, "uint16"), "n2r": _sb(V), "n2t": _sb(V), "xo": _sb(12, "uint16"),
-    "fl": _sb(V), "junk": _sb(V), "tot": _sb(2), "px": _sb(96), "pxt": _sb(96), "init": _sb(1), "cnt": _sb(V), "fb": _sb(V),
-    "fbt": _sb(V), "vt": _sb(V), "seg": _sb(V), "c0u": _sb(12, "uint16"), "vals": _sb(V), "m2": _sb(26, "uint16"),
+    "fl": _sb(V), "tot": _sb(2), "px": _sb(96), "pxt": _sb(96), "init": _sb(1), "cnt": _sb(V), "fb": _sb(V, "bfloat16"),
+    "fbt": _sb(V, "bfloat16"), "vt": _sb(V), "seg": _sb(V), "c0u": _sb(12, "uint16"), "vals": _sb(V), "m2": _sb(26, "uint16"),
     "land2": _sb(N * ML, "uint16"), "tab2": _sb(RB + 272), "y2": _sb(544), "g2": _sb(64), "r2": _sb(64), "p2off": _sb(32, "uint16"),
-    "mi": _sb(32, "int32"), "kk": _sb(112), "z2": _sb(N * ML), "zz": _sb(176), "bsum": _sb(1), "xe": _sb(12, "uint16"),
-    "fe": _sb(V), "de": _sb(V), "pe": _sb(V), "pt": _sb(V), "po": _sb(12, "uint16"), "d0u": _sb(12, "uint16"),
-    "d1u": _sb(12, "uint16"), "x3": _sb(V), "x3t": _sb(V), "t3": _sb(V), "v3": _sb(V), "v4": _sb(V), "tab3": _sb(RB + M + 16),
+    "mi": _sb(16, "int32"), "kk": _sb(64), "z2": _sb(N * ML), "zz": _sb(176), "bsum": _sb(1), "xe": _sb(12, "uint16"),
+    "fe": _sb(V), "de": _sb(V), "pe": _sb(V), "pt": _sb(V), "po": _sb(12, "uint16"), "bcu": _sb(12, "uint16"),
+    "x3": _sb(V), "x3t": _sb(V), "v3": _sb(V), "v4": _sb(V), "tab3": _sb(RB + M + 16),
     "y3": _sb(608), "g3": _sb(160), "r3": _sb(160), "fo": _sb(54, "uint16"), "ki": _sb(64, "int32"), "x5": _sb(64), "x5t": _sb(64),
-    "q0": _sb(A2, X4), "s0": _sb(A2, "uint8"), "wq": _sb(768, X4), "ws": _sb(768, "uint8"),
+    "q0": _sb(A1, X4), "s0": _sb(A1, "uint8"), "wq": _sb(768, X4), "ws": _sb(768, "uint8"),
     "stq": _sb(V, X4), "sts": _sb(V, "uint8"), "p1q": _sb(256, X4), "p1s": _sb(256, "uint8"),
-    "q1": _sb(QW, X4), "s1": _sb(QW, "uint8"), "p2q": _sb(512, X4), "p2s": _sb(512, "uint8"),
+    "q1": _sb(A2, X4), "s1": _sb(A2, "uint8"), "p2q": _sb(512, X4), "p2s": _sb(512, "uint8"),
     "q2": _sb(QW, X4), "s2": _sb(QW, "uint8"), "fq": _sb(3 * M, X4), "fs": _sb(3 * M, "uint8"),
     "yo0": _sb(M), "yo1": _sb(M), "ps": ("psum", [128, 1024], "float32"),
 }
-SEMAPHORES = ["cv", "cs_", "ct", "cg", "dst", "ds2", "dbt", "dnx", "dnw", "dn0", "dnl", "dx", "dw0", "dw1", "dc1", "dm1", "dm2",
-              "dq1", "dq2", "dy0", "dy1", "did", "sent", "sent1", "sent2", "al1", "aq1", "as1", "al2", "aq2", "as2", "aq3", "as3"]
+SEMAPHORES = ["cv", "cs_", "ct", "cg", "dst", "ds2", "dbt", "dnx", "dnw", "dn0", "dnl", "dx", "dw0", "dw1", "dc1", "dq1", "dq2",
+              "dy0", "dy1", "did", "sent", "sent1", "sent2", "al1", "aq1", "as1", "al2", "aq2", "as2", "aq3", "as3"]
 
 
 def _parts(core, others, topo):
@@ -124,6 +125,9 @@ def rank_program(g, core, T, topo):
     def act(r_, w_, out, in_, fn=F.Copy, **k):
         op("s", r_, w_, lambda e: e.activation(out, in_, fn, **k))
 
+    def affine(r_, w_, out, in_, scale=1.0, bias=0.0):
+        act(r_, w_, out, in_, F.Identity, scale=scale, bias=bias)
+
     def ts(r_, w_, out, in0, s1, o0, s2=None, o1=None):
         if o1 is None:
             op("v", r_, w_, lambda e: e.tensor_scalar(out, in0, s1, None, o0))
@@ -151,6 +155,13 @@ def rank_program(g, core, T, topo):
     def quant(r_, w_, q, s, in_):
         op("v", r_, w_, lambda e: e.quantize_mx(q, s, in_))
 
+    def quant_x(w_, q, s, k):
+        h = A1 // 4
+        quant("xt xz", w_, q[:, h * k:h * k + h], s[:, h * k:h * k + h], T.xt[:, 4 * h * k:4 * h * k + 4 * h])
+
+    def quant_w(k):
+        quant("wt%d" % (k // 3), "wq%d" % k, T.wq[:, 128 * k:128 * k + 128], T.ws[:, 128 * k:128 * k + 128], T.wt[:, 512 * k:512 * k + 512])
+
     def pick(deps_q, deps_s, w_q, w_s, oq, os_, iq, is_, off, off_key):
         copy(deps_q + " " + off_key, w_q, oq.bitcast(dt.uint32), iq.bitcast(dt.uint32).indirect(off))
         act(deps_s + " " + off_key, w_s, os_, is_.indirect(off))
@@ -158,6 +169,11 @@ def rank_program(g, core, T, topo):
     def move(q, s, r_q, r_s, w_, dq, ds, a, sq, ss, b, n):
         dma(q, s, r_q, w_, dq[:, a:a + n].bitcast(dt.uint8), sq[:, b:b + n].bitcast(dt.uint8))
         dma(q, s, r_s, w_, ds[:, a:a + n], ss[:, b:b + n])
+
+    def landed(r_, w_, out, land, n):
+        for a, b in ((0, n * r), (n * r + n, n * N)):
+            if b > a:
+                copy(r_, w_, out[:, a:b], land[:, a:b])
 
     others = [c for c in T.cores if c != core]
     rest = lambda c: [b for b in T.cores if b != c]
@@ -192,8 +208,7 @@ def rank_program(g, core, T, topo):
     for k in range(2, 8):
         dma("y", "ds2", "", "stw2", T.stw[16 * k:16 * k + 16, :], T.st[:])
     dma("y", "dnx", "", "nxrow", T.nxrow[0:1, :], T.nx[:])
-    dma("y", "dx", "", "xt", T.xt[:, 4 * XB:4 * A2], T.x[:])
-    dma("y", "dw1", "", "wt1", T.wt[:, 1536:3072], T.w[:, 1536:3072])
+    dma("y", "dx", "", "xt", T.xt[:, 4 * XB:4 * A1], T.x[:])
 
     ic, ict, cf, cl, ioL, iw, iw2, ie = T.ic, T.ict, T.cf, T.cl, T.ioL, T.iw, T.iw2, T.ie
     iota("ic", ic[:, 0:32], [[1, 2], [2, 16]], 0)
@@ -223,8 +238,10 @@ def rank_program(g, core, T, topo):
     fill("x5", T.x5[0:32, :], 0.0)
     f = lambda j: cf[:, j:j + 1]
     q15, odd = ict[:, 96:97], ict[:, 128:129]
-    for k in range(1, 6):
-        act("ioL0", "ioL", ioL[:, 256 * k:256 * k + 256], ioL[:, 0:256], F.Identity, bias=256.0 * k)
+    for k in range(4):
+        affine("ioL0", "nxl", T.nxl[:, 8 + 512 * (k // 2) + k % 2:520 + 512 * (k // 2):2], ioL[:, 0:256], bias=XB + 256.0 * (k // 2))
+    for k in range(1, 4):
+        affine("ioL0", "ioL", ioL[:, 256 * k:256 * k + 256], ioL[:, 0:256], bias=256.0 * k)
 
     o1 = T.o1
     ts("btw", "b0", o1[0:32, 0:12], T.btw[0:32, :], 1, A.bitwise_and)
@@ -254,25 +271,19 @@ def rank_program(g, core, T, topo):
         if k == 1:
             copy("jf m1z", "m1", T.m1[32 * (r // 2):32 * (r // 2) + 32, :], T.jf[0:32, :])
     spread("m1", "al1", "land1", T.m1[:], T.land1[:, 6 * r:6 * r + 6], "sent1")
-    act("iw2", "m1c", f(8), iw2[:, 1:2], F.Identity, scale=XB - 4 - BIG, bias=BIG)
-    for k in range(2):
-        act("ioL0 ioL iw2 m1c", "nxl", T.nxl[:, k:1040:2], ioL[:, 0:520], F.Identity, bias=f(8), scale=iw2[:, 1:2])
-    dma("s", "dm1", "m1", "land1o", T.land1[:, 6 * r:6 * r + 6], T.m1[:])
+    affine("iw2", "b0c", f(8), iw2[:, 0:1], scale=BIG)
+    act("ict", "aq", f(9), q15, F.Abs, bias=-4.5)
+    affine("ioL0 ioL iw2", "wa", T.wa[:], ioL[:, A1:A2], scale=iw2[:, 2:3])
+    for a in (0, 1032):
+        affine("ioL0 b0c", "nxe", T.nxl[:, a:a + 8], ioL[:, 0:8], scale=0.0, bias=f(8))
     dma("y", "dn0", "nxt", "nxl0 nxl", T.nxl[0:1, 8:1032], T.nxt[0:64, 0:16])
-    dma("y", "dw0", "", "wt0", T.wt[:, 0:1536], T.w[:, 0:1536])
     for k in range(1, 8):
         dma("y", "dnl", "nxl0", "nxl1", T.nxl[16 * k:16 * k + 1, 8:1032], T.nxl[0:1, 8:1032])
-    iota("ic3", ic[:, 256:272], [[32, 2], [320, 2], [1, 4]], 0)
-    iota("ic3", ic[:, 272:288], [[32, 2], [-288, 2], [1, 4]], 288)
-    iota("ic3", ic[:, 288:320], [[256, 2], [1, 16]], 257, 16)
+    iota("ic3", ic[:, 256:272], [[32, 2], [320, 2], [1, 4]], 1)
+    iota("ic3", ic[:, 272:288], [[32, 2], [-288, 2], [1, 4]], 289)
+    iota("ic3", ic[:, 288:320], [[256, 2], [1, 16]], 257 + LIFT, 16)
 
-    def quant_x(w_, q, s, k):
-        h = A2 // 4
-        quant("xt xz", w_, q[:, h * k:h * k + h], s[:, h * k:h * k + h], T.xt[:, 4 * h * k:4 * h * k + 4 * h])
-
-    def quant_w(k):
-        quant("wt%d" % (k // 3), "wq%d" % k, T.wq[:, 128 * k:128 * k + 128], T.ws[:, 128 * k:128 * k + 128], T.wt[:, 512 * k:512 * k + 512])
-
+    copy("m1", "zfo", T.zf[:, 6 * r:6 * r + 6], T.m1[:])
     ts("stw stw2", "stu", T.stu[:], T.stw[:], float(XB), A.add)
     tt("di diz rlu cdest", "f1", T.f1[:], T.di[:].indirect(cl[:, 2:14]), T.cdest[:], A.is_equal)
     quant_x("q0 s0", T.q0, T.s0, 0)
@@ -295,92 +306,99 @@ def rank_program(g, core, T, topo):
         dma("y" if k % 2 else "s", "dc1", "x1t", "w1", T.w1[16 * k:16 * k + 16, :], T.x1t[0:128:32, :])
     pick("q0", "s0", "stq", "sts", T.stq[:], T.sts[:], T.q0[:], T.s0[:], T.stu[:], "stu")
     move("y", "dq1", "stq", "sts", "q1s", T.q1, T.s1, SB, T.stq, T.sts, 0, V)
-    act("ioL m9", "ci", T.ci[:], ioL[:, SB:SB + V], F.Identity, scale=f(4))
-    act("iw2", "nb", f(5), iw2[:, r + 1:r + 2], F.Identity, scale=-BIG, bias=BIG)
-    act("ioL0 ioL", "tab2", T.tab2[:], ioL[:, 0:RB + 272], F.Identity, scale=0.0)
+    for k in (1, 0):
+        dma("y", "dw%d" % k, "", "wt%d" % k, T.wt[:, 1536 * k:1536 * k + 1536], T.w[:, 1536 * k:1536 * k + 1536])
+    affine("ioL m9", "ci", T.ci[:], ioL[:, SB:SB + V], scale=f(4))
+    affine("iw2", "nb", f(5), iw2[:, r + 1:r + 2], scale=-BIG, bias=BIG)
+    affine("ioL0 ioL", "tab2", T.tab2[:], ioL[:, 0:RB + 272], scale=0.0)
     ts("ioL0 q31 ict2", "pxc", T.px[:, 64:96], ioL[:, 0:32], f(3), A.is_equal, ict[:, 160:161], A.mult)
+    ts("aq", "valid", f(6), f(9), 4.0, A.is_lt)
+    ts("aq even", "valid", f(7), f(9), 4.0, A.is_lt, f(2), A.mult)
     ts("ioL0 ict2", "la", cl[:, 16:18], ioL[:, 0:129:128], ict[:, 192:193], A.add)
-    quant("xt", "q1x", T.q1[:, XB:A2], T.s1[:, XB:A2], T.xt[:, 4 * XB:4 * A2])
-    turn("ic3", "ict3", ict[:, 256:320], ic[:, 256:320])
     for k in range(4):
-        quant_x("q2x", T.q2, T.s2, k)
+        quant_x("q1x", T.q1, T.s1, k)
+
+    m2, tot, px, mi, kk, vt = T.m2, T.tot, T.px, T.mi, T.kk, T.vt
+    cba, bc, pa, c0m, cbb = (kk[:, 12 * k:12 * k + 12] for k in range(5))
+    landed("land1", "zf", T.zf, T.land1, 6)
+    quant_x("q2x", T.q2, T.s2, 0)
+    ts("zf zfo dg", "off2", T.off2[:], T.zf[:].indirect(cl[:, 14:15]), 8.0 - 1024 * r, A.add, 1032.0, A.min)
+    ts("zf zfo dg", "mi", mi[:], T.zf[:].indirect(cl[:, 14:15]), 1.0 / 1024, A.mult, -0.4995, A.add)
+    copy("nxl nxl1 nxe off2", "n2r", T.n2r[:], T.nxl[:].indirect(T.off2[:, 0:12]))
+    quant_x("q2x", T.q2, T.s2, 1)
+    turn("n2r", "n2t", T.n2t[:], T.n2r[:])
+    quant_x("q2x", T.q2, T.s2, 2)
+    ts("n2t", "xo", T.xo[:], T.n2t[:, 0:V:16], 1.0 / TN, A.mult, 0.501, A.add)
     ts("w1", "s1off", T.s1off[:], T.w1[:], V - 1.0, A.min)
-    ts("ioL0 ioL ict3", "le", cl[:, 18:23], ioL[:, 0:257:64], ict[:, 256:257], A.add, 590.0, A.min)
+    ts("n2t", "m2a", m2[:, 0:12], T.n2t[:, 0:V:16], -1.0, A.mult, float(N * TN), A.add)
+    act("iw xo", "tot fl", T.fl[:], iw[:, 0:32].indirect(T.xo[:]), F.Identity, accum_out=tot[:, 0:1])
+    affine("fl nb", "fb", T.fb[:], T.fl[:], scale=f(5))
     pick("stq", "sts", "p1q", "p1s", T.p1q[:], T.p1s[:], T.stq[:], T.sts[:], T.s1off[:], "s1off")
     at1 = A1 + CAP * r
     send("p1q", "aq1", "q1a", lambda d: T.p1q[:, CAP * d:CAP * d + CAP].bitcast(dt.uint8), T.q1[:, at1:at1 + CAP].bitcast(dt.uint8), "sent1")
     send("p1s", "as1", "s1a", lambda d: T.p1s[:, CAP * d:CAP * d + CAP], T.s1[:, at1:at1 + CAP], "sent1")
-
-    m2, tot, px, mi, kk, vt = T.m2, T.tot, T.px, T.mi, T.kk, T.vt
-    cba, c1m, bc, d1, d0, pa, c0m, cbb = (kk[:, 12 * k:12 * k + 12] for k in range(8))
-    copy("land1 land1o", "zf", T.zf[:], T.land1[:])
-    quant_w(5)
-    ts("zf dg", "off2", T.off2[:], T.zf[:].indirect(cl[:, 14:15]), 8.0 - 1024 * r, A.add, 1032.0, A.min)
-    ts("zf dg", "mi", mi[:, 0:16], T.zf[:].indirect(cl[:, 14:15]), 1.0 / 1024, A.mult, -0.4995, A.add)
-    copy("nxl nxl1 off2", "n2r", T.n2r[:], T.nxl[:].indirect(T.off2[:, 0:12]))
-    quant_w(4)
-    turn("n2r", "n2t", T.n2t[:], T.n2r[:])
-    quant_w(3)
-    ts("n2t", "xo", T.xo[:], T.n2t[:, 0:V:16], 1.0 / TN, A.mult, 0.501, A.add)
-    ts("n2t", "m2a", m2[:, 0:12], T.n2t[:, 0:V:16], -1.0, A.mult, float(N * TN), A.add)
-    ts("mi", "cba", cba, mi[:, 0:12], 64.0, A.mult, float(A2 + 32 - RB - CAP * r), A.add)
-    act("iw2 xo", "tot junk", T.junk[:], iw2[:].indirect(T.xo[:]), F.Identity, accum_out=tot[:, 0:1])
-    copy("iw xo", "fl", T.fl[:], iw[:, 0:32].indirect(T.xo[:]))
-    act("fl nb", "fb", T.fb[:], T.fl[:], F.Identity, scale=f(5))
-    act("ioL0 ioL", "tab3", T.tab3[:], ioL[:, 0:RB + M + 16], F.Identity, scale=0.0)
-    act("ioL0", "x3z", T.x3[:], ioL[:, 0:V], F.Identity, scale=0.0, bias=BIG)
-    quant_w(2)
+    affine("ioL0 ioL", "tab3", T.tab3[:], ioL[:, 0:RB + M + 16], scale=0.0)
+    affine("ioL0", "x3z", T.x3[:], ioL[:, 0:V], scale=0.0)
     copy("tot", "u1", tot[32:64, 1:2], tot[0:32, 0:1])
     ts("tot", "u2", tot[64:96, 1:2], tot[0:32, 0:1], tot[32:64, 0:1], A.add)
     ts("tot", "u3", tot[96:128, 1:2], tot[0:32, 0:1], tot[32:64, 0:1], A.add, tot[64:96, 0:1], A.add)
-    ts("iw2 tot even", "pxb", px[:, 48:64], iw2[:, 0:16], tot[:, 0:1], A.mult, f(2), A.mult)
-    ts("off2", "c1i", mi[:, 16:28], T.off2[:, 0:12], 0.5, A.mult, XB + 32 - 4.25, A.add)
-    ts("mk tot0 u1 u2 u3", "pxa", px[:, 0:32], T.mk[:], tot[:, 1:2], A.mult)
+    ts("iw2 tot valid", "pxb", px[:, 48:64], iw2[:, 0:16], tot[:, 0:1], A.mult, f(7), A.mult)
+    ts("mk tot0 u1 u2 u3 valid", "pxa", px[:, 0:32], T.mk[:], tot[:, 1:2], A.mult, f(6), A.mult)
     turn("fb", "fbt", T.fbt[:], T.fb[:])
     turn("pxa pxb pxc", "pxt", T.pxt[:], px[:])
-    quant_w(1)
+    quant_x("q2x", T.q2, T.s2, 3)
     summed("pxt", "init", T.init[:], T.pxt[:])
-    quant_w(0)
+    turn("ic3", "ict3", ict[:, 256:320], ic[:, 256:320])
+    ts("mi", "cba", cba, mi[:, 0:12], 64.0, A.mult, float(32 - RB - CAP * r), A.add)
     scan("fl ci init", "cnt", T.cnt[:], T.fl[:], T.ci[:], T.init[:], A.add, A.max)
     copy("init", "m2c", m2[:, 24:25], T.init[:])
+    ts("ioL0 ioL ict3", "le", cl[:, 18:23], ioL[:, 0:257:64], ict[:, 256:257], A.add, 590.0, A.min)
     turn("cnt", "vt", vt[:], T.cnt[:])
-    copy("vt", "c0u", T.c0u[:], vt[:, 9:V:16])
+    quant_w(5)
+    ts("vt", "c0u", T.c0u[:], vt[:, 9:V:16], -float(A1), A.add)
     scan("fbt vt", "seg", T.seg[:], T.fbt[:], vt[:], 0.0, A.max, A.min)
-    tt("ioL0 ioL c0u n2r", "vals", T.vals[:], ioL[:].indirect(T.c0u[:]), T.n2r[:], A.min)
+    tt("wa c0u n2r", "vals", T.vals[:], T.wa[:].indirect(T.c0u[:]), T.n2r[:], A.max)
     copy("seg", "m2b", m2[:, 12:24], T.seg[:, 8:V:16])
     spread("m2a m2b m2c", "al2", "land2", m2[:, 0:ML], T.land2[:, ML * r:ML * r + ML], "sent2")
-    dma("s", "dm2", "m2a m2b m2c", "land2o", T.land2[:, ML * r:ML * r + ML], m2[:, 0:ML])
-    for a, b in ((A1, at1), (at1 + CAP, QW)):
+    for a, b in ((A1, at1), (at1 + CAP, A2)):
         if b > a:
             move("y", "dq2", "q1a q1s sent2", "s1a q1s", "q2o", T.q2, T.s2, a, T.q1, T.s1, a, b - a)
     tt("vt fbt", "c0m", c0m, vt[:, 9:V:16], T.fbt[:, 9:V:16], A.min)
     op("v", "vals m2b tab2", "tab2s", lambda e: e.tensor_copy(T.tab2[:].indirect(m2[:, 12:24]), T.vals[:]))
 
-    def collect(tag, tab, y, n, lst, gg, rr, w):
+    def collect(tag, tab, y, n, lst, gg, rr, w, between):
         turn("tab%ss" % tag, "ya" + tag, y[:, 0:n], tab[:, RB:RB + n])
         turn("tab%ss" % tag, "yb" + tag, y[:, n:2 * n + 32], tab[:, RB - 16:RB + n + 16])
         ys = "ya%s yb%s l%s" % (tag, tag, "a" if tag == "2" else "e")
+        between(0)
         copy(ys, "ga" + tag, gg[:, 0:w], y[:, 0:2 * n + 16].indirect(lst))
+        between(1)
         tt(ys + " ga" + tag, "gb" + tag, gg[:, w:2 * w], y[:, 16:2 * n + 32].indirect(lst), gg[:, 0:w], A.add)
+        between(2)
         tt("gb" + tag, "ra" + tag, rr[0:64, 0:w], gg[0:64, w:2 * w], gg[64:128, w:2 * w], A.add)
         tt("ra" + tag, "rb" + tag, rr[0:32, w:2 * w], rr[0:32, 0:w], rr[32:64, 0:w], A.add)
 
     low, lift = 2.0 ** 30, N * (RB - 1 + CAP * r) - (RB - 1)
-    act("iw2", "al", f(11), iw2[:, 10:11], F.Identity, scale=-low)
-    act("iw2", "al", f(12), iw2[:, 10:11], F.Identity, scale=low + BIG, bias=1.0)
-    act("ict", "db", f(15), odd, F.Identity, scale=16.0, bias=1.0 + lift)
+    affine("iw2", "al", f(11), iw2[:, 10:11], scale=-low)
+    affine("iw2", "al", f(12), iw2[:, 10:11], scale=low + BIG, bias=1.0)
+    affine("ict", "db", f(15), odd, scale=16.0, bias=1.0 + lift)
     act("ioL0", "oh", ie[:, 16:32], ioL[:, 0:16], F.Abs, bias=-float(r))
-    act("ict3", "k8", f(13), ict[:, 288:289], F.Identity, scale=0.125)
-    act("iw2", "b3", f(14), iw2[:, 1:2], F.Identity, scale=-BIG, bias=BIG)
+    act("ict", "w12", f(13), q15, F.Abs, bias=-1.5)
     act("oh", "oh2", ie[:, 32:48], ie[:, 16:32], F.Relu, scale=-1.0, bias=1.0)
-    act("ioL0 k8 x3z", "x3", T.x3[:, 3:V:16], ioL[:, 0:V:16], F.Identity, scale=0.125, bias=f(13))
-    act("ioL0 db", "de", T.de[:], ioL[:, 0:V], F.Identity, bias=f(15))
-    act("oh2 al", "ie", ie[:, 0:16], ie[:, 32:48], F.Identity, scale=f(12), bias=f(11))
+    act("w12", "w12s", f(14), f(13), F.Relu, scale=-2.0, bias=2.0)
+    affine("ioL0 ict3 x3z", "x3", T.x3[:, 4:V:16], ioL[:, 0:V:16], bias=ict[:, 288:289])
+    affine("iw2", "w12a", f(10), iw2[:, 1:2], scale=-32.0, bias=float(A2))
+    affine("ioL0 db", "de", T.de[:], ioL[:, 0:V], bias=f(15))
+    affine("w12s w12a", "w12b", f(13), f(14), scale=f(10))
+    affine("oh2 al", "ie", ie[:, 0:16], ie[:, 32:48], scale=f(12), bias=f(11))
+    affine("ioL0", "wb", T.wb[:, 0:8], ioL[:, 0:8], scale=0.0)
+    affine("ioL0 ioL w12s w12b", "wb", T.wb[:, 8:768], ioL[:, 8:768], scale=f(14), bias=f(13))
+    copy("m2a m2b m2c", "z2o", T.z2[:, ML * r:ML * r + ML], m2[:, 0:ML])
     tt("cba c0m", "cbb", cbb, cba, c0m, A.subtract)
-    tt("c1i c0m", "c1m", c1m, mi[:, 16:28], c0m, A.min)
-    collect("2", T.tab2, T.y2, 256, cl[:, 16:18], T.g2, T.r2, 32)
+    collect("2", T.tab2, T.y2, 256, cl[:, 16:18], T.g2, T.r2, 32, lambda k: quant_w(4 - k))
     for k in range(4):
         ts("rb2", "p2off", T.p2off[32 * k:32 * k + 32, :], T.r2[0:32, 32:64], float(XB), A.max)
+    quant_w(1)
     at2 = A2 + 2 * CAP * r
 
     def leave(k):
@@ -396,35 +414,32 @@ def rank_program(g, core, T, topo):
     leave(0)
 
     z2, zz = T.z2, T.zz
-    copy("land2 land2o", "z2", z2[:], T.land2[:])
+    landed("land2", "z2", z2, T.land2, ML)
     leave(1)
-    tt("z2", "za", zz[:, 0:100], z2[:, 0:100], z2[:, 100:200], A.max)
-    summed("z2", "bsum", T.bsum[:], z2[:, 24:200:ML])
+    tt("z2 z2o", "za", zz[:, 0:100], z2[:, 0:100], z2[:, 100:200], A.max)
+    summed("z2 z2o", "bsum", T.bsum[:], z2[:, 24:200:ML])
     tt("za", "zb", zz[:, 100:150], zz[:, 0:50], zz[:, 50:100], A.max)
+    quant_w(0)
     tt("zb", "zc", zz[:, 150:175], zz[:, 100:125], zz[:, 125:150], A.max)
     an, bn = zz[:, 150:162], zz[:, 162:174]
     ts("zc", "xe", T.xe[:], an, -1.0 / TN, A.mult, N - 0.499, A.add)
     act("ie xe", "fe", T.fe[:], ie[:, 0:16].indirect(T.xe[:]))
     tt("zc cbb", "bc", bc, bn, cbb, A.add)
-    ts("zc x3z", "x3", T.x3[:, 2:V:16], an, -1.0, A.mult, float(XB + TN * (N - r)), A.add)
-    tt("bc c1m", "d1", d1, bc, c1m, A.max)
-    tt("bc c0m", "d0", d0, bc, c0m, A.max)
+    ts("zc x3z", "x3", T.x3[:, 3:V:16], an, -1.0, A.mult, float(LIFT + XB + TN * (N - r)), A.add)
+    copy("bc", "bcu", T.bcu[:], bc)
     turn("x3", "x3t", T.x3t[:], T.x3[:])
-    ts("d1", "d1u", T.d1u[:], d1, -32.0, A.add)
-    act("ioL0 ioL d1u b3", "t3", T.t3[:], ioL[:].indirect(T.d1u[:]), F.Identity, scale=iw2[:, 1:2], bias=f(14))
-    copy("d0", "d0u", T.d0u[:], d0)
     scan("fe de bsum", "pe", T.pe[:], T.fe[:], T.de[:], T.bsum[:], A.add, A.max)
-    tt("ioL0 ioL d0u x3t", "v3", T.v3[:], ioL[:].indirect(T.d0u[:]), T.x3t[:], A.min)
+    tt("wb bcu vals", "v3", T.v3[:], T.wb[:].indirect(T.bcu[:]), T.vals[:], A.max)
     turn("pe", "pt", T.pt[:], T.pe[:])
-    tt("v3 t3", "v4", T.v4[:], T.v3[:], T.t3[:], A.min)
+    tt("v3 x3t", "v4", T.v4[:], T.v3[:], T.x3t[:], A.max)
     tt("pt", "pa", pa, T.pt[:, r + 1:V:16], T.pt[:, 10:V:16], A.min)
     ts("pa", "po", T.po[:], pa, -float(lift), A.add)
     op("v", "v4 po tab3", "tab3s", lambda e: e.tensor_copy(T.tab3[:].indirect(T.po[:]), T.v4[:]))
-    collect("3", T.tab3, T.y3, M, cl[:, 18:23], T.g3, T.r3, 80)
+    collect("3", T.tab3, T.y3, M, cl[:, 18:23], T.g3, T.r3, 80, lambda k: None)
     for k in range(3):
-        copy("rb3", "fo0", T.fo[0:32, 18 * k:18 * k + 18], T.r3[0:32, 80 + k:152:4])
+        ts("rb3", "fo0", T.fo[0:32, 18 * k:18 * k + 18], T.r3[0:32, (81, 80, 82)[k]:152:4], -float(LIFT * (k == 2)), A.add)
     ki = T.ki
-    ts("rb3", "k0", ki[0:32, 0:18], T.r3[0:32, 83:152:4], 8.0, A.mult)
+    ts("rb3", "k0", ki[0:32, 0:18], T.r3[0:32, 83:152:4], -float(LIFT), A.add, 0.0, A.max)
     for k in range(1, 4):
         copy("fo0", "fo", T.fo[32 * k:32 * k + 32, :], T.fo[0:32, :])
     ts("k0", "k1", ki[0:32, 18:36], ki[0:32, 0:18], 8, A.arith_shift_right)

@@ -1,12 +1,13 @@
 from concourse.bass import DstId, RemoteDMATransfer
-from concourse.mybir import dt, AluOpType as A, AxisListType, ActivationFunctionType as F
+from concourse.mybir import dt, AluOpType as A, ActivationFunctionType as F
 
 N = 8
 TN, V, M, CAP = 512, 192, 288, 32
-XB, A1, SB, A2, QW = 16, 528, 784, 976, 1488
+XB, A1, A2, QW = 16, 528, 752, 1264
 RB = 224
-ML = 25
+ML = 13
 BIG = 8192.0
+LOW = 2.0 ** 30
 LIFT = 2048
 X4 = "float8_e4m3fn_x4"
 
@@ -16,30 +17,30 @@ def _sb(n, d="float32"):
 
 
 SCRATCH = {
-    "stw": _sb(12, "int32"), "btw": _sb(12, "int32"), "nxrow": _sb(1024, "int32"), "nxw": _sb(32, "int32"), "nxf": _sb(32),
-    "nxt": _sb(32), "nxl": _sb(1040), "xt": _sb(4 * A1, "bfloat16"), "wt": _sb(3072, "bfloat16"),
-    "ic": _sb(320), "ict": _sb(320), "cf": _sb(16), "ioL": _sb(1024), "wa": _sb(A2 - A1), "wb": _sb(768), "cl": _sb(32, "uint16"),
-    "rl": _sb(12), "cdest": _sb(V), "ci": _sb(V), "iw": _sb(64), "iw2": _sb(32), "ie": _sb(48), "mk": _sb(32),
-    "o1": _sb(64, "int32"), "off1": _sb(12, "uint16"), "stu": _sb(12, "uint16"), "b1s": _sb(16),
-    "n1r": _sb(V), "n1t": _sb(V), "jf": _sb(6), "m1": _sb(6, "uint16"), "land1": _sb(48, "uint16"), "di": _sb(8, "int32"),
-    "f1": _sb(V, "bfloat16"), "f1t": _sb(V, "bfloat16"), "c1L": _sb(V, "bfloat16"), "sg": _sb(2 * V, "bfloat16"), "cnt1": _sb(2),
+    "stw": _sb(12, "int32"), "btw": _sb(12, "int32"), "sb6": _sb(8, "int32"), "nxrow": _sb(512, "int32"), "nxw": _sb(32, "int32"),
+    "nxf": _sb(32), "nxt": _sb(32), "nxl": _sb(1040), "xt": _sb(4 * A1, "bfloat16"), "wt": _sb(3072, "bfloat16"),
+    "ic": _sb(320), "ict": _sb(320), "cf": _sb(24), "ioL": _sb(1024), "wa": _sb(A2), "wb": _sb(768), "cl": _sb(32, "uint16"),
+    "rl": _sb(12), "cdest": _sb(V), "ci": _sb(64 + V), "iw": _sb(96), "iw2": _sb(32), "ie": _sb(48), "mk": _sb(32),
+    "o1": _sb(24, "int32"), "off1": _sb(6, "uint16"), "stu": _sb(14, "uint16"), "b1s": _sb(64),
+    "n1r": _sb(96), "n1t": _sb(96), "jf": _sb(18), "m1": _sb(6, "uint16"), "land1": _sb(48, "uint16"), "di": _sb(8, "int32"),
+    "f1": _sb(V, "bfloat16"), "f1t": _sb(V, "bfloat16"), "c1L": _sb(V, "bfloat16"), "sg": _sb(2 * V, "bfloat16"),
     "x1": _sb(64), "x1t": _sb(64), "w1": _sb(16), "s1off": _sb(16, "uint16"),
     "zf": _sb(48), "off2": _sb(16, "uint16"), "n2r": _sb(V), "n2t": _sb(V), "xo": _sb(12, "uint16"),
-    "fl": _sb(V), "tot": _sb(2), "px": _sb(96), "pxt": _sb(96), "init": _sb(1), "cnt": _sb(V), "fb": _sb(V, "bfloat16"),
-    "fbt": _sb(V, "bfloat16"), "vt": _sb(V), "seg": _sb(V), "c0u": _sb(12, "uint16"), "vals": _sb(V), "m2": _sb(26, "uint16"),
-    "land2": _sb(N * ML, "uint16"), "tab2": _sb(RB + 272), "y2": _sb(544), "g2": _sb(64), "r2": _sb(64), "p2off": _sb(32, "uint16"),
-    "mi": _sb(16, "int32"), "kk": _sb(64), "z2": _sb(N * ML), "zz": _sb(176), "bsum": _sb(1), "xe": _sb(12, "uint16"),
+    "fl": _sb(64 + V), "tot": _sb(2), "px": _sb(64), "cnt": _sb(64 + V), "fb": _sb(V, "bfloat16"), "fbt": _sb(V, "bfloat16"),
+    "vt": _sb(V), "seg": _sb(V), "c0u": _sb(12, "uint16"), "vals": _sb(V), "m2": _sb(16), "so": _sb(12, "uint16"), "ab": _sb(24),
+    "land2": _sb((N - 1) * ML), "tab2": _sb(RB + 272), "y2": _sb(544), "g2": _sb(64), "r2": _sb(64), "p2off": _sb(32, "uint16"),
+    "mi": _sb(16, "int32"), "kk": _sb(48), "zz": _sb(96), "zi": _sb(24, "int32"), "xe": _sb(12, "uint16"),
     "fe": _sb(V), "de": _sb(V), "pe": _sb(V), "pt": _sb(V), "po": _sb(12, "uint16"), "bcu": _sb(12, "uint16"),
-    "x3": _sb(V), "x3t": _sb(V), "v3": _sb(V), "v4": _sb(V), "tab3": _sb(RB + M + 16),
+    "x3": _sb(V), "x3t": _sb(V), "v4": _sb(V), "tab3": _sb(RB + M + 16),
     "y3": _sb(608), "g3": _sb(160), "r3": _sb(160), "fo": _sb(54, "uint16"), "ki": _sb(64, "int32"), "x5": _sb(64), "x5t": _sb(64),
     "q0": _sb(A1, X4), "s0": _sb(A1, "uint8"), "wq": _sb(768, X4), "ws": _sb(768, "uint8"),
-    "stq": _sb(V, X4), "sts": _sb(V, "uint8"), "p1q": _sb(256, X4), "p1s": _sb(256, "uint8"),
+    "stq": _sb(V + 16, X4), "sts": _sb(V + 16, "uint8"), "p1q": _sb(256, X4), "p1s": _sb(256, "uint8"),
     "q1": _sb(A2, X4), "s1": _sb(A2, "uint8"), "p2q": _sb(512, X4), "p2s": _sb(512, "uint8"),
     "q2": _sb(QW, X4), "s2": _sb(QW, "uint8"), "fq": _sb(3 * M, X4), "fs": _sb(3 * M, "uint8"),
-    "yo0": _sb(M), "yo1": _sb(M), "ps": ("psum", [128, 1024], "float32"),
+    "hq": _sb(2 * CAP, X4), "hs": _sb(2 * CAP, "uint8"), "yo0": _sb(M), "yo1": _sb(M), "ps": ("psum", [128, 2048], "float32"),
 }
-SEMAPHORES = ["cv", "cs_", "ct", "cg", "dst", "ds2", "dbt", "dnx", "dnw", "dn0", "dnl", "dx", "dw0", "dw1", "dc1", "dq1", "dq2",
-              "dy0", "dy1", "did", "sent", "sent1", "sent2", "al1", "aq1", "as1", "al2", "aq2", "as2", "aq3", "as3"]
+SEMAPHORES = ["cv", "cs_", "ct", "cg", "dst", "ds2", "dbt", "dnx", "dnw", "dnl", "dx", "dw0", "dw1", "dc1", "dq1", "dq2", "dy0", "dy1",
+              "dy2", "dy3", "did", "sent", "sent2", "al1", "al2", "aq0", "as0", "aq1", "as1", "aq2", "as2", "aq3", "as3", "ahq", "ahs"]
 
 
 def _parts(core, others, topo):
@@ -70,10 +71,33 @@ def _mask(engines):
     return sum(1 << e for e in engines)
 
 
+def _helpers(T, topo):
+    out = {}
+    for c in T.cores:
+        own = [b for b in T.cores if b in topo.cores_of(c)]
+        free = [b for b in topo.cores_of(c) if b not in T.cores and topo.die(b) != topo.die(c)]
+        far = [b for b in T.cores if b not in own]
+        out[c] = (free[own.index(c)], far[own.index(c)])
+    return out
+
+
+def hand_on(g, core, T, topo):
+    for c, (h, d) in _helpers(T, topo).items():
+        if h == core:
+            n_in = len(_parts(c, [b for b in T.cores if b != c], topo)[1][1])
+            at = A2 + 2 * CAP * T.rank_of(c)
+            rid, pid = topo.addr(d)[:2]
+            for s_in, s_out, src, dst in (("ahq", "aq2", T.hq[:].bitcast(dt.uint8), T.q2[:, at:at + 2 * CAP].bitcast(dt.uint8)),
+                                          ("ahs", "as2", T.hs[:], T.s2[:, at:at + 2 * CAP])):
+                g.wait_ge(T.sem[s_in], n_in)
+                g.remote_dma(dst, src, T.sem[s_out], T.sem.sent, pid, rid, topo.mask(core, d))
+            g.wait_ge(T.sem.sent, 2 * len(topo.engines(core, d)))
+
+
 def rank_program(g, core, T, topo):
     r = T.rank_of(core)
     if r is None:
-        return
+        return hand_on(g, core, T, topo)
     sem = T.sem
     queues = {"v": (g.vector, "cv"), "s": (g.scalar, "cs_"), "t": (g.tensor, "ct"), "g": (g, "cg"), "y": (g.sync, None)}
     total, seen = {}, {q: {} for q in queues}
@@ -149,15 +173,12 @@ def rank_program(g, core, T, topo):
     def scan(r_, w_, out, a, b, init, o0, o1):
         op("v", r_, w_, lambda e: e.tensor_tensor_scan(out, a, b, init, o0, o1))
 
-    def summed(r_, w_, out, in_):
-        op("v", r_, w_, lambda e: e.tensor_reduce(out, in_, AxisListType.X, A.add))
-
     def quant(r_, w_, q, s, in_):
         op("v", r_, w_, lambda e: e.quantize_mx(q, s, in_))
 
-    def quant_x(w_, q, s, k):
+    def quant_x(k):
         h = A1 // 4
-        quant("xt xz", w_, q[:, h * k:h * k + h], s[:, h * k:h * k + h], T.xt[:, 4 * h * k:4 * h * k + 4 * h])
+        quant("xt xz", "q0 s0", T.q0[:, h * k:h * k + h], T.s0[:, h * k:h * k + h], T.xt[:, 4 * h * k:4 * h * k + 4 * h])
 
     def quant_w(k):
         quant("wt%d" % (k // 3), "wq%d" % k, T.wq[:, 128 * k:128 * k + 128], T.ws[:, 128 * k:128 * k + 128], T.wt[:, 512 * k:512 * k + 512])
@@ -166,58 +187,68 @@ def rank_program(g, core, T, topo):
         copy(deps_q + " " + off_key, w_q, oq.bitcast(dt.uint32), iq.bitcast(dt.uint32).indirect(off))
         act(deps_s + " " + off_key, w_s, os_, is_.indirect(off))
 
-    def move(q, s, r_q, r_s, w_, dq, ds, a, sq, ss, b, n):
-        dma(q, s, r_q, w_, dq[:, a:a + n].bitcast(dt.uint8), sq[:, b:b + n].bitcast(dt.uint8))
-        dma(q, s, r_s, w_, ds[:, a:a + n], ss[:, b:b + n])
-
-    def landed(r_, w_, out, land, n):
-        for a, b in ((0, n * r), (n * r + n, n * N)):
-            if b > a:
-                copy(r_, w_, out[:, a:b], land[:, a:b])
-
     others = [c for c in T.cores if c != core]
     rest = lambda c: [b for b in T.cores if b != c]
     place = lambda c: DstId(rid=topo.addr(c)[0], pnc=topo.addr(c)[1])
+    helpers = _helpers(T, topo)
 
-    def send(r_, s, w_, src, dst, left="sent", only=lambda a, b: True):
+    def send(r_, s, w_, src, dst, only, via=None):
         deps("g", r_.split(), [])
         engines = _split(core, others, topo)
-        g.remote_dma_fused([RemoteDMATransfer(dst_ids=[place(c)], dma_engine_mask=_mask(engines[c]), remote_sem=sem[s],
-                                              src=src(T.rank_of(c)), dst=dst) for c in others if only(core, c)], local_sem=sem[left])
-        total[left] = total.get(left, 0) + sum(len(engines[c]) for c in others if only(core, c))
-        wrote[left] = [(left, None)]
-        total[s] = sum(len(_split(c, rest(c), topo)[core]) for c in others if only(c, core))
+        ways = [(c, engines[c], s, dst(T.rank_of(c)), c) for c in others if only(core, c)]
+        if via:
+            h, d = helpers[core]
+            ways = [w for w in ways if w[0] != d] + [(h, _parts(core, others, topo)[1][1], via[0], via[1], d)]
+        g.remote_dma_fused([RemoteDMATransfer(dst_ids=[place(c)], dma_engine_mask=_mask(e), remote_sem=sem[a], src=src(T.rank_of(d)),
+                                              dst=to) for c, e, a, to, d in ways], local_sem=sem.sent)
+        total["sent"] = total.get("sent", 0) + sum(len(w[1]) for w in ways)
+        total[s] = sum(len(topo.engines(helpers[c][0], core)) if via and helpers[c][1] == core else len(_split(c, rest(c), topo)[core])
+                       for c in others if only(c, core))
         wrote.setdefault(w_, []).append((s, total[s]))
 
     def spread(r_, s, w_, src, dst, left):
         deps("g", r_.split(), [])
         parts = _parts(core, others, topo)
         g.remote_dma_fused([RemoteDMATransfer(dst_ids=[place(c) for c in part], dma_engine_mask=_mask(free), remote_sem=sem[s],
-                                              srcs=[src], dsts=[dst] * len(part)) for part, free in parts], local_sem=sem[left])
+                                              srcs=[src], dsts=[dst(T.rank_of(c)) for c in part]) for part, free in parts],
+                           local_sem=sem[left])
         total[left] = total.get(left, 0) + sum(len(free) for part, free in parts)
         wrote[left] = [(left, None)]
         total[s] = sum(len(free) for c in others for part, free in _parts(c, rest(c), topo) if core in part)
         wrote.setdefault(w_, []).append((s, total[s]))
 
+    def leave(tag, k, n, rq, rs, pq, pz, q, s, off, dq, ds, at):
+        part = _parts(core, others, topo)[k][0]
+        a, b = min(T.rank_of(c) for c in part), max(T.rank_of(c) for c in part) + 1
+        only = lambda c, d: (d in topo.cores_of(c)) == (k == 1)
+        key = "%d%d" % (tag, k)
+        pick(rq, rs, "pq" + key, "pz" + key, pq[:, n * a:n * b], pz[:, n * a:n * b], q, s, off[:, n * a // 16:n * b // 16], "p%doff" % tag)
+        send("pq" + key, "aq%d" % (2 * tag - 2 + k), "q%da" % tag, lambda d: pq[:, n * d:n * d + n].bitcast(dt.uint8),
+             lambda d: dq[:, at(d):at(d) + n].bitcast(dt.uint8), only, key == "20" and ("ahq", T.hq[:].bitcast(dt.uint8)))
+        send("pz" + key, "as%d" % (2 * tag - 2 + k), "s%da" % tag, lambda d: pz[:, n * d:n * d + n],
+             lambda d: ds[:, at(d):at(d) + n], only, key == "20" and ("ahs", T.hs[:]))
+
     fill("nxrow", T.nxrow[:], 0)
     for k in range(2):
-        dma("s", "dst", "", "stw", T.stw[16 * k:16 * k + 16, :], T.st[:])
+        dma("s", "dst", "", "sb6", T.sb6[16 * k:16 * k + 16, 0:6], T.st[:, 6 * k:6 * k + 6])
         dma("y", "dbt", "", "btw", T.btw[16 * k:16 * k + 16, :], T.bt[:])
     for k in range(4):
         dma("s", "dnw", "", "nxw", T.nxw[16 * k:16 * k + 16, :], T.nx[:, 32 * (k // 2):32 * (k // 2) + 32])
-    for k in range(2, 8):
-        dma("y", "ds2", "", "stw2", T.stw[16 * k:16 * k + 16, :], T.st[:])
-    dma("y", "dnx", "", "nxrow", T.nxrow[0:1, :], T.nx[:])
+    for k in range(4):
+        dma("ys"[k % 2], "dnx", "", "nxrow", T.nxrow[16 * (k // 2) + k % 2:16 * (k // 2) + k % 2 + 1, :], T.nx[k % 2:16:2, :])
+    for k in range(8):
+        dma("y", "ds2", "", "stw", T.stw[16 * k:16 * k + 16, :], T.st[:])
     dma("y", "dx", "", "xt", T.xt[:, 4 * XB:4 * A1], T.x[:])
 
     ic, ict, cf, cl, ioL, iw, iw2, ie = T.ic, T.ict, T.cf, T.cl, T.ioL, T.iw, T.iw2, T.ie
-    iota("ic", ic[:, 0:32], [[1, 2], [2, 16]], 0)
+    iota("ic0", ic[:, 0:32], [[1, 2], [2, 8], [6, 2]], 0)
     iota("ioL0", ioL[:, 0:256], [[1, 256]], 0)
     iota("ic", ic[:, 32:64], [[8, 2], [0, 8], [128, 2]], 4, 1)
-    iota("ic", ic[:, 64:96], [[0, 2], [8, 8], [48, 2]], 0, 3)
+    for k in range(2):
+        iota("ic", ic[:, 64 + 16 * k:76 + 16 * k], [[8, 2], [16, 3], [48, 2]], 0, 3)
     iota("ic", ic[:, 96:128], [[0, 2], [1, 16]], 0)
     iota("ic", ic[:, 128:160], [[1, 2], [0, 16]], 0)
-    iota("rl", T.rl[:], [[1, 6], [0, 2]], 0)
+    iota("rl", T.rl[:], [[1, 2], [2, 3], [0, 2]], 0)
     iota("ic1", ic[:, 160:192], [[0, 2], [32, 16]], RB - 33)
     iota("ic2", ic[:, 192:208], [[32, 4], [1, 2], [288, 2]], 1)
     iota("ic2", ic[:, 208:224], [[32, 4], [1, 2], [-256, 2]], 257)
@@ -230,212 +261,202 @@ def rank_program(g, core, T, topo):
         fill("btz", T.btw[a:b, :], 0)
         fill("offz", T.off1[a:b, :], 0)
     fill("m1z", T.m1[:], 0)
+    for k in range(2):
+        fill("icz", ic[:, 76 + 16 * k:80 + 16 * k], 0.0)
     fill("diz", T.di[:, 6:8], 0)
     fill("xz", T.xt[:, 0:4 * XB], 0.0)
     fill("x1", T.x1[:], 0.0)
-    fill("tot0", T.tot[0:32, 1:2], 0.0)
+    fill("stz", T.stu[:, 12:14], 0)
+    fill("pxc", T.px[0:32, 0:32], 0.0)
     fill("pxc", T.px[:, 32:48], 0.0)
     fill("x5", T.x5[0:32, :], 0.0)
+    turn("ic0", "ic0t", ict[:, 0:32], ic[:, 0:32])
     f = lambda j: cf[:, j:j + 1]
-    q15, odd = ict[:, 96:97], ict[:, 128:129]
-    for k in range(4):
-        affine("ioL0", "nxl", T.nxl[:, 8 + 512 * (k // 2) + k % 2:520 + 512 * (k // 2):2], ioL[:, 0:256], bias=XB + 256.0 * (k // 2))
+    q15, odd, part = ict[:, 96:97], ict[:, 128:129], ict[:, 224:225]
     for k in range(1, 4):
         affine("ioL0", "ioL", ioL[:, 256 * k:256 * k + 256], ioL[:, 0:256], bias=256.0 * k)
 
-    o1 = T.o1
-    ts("btw", "b0", o1[0:32, 0:12], T.btw[0:32, :], 1, A.bitwise_and)
-    ts("stw", "e0", o1[0:32, 24:36], T.stw[0:32, :], 2, A.mult)
-    turn("ic", "ict", ict[:, 0:160], ic[:, 0:160])
-    tt("e0 b0", "e1", o1[0:32, 36:48], o1[0:32, 24:36], o1[0:32, 0:12], A.add)
+    o1, b1s, jf, bits = T.o1, T.b1s, T.jf, T.btw[:].indirect(cl[:, 0:1])
+    ts("ic0t", "bl", cl[:, 0:1], ict[:, 0:1], 11.0, A.min)
+    ts("sb6", "e2", o1[0:32, 0:6], T.sb6[0:32, 0:6], 513, A.mult)
+    ts("btw btz bl", "bp", b1s[:, 0:16], bits, BIG, A.mult, -0.5 * BIG, A.add)
+    ts("btw btz bl", "bq0", b1s[:, 16:32], bits, 2.0, A.is_ge, 2 * BIG + 1, A.mult)
+    ts("e2", "e3", o1[0:32, 12:18], o1[0:32, 0:6], 3, A.arith_shift_right, 511, A.bitwise_and)
+    ts("btw btz bl", "bq1", b1s[:, 32:48], bits, 2.0, A.is_ge, 2 * BIG - 1, A.mult)
     copy("nxw", "nxf", T.nxf[0:64, :], T.nxw[0:64, :])
-    ts("ict", "bl", cl[:, 0:1], ict[:, 0:1], 11.0, A.min)
-    ts("e1", "e2", o1[0:32, 48:60], o1[0:32, 36:48], 1025, A.mult)
-    turn("nxf", "nxt", T.nxt[0:64, :], T.nxf[0:64, :])
-    ts("ioL0 ict", "iw2", iw2[:], ioL[:, 0:32], q15, A.is_equal)
-    ts("e2", "e3", o1[0:32, 12:24], o1[0:32, 48:60], 4, A.arith_shift_right, 1023, A.bitwise_and)
-    copy("rl", "rlu", cl[:, 2:14], T.rl[:])
-    ts("btw btz bl", "b1s", T.b1s[:], T.btw[:].indirect(cl[:, 0:1]), 2.0, A.is_ge)
-    copy("e3", "off1", T.off1[0:32, :], o1[0:32, 12:24])
-    ts("ict", "even", f(2), odd, -1.0, A.mult, 1.0, A.add)
-    ts("ict", "q31", f(3), odd, 16.0, A.mult, q15, A.add)
+    copy("e3", "off1", T.off1[0:32, :], o1[0:32, 12:18])
+    turn("ic icz", "ict", ict[:, 32:160], ic[:, 32:160])
     ts("nxrow off1 offz", "n1r", T.n1r[:], T.nxrow[:].indirect(T.off1[:]), 2.0, A.mult)
+    ts("ioL0 ict", "iw2", iw2[:], ioL[:, 0:32], q15, A.is_equal)
+    for k in range(2):
+        tt("bp bq%d" % k, "mk%d" % k, b1s[0:32, 48 + 8 * k:54 + 8 * k], b1s[0:32, 0:6], b1s[0:32, 16 + 16 * k:22 + 16 * k], A.subtract)
+    turn("n1r", "n1t", T.n1t[0:32, :], T.n1r[0:32, :])
+    turn("nxf", "nxt", T.nxt[0:64, :], T.nxf[0:64, :])
+    ts("ict", "q31", f(3), odd, 16.0, A.mult, q15, A.add)
+    tt("n1t mk0", "j0", jf[0:32, 0:6], T.n1t[0:32, 0:96:16], b1s[0:32, 48:54], A.subtract)
+    tt("n1t mk1", "j1", jf[0:32, 6:12], T.n1t[0:32, 1:96:16], b1s[0:32, 56:62], A.add)
+    copy("rl", "rlu", cl[:, 2:14], T.rl[:])
+    ts("ict", "even", f(2), odd, -1.0, A.mult, 1.0, A.add)
+    tt("j0 j1", "jf", jf[0:32, 12:18], jf[0:32, 0:6], jf[0:32, 6:12], A.max)
     ts("ict", "sb", f(0), ict[:, 32:33], -0.125, A.mult)
     ts("ict", "sb", f(1), ict[:, 32:33], -0.125, A.mult, -2.0, A.add)
-    turn("n1r", "n1t", T.n1t[0:32, :], T.n1r[0:32, :])
-    ts("ic q31", "iwf", iw[:, 32:64], ic[:, 96:128], f(3), A.is_equal)
-    ts("ic ict", "mk", T.mk[:], ic[:, 96:128], q15, A.is_equal)
-    tt("n1t b1s", "jf", T.jf[0:32, :], T.n1t[0:32, 0:V:32], T.b1s[0:32, 0:6], A.add)
+    ts("jf m1z", "m1", T.m1[32 * (r // 2):32 * (r // 2) + 32, :], jf[0:32, 12:18], -0.5 * BIG, A.add)
     for k in range(4):
-        ts("n1t", "di", T.di[32 * k:32 * k + 32, 0:6], T.n1t[0:32, 0:V:32], 1.0 / 1024, A.mult, -0.4995, A.add)
-        if k == 1:
-            copy("jf m1z", "m1", T.m1[32 * (r // 2):32 * (r // 2) + 32, :], T.jf[0:32, :])
-    spread("m1", "al1", "land1", T.m1[:], T.land1[:, 6 * r:6 * r + 6], "sent1")
-    affine("iw2", "b0c", f(8), iw2[:, 0:1], scale=BIG)
+        ts("jf", "di", T.di[32 * k:32 * k + 32, 0:6], jf[0:32, 12:18], 1.0 / 1024, A.mult, -0.4995 - BIG / 2048, A.add)
+    spread("m1", "al1", "land1", T.m1[:], lambda d: T.land1[:, 6 * r:6 * r + 6], "sent")
+    for k in range(2):
+        affine("ioL0 ioL iw2", "nxl", T.nxl[:, 8 + k:1032:2], ioL[:, XB:XB + TN], scale=iw2[:, 1:2])
+    affine("iw2", "b0c", f(8), iw2[:, 0:1], scale=float(N * TN))
     act("ict", "aq", f(9), q15, F.Abs, bias=-4.5)
-    affine("ioL0 ioL iw2", "wa", T.wa[:], ioL[:, A1:A2], scale=iw2[:, 2:3])
+    affine("ioL0 ioL iw2", "wa", T.wa[:], ioL[:, 0:A2], scale=iw2[:, 2:3])
     for a in (0, 1032):
         affine("ioL0 b0c", "nxe", T.nxl[:, a:a + 8], ioL[:, 0:8], scale=0.0, bias=f(8))
-    dma("y", "dn0", "nxt", "nxl0 nxl", T.nxl[0:1, 8:1032], T.nxt[0:64, 0:16])
-    for k in range(1, 8):
-        dma("y", "dnl", "nxl0", "nxl1", T.nxl[16 * k:16 * k + 1, 8:1032], T.nxl[0:1, 8:1032])
+    for k in range(8):
+        dma("y", "dnl", "nxt", "nxl", T.nxl[16 * k:16 * k + 1, 8:1032], T.nxt[0:64, 0:16])
     iota("ic3", ic[:, 256:272], [[32, 2], [320, 2], [1, 4]], 1)
     iota("ic3", ic[:, 272:288], [[32, 2], [-288, 2], [1, 4]], 289)
     iota("ic3", ic[:, 288:320], [[256, 2], [1, 16]], 257 + LIFT, 16)
 
+    ts("stw", "stu", T.stu[:, 0:12], T.stw[:], float(XB), A.add)
     copy("m1", "zfo", T.zf[:, 6 * r:6 * r + 6], T.m1[:])
-    ts("stw stw2", "stu", T.stu[:], T.stw[:], float(XB), A.add)
     tt("di diz rlu cdest", "f1", T.f1[:], T.di[:].indirect(cl[:, 2:14]), T.cdest[:], A.is_equal)
-    quant_x("q0 s0", T.q0, T.s0, 0)
+    quant_x(0)
     turn("f1", "f1t", T.f1t[:], T.f1[:])
-    quant_x("q0 s0", T.q0, T.s0, 1)
+    quant_x(1)
     scan("f1t", "c1L", T.c1L[:], T.f1t[:], T.f1t[:], 0.0, A.add, A.max)
     for k in range(2):
-        act("c1L sb", "cnt1 sg", T.sg[:, V * k:V * k + V], T.c1L[:], F.Sign, bias=f(k), accum_out=T.cnt1[:, k:k + 1])
-    quant_x("q0 s0", T.q0, T.s0, 2)
-    quant_x("q0 s0", T.q0, T.s0, 3)
+        act("c1L sb", "x1 sg", T.sg[:, V * k:V * k + V], T.c1L[:], F.Sign, bias=f(k), accum_out=T.x1[:, 32 * k:32 * k + 1])
+    quant_x(2)
+    quant_x(3)
+    ts("ic q31", "iwf0", iw[:, 32:64], ic[:, 96:128], f(3), A.is_equal)
     turn("ic2", "ict2", ict[:, 160:256], ic[:, 160:256])
-    ts("ict even iwf", "iwf", iw[:, 41:64:16], ict[:, 96:98], 9.0, A.is_lt, f(2), A.mult)
+    for k in (9, 11):
+        ts("ict even iwf0", "iwf", iw[:, 32 + k:64:16], ict[:, 96:98], 9.0, A.is_lt, f(2), A.mult)
     fill("iwf", iw[:, 32:64:16], 1.0)
-    ts("ict2", "m9", f(4), ict[:, 224:225], 16.0 * r + 9, A.is_equal)
-    ts("cnt1", "x1", T.x1[:, 0:64:32], T.cnt1[:], -0.5, A.mult, V / 2.0, A.add)
-    ts("ict", "dg", cl[:, 14:15], ict[:, 64:65], 0.125, A.mult, 47.0, A.min)
-    turn("iwf", "iw", iw[:, 0:32], iw[:, 32:64])
+    ts("ict2", "m9", f(4), part, 16.0 * r + 9, A.is_equal)
     turn("x1", "x1t", T.x1t[:], T.x1[:])
     for k in range(8):
         dma("y" if k % 2 else "s", "dc1", "x1t", "w1", T.w1[16 * k:16 * k + 16, :], T.x1t[0:128:32, :])
-    pick("q0", "s0", "stq", "sts", T.stq[:], T.sts[:], T.q0[:], T.s0[:], T.stu[:], "stu")
-    move("y", "dq1", "stq", "sts", "q1s", T.q1, T.s1, SB, T.stq, T.sts, 0, V)
+    ts("ict2 iw2", "late", f(10), part, 16.0 * r + 15, A.is_gt, iw2[:, 9:10], A.mult)
+    ts("ict", "dg", cl[:, 14:15], ict[:, 64:65], 0.125, A.mult, 47.0, A.min)
+    turn("iwf0 iwf", "iw0", iw[:, 64:96], iw[:, 32:64])
+    pick("q0", "s0", "stq", "sts", T.stq[:], T.sts[:], T.q0[:], T.s0[:], T.stu[:, 0:13], "stu stz")
+    dma("y", "dq1", "q0", "q1x", T.q1[:, 0:A1].bitcast(dt.uint8), T.q0[:].bitcast(dt.uint8))
+    dma("y", "dq1", "s0", "q1x", T.s1[:, 0:A1], T.s0[:])
     for k in (1, 0):
         dma("y", "dw%d" % k, "", "wt%d" % k, T.wt[:, 1536 * k:1536 * k + 1536], T.w[:, 1536 * k:1536 * k + 1536])
-    affine("ioL m9", "ci", T.ci[:], ioL[:, SB:SB + V], scale=f(4))
+    affine("m9", "m9n", f(19), f(4), scale=-LOW)
+    affine("ioL0 ioL m9 stu", "ci", T.ci[:, 64:64 + V], ioL[:].indirect(T.stu[:, 0:12]), scale=f(4))
+    affine("iw0 m9n", "iw", iw[:, 0:32], iw[:, 64:96], bias=f(19))
+    affine("ioL0", "ci", T.ci[:, 0:64], ioL[:, 0:64], scale=0.0)
+    affine("late ict2", "first", f(16), f(10), scale=-32.0, bias=ict[:, 160:161])
     affine("iw2", "nb", f(5), iw2[:, r + 1:r + 2], scale=-BIG, bias=BIG)
     affine("ioL0 ioL", "tab2", T.tab2[:], ioL[:, 0:RB + 272], scale=0.0)
-    ts("ioL0 q31 ict2", "pxc", T.px[:, 64:96], ioL[:, 0:32], f(3), A.is_equal, ict[:, 160:161], A.mult)
-    ts("aq", "valid", f(6), f(9), 4.0, A.is_lt)
-    ts("aq even", "valid", f(7), f(9), 4.0, A.is_lt, f(2), A.mult)
-    ts("ioL0 ict2", "la", cl[:, 16:18], ioL[:, 0:129:128], ict[:, 192:193], A.add)
-    for k in range(4):
-        quant_x("q1x", T.q1, T.s1, k)
 
-    m2, tot, px, mi, kk, vt = T.m2, T.tot, T.px, T.mi, T.kk, T.vt
-    cba, bc, pa, c0m, cbb = (kk[:, 12 * k:12 * k + 12] for k in range(5))
-    landed("land1", "zf", T.zf, T.land1, 6)
-    quant_x("q2x", T.q2, T.s2, 0)
+    m2, tot, px, mi, vt = T.m2, T.tot, T.px, T.mi, T.vt
+    cba, bc, pa, cbb = (T.kk[:, 12 * k:12 * k + 12] for k in range(4))
+    for a, b in ((0, 6 * r), (6 * r + 6, 6 * N)):
+        if b > a:
+            copy("land1", "zf", T.zf[:, a:b], T.land1[:, a:b])
+    ts("ic ict", "mk", T.mk[:], ic[:, 96:128], q15, A.is_equal)
+    ts("aq", "valid", f(6), f(9), 4.0, A.is_lt)
     ts("zf zfo dg", "off2", T.off2[:], T.zf[:].indirect(cl[:, 14:15]), 8.0 - 1024 * r, A.add, 1032.0, A.min)
     ts("zf zfo dg", "mi", mi[:], T.zf[:].indirect(cl[:, 14:15]), 1.0 / 1024, A.mult, -0.4995, A.add)
-    copy("nxl nxl1 nxe off2", "n2r", T.n2r[:], T.nxl[:].indirect(T.off2[:, 0:12]))
-    quant_x("q2x", T.q2, T.s2, 1)
+    ts("aq even", "valid", f(7), f(9), 4.0, A.is_lt, f(2), A.mult)
+    copy("nxl nxe off2", "n2r", T.n2r[:], T.nxl[:].indirect(T.off2[:, 0:12]))
+    ts("mi", "cba", cba, mi[:, 0:12], 64.0, A.mult, float(31 - CAP * r), A.add)
+    ts("ioL0 ict2", "la", cl[:, 16:18], ioL[:, 0:129:128], ict[:, 192:193], A.add)
     turn("n2r", "n2t", T.n2t[:], T.n2r[:])
-    quant_x("q2x", T.q2, T.s2, 2)
+    turn("ic3", "ict3", ict[:, 256:320], ic[:, 256:320])
     ts("n2t", "xo", T.xo[:], T.n2t[:, 0:V:16], 1.0 / TN, A.mult, 0.501, A.add)
-    ts("w1", "s1off", T.s1off[:], T.w1[:], V - 1.0, A.min)
-    ts("n2t", "m2a", m2[:, 0:12], T.n2t[:, 0:V:16], -1.0, A.mult, float(N * TN), A.add)
-    act("iw xo", "tot fl", T.fl[:], iw[:, 0:32].indirect(T.xo[:]), F.Identity, accum_out=tot[:, 0:1])
-    affine("fl nb", "fb", T.fb[:], T.fl[:], scale=f(5))
-    pick("stq", "sts", "p1q", "p1s", T.p1q[:], T.p1s[:], T.stq[:], T.sts[:], T.s1off[:], "s1off")
-    at1 = A1 + CAP * r
-    send("p1q", "aq1", "q1a", lambda d: T.p1q[:, CAP * d:CAP * d + CAP].bitcast(dt.uint8), T.q1[:, at1:at1 + CAP].bitcast(dt.uint8), "sent1")
-    send("p1s", "as1", "s1a", lambda d: T.p1s[:, CAP * d:CAP * d + CAP], T.s1[:, at1:at1 + CAP], "sent1")
+    ts("w1", "p1off", T.s1off[:], T.w1[:], -0.5, A.mult, V / 2.0, A.add)
+    ts("n2t", "m2a", T.ab[:, 0:12], T.n2t[:, 0:V:16], -512.0, A.mult, 512.0 * N * TN, A.add)
+    act("iw xo", "tot fl", T.fl[:, 64:64 + V], iw[:, 0:32].indirect(T.xo[:]), F.Identity, accum_out=tot[:, 0:1])
+    affine("fl nb", "fb", T.fb[:], T.fl[:, 64:64 + V], scale=f(5))
+    for k in range(2):
+        leave(1, k, CAP, "stq", "sts", T.p1q, T.p1s, T.stq[:], T.sts[:], T.s1off, T.q1, T.s1, lambda d: A1 + CAP * (r - (r > d)))
     affine("ioL0 ioL", "tab3", T.tab3[:], ioL[:, 0:RB + M + 16], scale=0.0)
-    affine("ioL0", "x3z", T.x3[:], ioL[:, 0:V], scale=0.0)
-    copy("tot", "u1", tot[32:64, 1:2], tot[0:32, 0:1])
     ts("tot", "u2", tot[64:96, 1:2], tot[0:32, 0:1], tot[32:64, 0:1], A.add)
     ts("tot", "u3", tot[96:128, 1:2], tot[0:32, 0:1], tot[32:64, 0:1], A.add, tot[64:96, 0:1], A.add)
+    ts("mk tot valid", "pxa", px[32:64, 0:32], T.mk[0:32, :], tot[0:32, 0:1], A.mult, cf[0:32, 6:7], A.mult)
     ts("iw2 tot valid", "pxb", px[:, 48:64], iw2[:, 0:16], tot[:, 0:1], A.mult, f(7), A.mult)
-    ts("mk tot0 u1 u2 u3 valid", "pxa", px[:, 0:32], T.mk[:], tot[:, 1:2], A.mult, f(6), A.mult)
+    ts("mk u2 u3 valid", "pxa", px[64:128, 0:32], T.mk[64:128, :], tot[64:128, 1:2], A.mult, cf[64:128, 6:7], A.mult)
     turn("fb", "fbt", T.fbt[:], T.fb[:])
-    turn("pxa pxb pxc", "pxt", T.pxt[:], px[:])
-    quant_x("q2x", T.q2, T.s2, 3)
-    summed("pxt", "init", T.init[:], T.pxt[:])
-    turn("ic3", "ict3", ict[:, 256:320], ic[:, 256:320])
-    ts("mi", "cba", cba, mi[:, 0:12], 64.0, A.mult, float(32 - RB - CAP * r), A.add)
-    scan("fl ci init", "cnt", T.cnt[:], T.fl[:], T.ci[:], T.init[:], A.add, A.max)
-    copy("init", "m2c", m2[:, 24:25], T.init[:])
+    turn("pxa pxb pxc", "pxt", T.fl[:, 0:64], px[:])
     ts("ioL0 ioL ict3", "le", cl[:, 18:23], ioL[:, 0:257:64], ict[:, 256:257], A.add, 590.0, A.min)
-    turn("cnt", "vt", vt[:], T.cnt[:])
-    quant_w(5)
-    ts("vt", "c0u", T.c0u[:], vt[:, 9:V:16], -float(A1), A.add)
+    tt("cba fbt", "cbb", cbb, cba, T.fbt[:, 11:V:16], A.subtract)
+    scan("fl pxt ci first", "cnt", T.cnt[:], T.fl[:], T.ci[:], f(16), A.add, A.max)
+    turn("cnt", "vt", vt[:], T.cnt[:, 64:64 + V])
+    copy("cnt", "m2c", m2[:, 12:13], T.cnt[:, 63:64])
+    copy("vt", "c0u", T.c0u[:], vt[:, 9:V:16])
     scan("fbt vt", "seg", T.seg[:], T.fbt[:], vt[:], 0.0, A.max, A.min)
     tt("wa c0u n2r", "vals", T.vals[:], T.wa[:].indirect(T.c0u[:]), T.n2r[:], A.max)
-    copy("seg", "m2b", m2[:, 12:24], T.seg[:, 8:V:16])
-    spread("m2a m2b m2c", "al2", "land2", m2[:, 0:ML], T.land2[:, ML * r:ML * r + ML], "sent2")
-    for a, b in ((A1, at1), (at1 + CAP, A2)):
-        if b > a:
-            move("y", "dq2", "q1a q1s sent2", "s1a q1s", "q2o", T.q2, T.s2, a, T.q1, T.s1, a, b - a)
-    tt("vt fbt", "c0m", c0m, vt[:, 9:V:16], T.fbt[:, 9:V:16], A.min)
-    op("v", "vals m2b tab2", "tab2s", lambda e: e.tensor_copy(T.tab2[:].indirect(m2[:, 12:24]), T.vals[:]))
+    act("seg", "m2b", T.ab[:, 12:24], T.seg[:, 8:V:16], F.Relu, bias=1.0 - RB)
+    copy("seg", "so", T.so[:], T.seg[:, 8:V:16])
+    tt("m2a m2b", "m2", m2[:, 0:12], T.ab[:, 0:12], T.ab[:, 12:24], A.add)
+    spread("m2 m2c", "al2", "land2", m2[:, 0:ML], lambda d: T.land2[:, ML * (r - (r > d)):ML * (r - (r > d)) + ML], "sent2")
+    dma("y", "dq2", "q1x q1a sent2", "q2o", T.q2[:, 0:A2].bitcast(dt.uint8), T.q1[:].bitcast(dt.uint8))
+    dma("y", "dq2", "s1a", "q2o", T.s2[:, 0:A2], T.s1[:])
+    op("v", "vals so tab2", "tab2s", lambda e: e.tensor_copy(T.tab2[:].indirect(T.so[:]), T.vals[:]))
 
     def collect(tag, tab, y, n, lst, gg, rr, w, between):
         turn("tab%ss" % tag, "ya" + tag, y[:, 0:n], tab[:, RB:RB + n])
         turn("tab%ss" % tag, "yb" + tag, y[:, n:2 * n + 32], tab[:, RB - 16:RB + n + 16])
-        ys = "ya%s yb%s l%s" % (tag, tag, "a" if tag == "2" else "e")
+        ys, u = "ya%s yb%s l%s" % (tag, tag, "a" if tag == "2" else "e"), min(w, n // 4)
         between(0)
         copy(ys, "ga" + tag, gg[:, 0:w], y[:, 0:2 * n + 16].indirect(lst))
         between(1)
         tt(ys + " ga" + tag, "gb" + tag, gg[:, w:2 * w], y[:, 16:2 * n + 32].indirect(lst), gg[:, 0:w], A.add)
         between(2)
-        tt("gb" + tag, "ra" + tag, rr[0:64, 0:w], gg[0:64, w:2 * w], gg[64:128, w:2 * w], A.add)
-        tt("ra" + tag, "rb" + tag, rr[0:32, w:2 * w], rr[0:32, 0:w], rr[32:64, 0:w], A.add)
+        tt("gb" + tag, "ra" + tag, rr[0:64, 0:u], gg[0:64, w:w + u], gg[64:128, w:w + u], A.add)
+        tt("ra" + tag, "rb" + tag, rr[0:32, w:w + u], rr[0:32, 0:u], rr[32:64, 0:u], A.add)
 
-    low, lift = 2.0 ** 30, N * (RB - 1 + CAP * r) - (RB - 1)
-    affine("iw2", "al", f(11), iw2[:, 10:11], scale=-low)
-    affine("iw2", "al", f(12), iw2[:, 10:11], scale=low + BIG, bias=1.0)
+    lift = N * (RB - 1 + CAP * r) - (RB - 1)
+    affine("iw2", "al", f(11), iw2[:, 10:11], scale=-LOW)
+    affine("iw2", "al", f(12), iw2[:, 10:11], scale=LOW + BIG, bias=1.0)
     affine("ict", "db", f(15), odd, scale=16.0, bias=1.0 + lift)
     act("ioL0", "oh", ie[:, 16:32], ioL[:, 0:16], F.Abs, bias=-float(r))
     act("ict", "w12", f(13), q15, F.Abs, bias=-1.5)
     act("oh", "oh2", ie[:, 32:48], ie[:, 16:32], F.Relu, scale=-1.0, bias=1.0)
     act("w12", "w12s", f(14), f(13), F.Relu, scale=-2.0, bias=2.0)
-    affine("ioL0 ict3 x3z", "x3", T.x3[:, 4:V:16], ioL[:, 0:V:16], bias=ict[:, 288:289])
-    affine("iw2", "w12a", f(10), iw2[:, 1:2], scale=-32.0, bias=float(A2))
+    affine("iw2", "w12a", f(17), iw2[:, 1:2], scale=-32.0, bias=float(A2))
     affine("ioL0 db", "de", T.de[:], ioL[:, 0:V], bias=f(15))
-    affine("w12s w12a", "w12b", f(13), f(14), scale=f(10))
+    affine("w12s w12a", "w12b", f(18), f(14), scale=f(17))
     affine("oh2 al", "ie", ie[:, 0:16], ie[:, 32:48], scale=f(12), bias=f(11))
     affine("ioL0", "wb", T.wb[:, 0:8], ioL[:, 0:8], scale=0.0)
-    affine("ioL0 ioL w12s w12b", "wb", T.wb[:, 8:768], ioL[:, 8:768], scale=f(14), bias=f(13))
-    copy("m2a m2b m2c", "z2o", T.z2[:, ML * r:ML * r + ML], m2[:, 0:ML])
-    tt("cba c0m", "cbb", cbb, cba, c0m, A.subtract)
-    collect("2", T.tab2, T.y2, 256, cl[:, 16:18], T.g2, T.r2, 32, lambda k: quant_w(4 - k))
+    affine("ioL0 ioL w12s w12b", "wb", T.wb[:, 8:768], ioL[:, 8:768], scale=f(14), bias=f(18))
+    turn("vals", "x3z", T.x3[:], T.vals[:])
+    affine("ioL0 ict3 x3z", "x3", T.x3[:, 4:V:16], ioL[:, 0:V:16], bias=ict[:, 288:289])
+    collect("2", T.tab2, T.y2, 256, cl[:, 16:18], T.g2, T.r2, 32, lambda k: None)
     for k in range(4):
         ts("rb2", "p2off", T.p2off[32 * k:32 * k + 32, :], T.r2[0:32, 32:64], float(XB), A.max)
-    quant_w(1)
-    at2 = A2 + 2 * CAP * r
+    for k in range(2):
+        leave(2, k, 2 * CAP, "q1x q1a", "q1x s1a", T.p2q, T.p2s, T.q1[:], T.s1[:], T.p2off, T.q2, T.s2, lambda d: A2 + 2 * CAP * r)
 
-    def leave(k):
-        part = _parts(core, others, topo)[k][0]
-        a, b = min(T.rank_of(c) for c in part), max(T.rank_of(c) for c in part) + 1
-        only = lambda c, d: (d in topo.cores_of(c)) == (k == 1)
-        pick("q1x q1s q1a", "q1x q1s s1a", "p2q%d" % k, "p2s%d" % k, T.p2q[:, 64 * a:64 * b], T.p2s[:, 64 * a:64 * b],
-             T.q1[:], T.s1[:], T.p2off[:, 4 * a:4 * b], "p2off")
-        send("p2q%d" % k, "aq%d" % (2 + k), "q2a", lambda d: T.p2q[:, 64 * d:64 * d + 64].bitcast(dt.uint8),
-             T.q2[:, at2:at2 + 64].bitcast(dt.uint8), only=only)
-        send("p2s%d" % k, "as%d" % (2 + k), "s2a", lambda d: T.p2s[:, 64 * d:64 * d + 64], T.s2[:, at2:at2 + 64], only=only)
-
-    leave(0)
-
-    z2, zz = T.z2, T.zz
-    landed("land2", "z2", z2, T.land2, ML)
-    leave(1)
-    tt("z2 z2o", "za", zz[:, 0:100], z2[:, 0:100], z2[:, 100:200], A.max)
-    summed("z2 z2o", "bsum", T.bsum[:], z2[:, 24:200:ML])
-    tt("za", "zb", zz[:, 100:150], zz[:, 0:50], zz[:, 50:100], A.max)
-    quant_w(0)
-    tt("zb", "zc", zz[:, 150:175], zz[:, 100:125], zz[:, 125:150], A.max)
-    an, bn = zz[:, 150:162], zz[:, 162:174]
-    ts("zc", "xe", T.xe[:], an, -1.0 / TN, A.mult, N - 0.499, A.add)
+    zz, zi, l2 = T.zz, T.zi, T.land2
+    tt("land2", "za", zz[:, 0:39], l2[:, 0:39], l2[:, 39:78], A.add)
+    tt("land2 m2 m2c", "za", zz[:, 39:52], l2[:, 78:91], m2[:, 0:ML], A.add)
+    quant_w(5)
+    tt("za", "zb", zz[:, 52:78], zz[:, 0:26], zz[:, 26:52], A.add)
+    quant_w(4)
+    tt("zb", "zc", zz[:, 78:91], zz[:, 52:65], zz[:, 65:78], A.add)
+    quant_w(3)
+    an = zz[:, 78:90]
+    ts("zc", "xe", T.xe[:], an, -1.0 / (512 * TN), A.mult, N - 0.5 + 0.6 / TN, A.add)
     act("ie xe", "fe", T.fe[:], ie[:, 0:16].indirect(T.xe[:]))
-    tt("zc cbb", "bc", bc, bn, cbb, A.add)
-    ts("zc x3z", "x3", T.x3[:, 3:V:16], an, -1.0, A.mult, float(LIFT + XB + TN * (N - r)), A.add)
-    copy("bc", "bcu", T.bcu[:], bc)
+    copy("zc", "zi", zi[:, 0:12], an)
+    ts("zc x3z", "x3", T.x3[:, 3:V:16], an, -1.0 / 512, A.mult, LIFT + XB + TN * (N - r) + 0.25, A.add)
+    ts("zi", "zj", zi[:, 12:24], zi[:, 0:12], 511, A.bitwise_and)
     turn("x3", "x3t", T.x3t[:], T.x3[:])
-    scan("fe de bsum", "pe", T.pe[:], T.fe[:], T.de[:], T.bsum[:], A.add, A.max)
-    tt("wb bcu vals", "v3", T.v3[:], T.wb[:].indirect(T.bcu[:]), T.vals[:], A.max)
+    tt("zj cbb", "bc", bc, zi[:, 12:24], cbb, A.add)
+    scan("fe de zc", "pe", T.pe[:], T.fe[:], T.de[:], zz[:, 90:91], A.add, A.max)
+    copy("bc", "bcu", T.bcu[:], bc)
     turn("pe", "pt", T.pt[:], T.pe[:])
-    tt("v3 x3t", "v4", T.v4[:], T.v3[:], T.x3t[:], A.max)
+    tt("wb bcu x3t", "v4", T.v4[:], T.wb[:].indirect(T.bcu[:]), T.x3t[:], A.max)
     tt("pt", "pa", pa, T.pt[:, r + 1:V:16], T.pt[:, 10:V:16], A.min)
     ts("pa", "po", T.po[:], pa, -float(lift), A.add)
     op("v", "v4 po tab3", "tab3s", lambda e: e.tensor_copy(T.tab3[:].indirect(T.po[:]), T.v4[:]))
-    collect("3", T.tab3, T.y3, M, cl[:, 18:23], T.g3, T.r3, 80, lambda k: None)
+    collect("3", T.tab3, T.y3, M, cl[:, 18:23], T.g3, T.r3, 80, lambda k: quant_w(2 - k))
     for k in range(3):
         ts("rb3", "fo0", T.fo[0:32, 18 * k:18 * k + 18], T.r3[0:32, (81, 80, 82)[k]:152:4], -float(LIFT * (k == 2)), A.add)
     ki = T.ki
@@ -445,22 +466,37 @@ def rank_program(g, core, T, topo):
     ts("k0", "k1", ki[0:32, 18:36], ki[0:32, 0:18], 8, A.arith_shift_right)
     ts("k0", "k2", ki[0:32, 36:54], ki[0:32, 0:18], 255, A.bitwise_and)
 
-    for k in (2, 1, 0):
-        src = ("q0", "s0", T.q0[:], T.s0[:]) if k == 2 else ("q2o q2x q2a", "q2o q2x s2a", T.q2[:], T.s2[:])
-        pick(src[0], src[1], "fq%d" % k, "fs%d" % k, T.fq[:, M * k:M * k + M], T.fs[:, M * k:M * k + M], src[2], src[3],
-             T.fo[:, 18 * k:18 * k + 18], "fo0 fo")
-        for o in range(2):
-            c = 128 * (2 * k + o)
-            op("t", "fq%d fs%d wq%d" % (k, k, c // 128), "ps%d" % o, lambda e: e.matmul_mx(
-                T.ps[:, 512 * o:512 * o + M], T.wq[:, c:c + 128], T.ws[:, c:c + 128], T.fq[:, M * k:M * k + M],
-                T.fs[:, M * k:M * k + M], k == 2, k == 0))
+    halves = ((0, 160), (160, M))
+
+    def products(k, parts):
+        a, b = parts[0][0], parts[-1][1]
+        src = ("q0", "s0", T.q0[:], T.s0[:]) if k == 2 else ("q2o q2a", "q2o s2a", T.q2[:], T.s2[:])
+        key = "%d_%d" % (k, a)
+        pick(src[0], src[1], "fq" + key, "fs" + key, T.fq[:, M * k + a:M * k + b], T.fs[:, M * k + a:M * k + b], src[2], src[3],
+             T.fo[:, 18 * k + a // 16:18 * k + b // 16], "fo0 fo")
+        for a, b in parts:
+            for o in range(2):
+                c, bank = 128 * (2 * k + o), 512 * (2 * (a > 0) + o)
+                op("t", "fq%s fs%s wq%d" % (key, key, c // 128), "ps%d" % bank, lambda e: e.matmul_mx(
+                    T.ps[:, bank:bank + b - a], T.wq[:, c:c + 128], T.ws[:, c:c + 128], T.fq[:, M * k + a:M * k + b],
+                    T.fs[:, M * k + a:M * k + b], k == 2, k == 0))
+
+    def store(a, b):
+        bank = 1024 * (a > 0)
+        copy("ps%d" % bank, "yo0%d" % a, T.yo0[:, a:b], T.ps[:, bank:bank + b - a])
+        dma("y", "dy%d" % (2 * (a > 0)), "yo0%d" % a, "y0%d" % a, T.y[:, a:b], T.yo0[:, a:b])
+        act("ps%d" % (bank + 512), "yo1%d" % a, T.yo1[:, a:b], T.ps[:, bank + 512:bank + 512 + b - a])
+        dma("y", "dy%d" % (2 * (a > 0) + 1), "yo1%d" % a, "y1%d" % a, T.y[:, M + a:M + b], T.yo1[:, a:b])
+
+    products(2, halves)
+    for half in halves:
+        products(1, [half])
+        products(0, [half])
     for k in range(2):
         ts("k1 k2", "x5", T.x5[0:32, 32 * k:32 * k + 18], ki[0:32, 18 + 18 * k:36 + 18 * k], -1.0, A.add)
+    store(*halves[0])
     turn("x5", "x5t", T.x5t[0:32, :], T.x5[0:32, :])
-    copy("ps0", "yo0", T.yo0[:], T.ps[:, 0:M])
-    dma("y", "dy0", "yo0", "y0", T.y[:, 0:M], T.yo0[:])
-    act("ps1", "yo1", T.yo1[:], T.ps[:, 512:512 + M])
-    dma("s", "dy1", "yo1", "y1", T.y[:, M:2 * M], T.yo1[:])
+    store(*halves[1])
     for k in range(2):
-        dma("y", "did", "x5t", "id%d" % k, T["id"][k:k + 1, :], T.x5t[0:18, 32 * k:32 * k + 16])
+        dma("s", "did", "x5t", "id%d" % k, T["id"][k:k + 1, :], T.x5t[0:18, 32 * k:32 * k + 16])
     await_("g", [(s, None) for s in total])

@@ -3,12 +3,21 @@ from concourse.mybir import dt, AluOpType as A, ActivationFunctionType as F
 
 N = 8
 TN, V, M, CAP = 512, 192, 288, 32
-XB, A1, A2, QW = 16, 528, 752, 1264
-RB = 224
-ML = 13
+XB, A1, A2, QW = 16, 528, 752, 1200
+NS = (N - 1) * CAP
+U0, U1 = A1 - 16, 272
+KC = 16768
+S0 = KC + U1 + 2 * NS
+P0 = S0 + NS
+CORES = 64
+HANDED = {"s1": 2, "q2": 2, "s2": 2}
+HELP = 2
+ACROSS = 1
+HALF = 160
 BIG = 8192.0
-LOW = 2.0 ** 30
-LIFT = 2048
+MARK = 32768.0
+ROW = 32768.0
+PART = (0, 2, 1, 3)
 X4 = "float8_e4m3fn_x4"
 
 
@@ -17,30 +26,30 @@ def _sb(n, d="float32"):
 
 
 SCRATCH = {
-    "stw": _sb(12, "int32"), "btw": _sb(12, "int32"), "sb6": _sb(8, "int32"), "nxrow": _sb(512, "int32"), "nxw": _sb(32, "int32"),
-    "nxf": _sb(32), "nxt": _sb(32), "nxl": _sb(1040), "xt": _sb(4 * A1, "bfloat16"), "wt": _sb(3072, "bfloat16"),
-    "ic": _sb(320), "ict": _sb(320), "cf": _sb(24), "ioL": _sb(1024), "wa": _sb(A2), "wb": _sb(768), "cl": _sb(32, "uint16"),
-    "rl": _sb(12), "cdest": _sb(V), "ci": _sb(64 + V), "iw": _sb(96), "iw2": _sb(32), "ie": _sb(48), "mk": _sb(32),
-    "o1": _sb(24, "int32"), "off1": _sb(6, "uint16"), "stu": _sb(14, "uint16"), "b1s": _sb(64),
-    "n1r": _sb(96), "n1t": _sb(96), "jf": _sb(18), "m1": _sb(6, "uint16"), "land1": _sb(48, "uint16"), "di": _sb(8, "int32"),
-    "f1": _sb(V, "bfloat16"), "f1t": _sb(V, "bfloat16"), "c1L": _sb(V, "bfloat16"), "sg": _sb(2 * V, "bfloat16"),
-    "x1": _sb(64), "x1t": _sb(64), "w1": _sb(16), "s1off": _sb(16, "uint16"),
-    "zf": _sb(48), "off2": _sb(16, "uint16"), "n2r": _sb(V), "n2t": _sb(V), "xo": _sb(12, "uint16"),
+    "stw": _sb(12, "int32"), "btw": _sb(12, "int32"), "nxrow": _sb(512, "int32"), "nxw": _sb(64, "int32"),
+    "landn": _sb(128, "uint16"), "nxa": _sb(512), "xt": _sb(4 * A1, "bfloat16"), "wt": _sb(3072, "bfloat16"),
+    "ic": _sb(320), "ict": _sb(320), "cf": _sb(48), "ioL": _sb(264), "wa": _sb(U1 + 2 * NS), "cl": _sb(48, "uint16"),
+    "w8": _sb(N), "iq": _sb(V), "iw": _sb(1024), "iwe": _sb(64), "mk": _sb(32),
+    "o1": _sb(32, "int32"), "off1": _sb(16, "uint16"), "stu": _sb(14, "uint16"), "b1s": _sb(64),
+    "n1r": _sb(V), "n1t": _sb(V), "jf": _sb(36), "land1": _sb(128, "uint16"), "di": _sb(12, "uint16"),
+    "f1t": _sb(V, "bfloat16"), "c1L": _sb(V, "bfloat16"), "sg": _sb(2 * V, "bfloat16"),
+    "x1t": _sb(64), "w1": _sb(64, "uint16"), "s1off": _sb(16, "uint16"),
+    "zf": _sb(128), "hi": _sb(16, "uint16"), "ek": _sb(16, "int32"), "lo": _sb(16, "int32"), "nm": _sb(V),
+    "n2r": _sb(V), "n2t": _sb(V), "sel": _sb(V), "xo": _sb(12, "uint16"), "kk": _sb(96),
     "fl": _sb(64 + V), "tot": _sb(2), "px": _sb(64), "cnt": _sb(64 + V), "fb": _sb(V, "bfloat16"), "fbt": _sb(V, "bfloat16"),
-    "vt": _sb(V), "seg": _sb(V), "c0u": _sb(12, "uint16"), "vals": _sb(V), "m2": _sb(16), "so": _sb(12, "uint16"), "ab": _sb(24),
-    "land2": _sb((N - 1) * ML), "tab2": _sb(RB + 272), "y2": _sb(544), "g2": _sb(64), "r2": _sb(64), "p2off": _sb(32, "uint16"),
-    "mi": _sb(16, "int32"), "kk": _sb(48), "zz": _sb(96), "zi": _sb(24, "int32"), "xe": _sb(12, "uint16"),
-    "fe": _sb(V), "de": _sb(V), "pe": _sb(V), "pt": _sb(V), "po": _sb(12, "uint16"), "bcu": _sb(12, "uint16"),
-    "x3": _sb(V), "x3t": _sb(V), "v4": _sb(V), "tab3": _sb(RB + M + 16),
-    "y3": _sb(608), "g3": _sb(160), "r3": _sb(160), "fo": _sb(54, "uint16"), "ki": _sb(64, "int32"), "x5": _sb(64), "x5t": _sb(64),
+    "vt": _sb(V), "seg": _sb(V), "c0u": _sb(12, "uint16"), "vals": _sb(V), "so": _sb(12, "uint16"),
+    "tab": _sb(P0 + M + 16), "y2": _sb(2 * NS + 32), "g2": _sb(64), "r2": _sb(64), "p2off": _sb(28, "uint16"),
+    "po": _sb(12, "uint16"), "bcu": _sb(12, "uint16"), "x3t": _sb(V), "v4": _sb(V),
+    "y3": _sb(608), "g3": _sb(160), "r3": _sb(160), "fo": _sb(54, "uint16"), "ki": _sb(64, "int32"), "x5t": _sb(64),
     "q0": _sb(A1, X4), "s0": _sb(A1, "uint8"), "wq": _sb(768, X4), "ws": _sb(768, "uint8"),
     "stq": _sb(V + 16, X4), "sts": _sb(V + 16, "uint8"), "p1q": _sb(256, X4), "p1s": _sb(256, "uint8"),
-    "q1": _sb(A2, X4), "s1": _sb(A2, "uint8"), "p2q": _sb(512, X4), "p2s": _sb(512, "uint8"),
+    "q1": _sb(A2, X4), "s1": _sb(A2, "uint8"), "p2q": _sb(2 * NS, X4), "p2s": _sb(2 * NS, "uint8"),
     "q2": _sb(QW, X4), "s2": _sb(QW, "uint8"), "fq": _sb(3 * M, X4), "fs": _sb(3 * M, "uint8"),
-    "hq": _sb(2 * CAP, X4), "hs": _sb(2 * CAP, "uint8"), "yo0": _sb(M), "yo1": _sb(M), "ps": ("psum", [128, 2048], "float32"),
+    "hq1": _sb(CAP, X4), "hs1": _sb(CAP, "uint8"), "hq2": _sb(2 * CAP, X4), "hs2": _sb(2 * CAP, "uint8"),
+    "yo0": _sb(M), "yo1": _sb(M), "ps": ("psum", [128, 2048], "float32"),
 }
-SEMAPHORES = ["cv", "cs_", "ct", "cg", "dst", "ds2", "dbt", "dnx", "dnw", "dnl", "dx", "dw0", "dw1", "dc1", "dq1", "dq2", "dy0", "dy1",
-              "dy2", "dy3", "did", "sent", "sent2", "al1", "al2", "aq0", "as0", "aq1", "as1", "aq2", "as2", "aq3", "as3", "ahq", "ahs"]
+SEMAPHORES = ["cv", "cs_", "ct", "cg", "dst", "ds2", "dbt", "dnx", "dnw", "dx0", "dx1", "dw0", "dw1", "dc1", "dq1", "dq2", "dq3", "dy0", "dy1",
+              "dy2", "dy3", "did", "sent", "an", "al1", "aq1", "as1", "aq2", "as2", "hq1", "hs1", "hq2", "hs2"]
 
 
 def _parts(core, others, topo):
@@ -49,21 +58,9 @@ def _parts(core, others, topo):
     near = [c for c in others if c in own]
     out, taken = [], []
     for part in (far, near):
-        if part:
-            free = [e for e in topo.engines(core, part[0]) if e not in taken]
-            out.append((part, free))
-            taken += free
-    return out
-
-
-def _split(core, others, topo):
-    out = {}
-    for part, free in _parts(core, others, topo):
-        k = 1
-        while 2 * k * len(part) <= len(free):
-            k *= 2
-        for j, c in enumerate(part):
-            out[c] = free[j * k:(j + 1) * k]
+        free = [e for e in topo.engines(core, part[0]) if e not in taken]
+        out.append((part, free))
+        taken += free
     return out
 
 
@@ -72,26 +69,57 @@ def _mask(engines):
 
 
 def _helpers(T, topo):
-    out = {}
+    out, taken = {}, list(T.cores)
     for c in T.cores:
         own = [b for b in T.cores if b in topo.cores_of(c)]
-        free = [b for b in topo.cores_of(c) if b not in T.cores and topo.die(b) != topo.die(c)]
         far = [b for b in T.cores if b not in own]
-        out[c] = (free[own.index(c)], far[own.index(c)])
+        d = far[own.index(c)]
+        beside = [b for b in topo.cores_of(c) if topo.die(b) != topo.die(c)]
+        beyond = [b for b in range(CORES) if topo.mates(topo.chip(b), topo.chip(d)) and topo.may_write(c, b) and topo.may_write(b, d)]
+        if not beyond and own.index(c) < ACROSS:
+            beyond = [b for b in range(CORES) if topo.die(b) != topo.die(c) and all(topo.same_plane(topo.chip(b), topo.chip(a)) for a in (c, d))]
+        out[c] = []
+        for to, free in [(d, beside)] + [(far[own.index(c) - j], beyond) for j in range(1, HELP)]:
+            free = [b for b in free if b not in taken]
+            if free:
+                out[c].append((to, free[0]))
+                taken.append(free[0])
     return out
 
 
+def _calls(c, move, T, topo):
+    (far, ef), (near, en) = _parts(c, [b for b in T.cores if b != c], topo)
+    q = len(ef) // 4
+    three = lambda e: (e[:2 * q], e[2 * q:3 * q], e[3 * q:])
+    if move not in HANDED:
+        return [[(d, ef[q * j:q * j + q], None) for j, d in enumerate(far)] + [(d, e, None) for d, e in zip(near, three(en))]]
+    (d0, h0), *more = _helpers(T, topo)[c][:HANDED[move]]
+    if move == "s2":
+        more = [(d, h) for d, h in more if topo.mates(topo.chip(d), topo.chip(h))]
+    ways = more + [(d, None) for d in far if d != d0 and d not in dict(more)]
+    if move[1] == "1":
+        pairs = [(ef + en[2 * q:])[q * j:q * j + q] for j in range(6)]
+        return [[(d0, en[:2 * q], h0)] + [(d, e, h) for (d, h), e in zip(ways + [(d, None) for d in near], pairs)]]
+    return [[(d0, en, h0)] + [(d, e, h) for (d, h), e in zip(ways, three(ef))], [(d, e, None) for d, e in zip(near, three(en))]]
+
+
+def _among(T, c, b):
+    return [a for a in T.cores if a != c].index(b)
+
+
 def hand_on(g, core, T, topo):
-    for c, (h, d) in _helpers(T, topo).items():
-        if h == core:
-            n_in = len(_parts(c, [b for b in T.cores if b != c], topo)[1][1])
-            at = A2 + 2 * CAP * T.rank_of(c)
+    u8 = lambda ap: ap.bitcast(dt.uint8)
+    for c, ways in _helpers(T, topo).items():
+        for d in [d for d, h in ways if h == core]:
+            a, b = A1 + CAP * _among(T, d, c), A2 + 2 * CAP * _among(T, d, c)
             rid, pid = topo.addr(d)[:2]
-            for s_in, s_out, src, dst in (("ahq", "aq2", T.hq[:].bitcast(dt.uint8), T.q2[:, at:at + 2 * CAP].bitcast(dt.uint8)),
-                                          ("ahs", "as2", T.hs[:], T.s2[:, at:at + 2 * CAP])):
-                g.wait_ge(T.sem[s_in], n_in)
-                g.remote_dma(dst, src, T.sem[s_out], T.sem.sent, pid, rid, topo.mask(core, d))
-            g.wait_ge(T.sem.sent, 2 * len(topo.engines(core, d)))
+            sides = {"s1": (T.hs1[:], T.s1[:, a:a + CAP]), "q1": (u8(T.hq1[:]), u8(T.q1[:, a:a + CAP])),
+                     "q2": (u8(T.hq2[:]), u8(T.q2[:, b:b + 2 * CAP])), "s2": (T.hs2[:], T.s2[:, b:b + 2 * CAP])}
+            moves = [(move, len(e)) for move in HANDED for to, e, h in _calls(c, move, T, topo)[0] if h == core]
+            for move, n in moves:
+                g.wait_ge(T.sem["h" + move], n)
+                g.remote_dma(sides[move][1], sides[move][0], T.sem["a" + move], T.sem.sent, pid, rid, topo.mask(core, d))
+            g.wait_ge(T.sem.sent, len(moves) * len(topo.engines(core, d)))
 
 
 def rank_program(g, core, T, topo):
@@ -190,219 +218,231 @@ def rank_program(g, core, T, topo):
     others = [c for c in T.cores if c != core]
     rest = lambda c: [b for b in T.cores if b != c]
     place = lambda c: DstId(rid=topo.addr(c)[0], pnc=topo.addr(c)[1])
-    helpers = _helpers(T, topo)
+    u8 = lambda ap: ap.bitcast(dt.uint8)
 
-    def send(r_, s, w_, src, dst, only, via=None):
+    def send(move, k, kind, r_, src, dst, via=None):
         deps("g", r_.split(), [])
-        engines = _split(core, others, topo)
-        ways = [(c, engines[c], s, dst(T.rank_of(c)), c) for c in others if only(core, c)]
-        if via:
-            h, d = helpers[core]
-            ways = [w for w in ways if w[0] != d] + [(h, _parts(core, others, topo)[1][1], via[0], via[1], d)]
-        g.remote_dma_fused([RemoteDMATransfer(dst_ids=[place(c)], dma_engine_mask=_mask(e), remote_sem=sem[a], src=src(T.rank_of(d)),
-                                              dst=to) for c, e, a, to, d in ways], local_sem=sem.sent)
-        total["sent"] = total.get("sent", 0) + sum(len(w[1]) for w in ways)
-        total[s] = sum(len(topo.engines(helpers[c][0], core)) if via and helpers[c][1] == core else len(_split(c, rest(c), topo)[core])
-                       for c in others if only(c, core))
-        wrote.setdefault(w_, []).append((s, total[s]))
+        move = kind + str(move)
+        s, ways = "a" + move, _calls(core, move, T, topo)[k]
+        g.remote_dma_fused([RemoteDMATransfer(dst_ids=[place(h or c)], dma_engine_mask=_mask(e),
+                                              remote_sem=sem["h" + s[1:] if h else s], src=src(c), dst=via if h else dst(c))
+                            for c, e, h in ways], local_sem=sem.sent)
+        total["sent"] = total.get("sent", 0) + sum(len(e) for c, e, h in ways)
+        total[s] = sum(len(topo.engines(h, core) if h else e)
+                       for c in others for call in _calls(c, move, T, topo) for d, e, h in call if d == core)
+        wrote[move + "a"] = [(s, None)]
 
-    def spread(r_, s, w_, src, dst, left):
+    def spread(r_, s, w_, block):
         deps("g", r_.split(), [])
-        parts = _parts(core, others, topo)
-        g.remote_dma_fused([RemoteDMATransfer(dst_ids=[place(c) for c in part], dma_engine_mask=_mask(free), remote_sem=sem[s],
-                                              srcs=[src], dsts=[dst(T.rank_of(c)) for c in part]) for part, free in parts],
-                           local_sem=sem[left])
-        total[left] = total.get(left, 0) + sum(len(free) for part, free in parts)
-        wrote[left] = [(left, None)]
-        total[s] = sum(len(free) for c in others for part, free in _parts(c, rest(c), topo) if core in part)
-        wrote.setdefault(w_, []).append((s, total[s]))
-
-    def leave(tag, k, n, rq, rs, pq, pz, q, s, off, dq, ds, at):
-        part = _parts(core, others, topo)[k][0]
-        a, b = min(T.rank_of(c) for c in part), max(T.rank_of(c) for c in part) + 1
-        only = lambda c, d: (d in topo.cores_of(c)) == (k == 1)
-        key = "%d%d" % (tag, k)
-        pick(rq, rs, "pq" + key, "pz" + key, pq[:, n * a:n * b], pz[:, n * a:n * b], q, s, off[:, n * a // 16:n * b // 16], "p%doff" % tag)
-        send("pq" + key, "aq%d" % (2 * tag - 2 + k), "q%da" % tag, lambda d: pq[:, n * d:n * d + n].bitcast(dt.uint8),
-             lambda d: dq[:, at(d):at(d) + n].bitcast(dt.uint8), only, key == "20" and ("ahq", T.hq[:].bitcast(dt.uint8)))
-        send("pz" + key, "as%d" % (2 * tag - 2 + k), "s%da" % tag, lambda d: pz[:, n * d:n * d + n],
-             lambda d: ds[:, at(d):at(d) + n], only, key == "20" and ("ahs", T.hs[:]))
+        ways = _calls(core, 0, T, topo)[0]
+        g.remote_dma_fused([RemoteDMATransfer(dst_ids=[place(c)], dma_engine_mask=_mask(e), remote_sem=sem[s], src=block, dst=block)
+                            for c, e, by in ways], local_sem=sem.sent)
+        total["sent"] = total.get("sent", 0) + sum(len(e) for c, e, by in ways)
+        total[s] = sum(len(e) for c in others for d, e, by in _calls(c, 0, T, topo)[0] if d == core)
+        wrote[w_] = [(s, None)]
 
     fill("nxrow", T.nxrow[:], 0)
     for k in range(2):
-        dma("s", "dst", "", "sb6", T.sb6[16 * k:16 * k + 16, 0:6], T.st[:, 6 * k:6 * k + 6])
+        dma("sy"[k], "dnw", "", "nxw", T.nxw[16 * k:16 * k + 16, :], T.nx[:])
+    for k in range(2):
+        dma("s", "dst", "", "st01", T.stw[16 * k:16 * k + 16, :], T.st[:])
         dma("y", "dbt", "", "btw", T.btw[16 * k:16 * k + 16, :], T.bt[:])
     for k in range(4):
-        dma("s", "dnw", "", "nxw", T.nxw[16 * k:16 * k + 16, :], T.nx[:, 32 * (k // 2):32 * (k // 2) + 32])
-    for k in range(4):
         dma("ys"[k % 2], "dnx", "", "nxrow", T.nxrow[16 * (k // 2) + k % 2:16 * (k // 2) + k % 2 + 1, :], T.nx[k % 2:16:2, :])
-    for k in range(8):
-        dma("y", "ds2", "", "stw", T.stw[16 * k:16 * k + 16, :], T.st[:])
-    dma("y", "dx", "", "xt", T.xt[:, 4 * XB:4 * A1], T.x[:])
+    for k in range(2, 8):
+        dma("ys"[k % 2], "ds2", "", "stw", T.stw[16 * k:16 * k + 16, :], T.st[:])
+    dma("y", "dx0", "", "xt", T.xt[:, 4 * XB:4 * A1], T.x[:])
 
-    ic, ict, cf, cl, ioL, iw, iw2, ie = T.ic, T.ict, T.cf, T.cl, T.ioL, T.iw, T.iw2, T.ie
-    iota("ic0", ic[:, 0:32], [[1, 2], [2, 8], [6, 2]], 0)
-    iota("ioL0", ioL[:, 0:256], [[1, 256]], 0)
-    iota("ic", ic[:, 32:64], [[8, 2], [0, 8], [128, 2]], 4, 1)
-    for k in range(2):
-        iota("ic", ic[:, 64 + 16 * k:76 + 16 * k], [[8, 2], [16, 3], [48, 2]], 0, 3)
+    ic, ict, cf, cl, ioL, iw, mk = T.ic, T.ict, T.cf, T.cl, T.ioL, T.iw, T.mk
+    iq = T.iq
     iota("ic", ic[:, 96:128], [[0, 2], [1, 16]], 0)
-    iota("ic", ic[:, 128:160], [[1, 2], [0, 16]], 0)
-    iota("rl", T.rl[:], [[1, 2], [2, 3], [0, 2]], 0)
-    iota("ic1", ic[:, 160:192], [[0, 2], [32, 16]], RB - 33)
-    iota("ic2", ic[:, 192:208], [[32, 4], [1, 2], [288, 2]], 1)
-    iota("ic2", ic[:, 208:224], [[32, 4], [1, 2], [-256, 2]], 257)
-    iota("ic2", ic[:, 160:192:16], [[16, 2]], 0, after="ic1")
-    iota("ic2", ic[:, 169:192:16], [[32, 2]], A1 - 1, 2)
-    iota("ic2", ic[:, 170:192:16], [[0, 2]], 0)
-    iota("ic2", ic[:, 224:256], [[1, 32]], 0, 1)
-    iota("cdest", T.cdest[:], [[0, 12], [1, 8], [0, 2]], 0)
-    for a, b in ((32, 64), (64, 128)):
-        fill("btz", T.btw[a:b, :], 0)
-        fill("offz", T.off1[a:b, :], 0)
-    fill("m1z", T.m1[:], 0)
-    for k in range(2):
-        fill("icz", ic[:, 76 + 16 * k:80 + 16 * k], 0.0)
-    fill("diz", T.di[:, 6:8], 0)
-    fill("xz", T.xt[:, 0:4 * XB], 0.0)
-    fill("x1", T.x1[:], 0.0)
-    fill("stz", T.stu[:, 12:14], 0)
-    fill("pxc", T.px[0:32, 0:32], 0.0)
-    fill("pxc", T.px[:, 32:48], 0.0)
-    fill("x5", T.x5[0:32, :], 0.0)
-    turn("ic0", "ic0t", ict[:, 0:32], ic[:, 0:32])
+    iota("ic", ic[:, 128:160], [[-1, 2], [0, 16]], 1)
+    iota("ic", ic[:, 160:192], [[1, 32]], 0, 1)
+    iota("ic0", ic[:, 0:32], [[1, 2], [2, 8], [0, 2]], 0)
+    iota("ic0", ic[:, 32:64], [[-8, 2], [0, 8], [-128, 2]], -4, -1)
+    iota("ic0", ic[:, 64:96], [[1, 2], [2, 8], [16, 2]], 0, 1)
+    iota("ioL0", ioL[:, 0:132], [[1, 132]], 0)
+    iota("iq", iq[:], [[0, 12], [1, 16]], 0)
+    mine1, minen = T.land1[:, 16 * r:16 * r + 16], T.landn[:, 16 * r:16 * r + 16]
     f = lambda j: cf[:, j:j + 1]
-    q15, odd, part = ict[:, 96:97], ict[:, 128:129], ict[:, 224:225]
-    for k in range(1, 4):
-        affine("ioL0", "ioL", ioL[:, 256 * k:256 * k + 256], ioL[:, 0:256], bias=256.0 * k)
+    q15, even, part = ict[:, 96:97], ict[:, 128:129], ict[:, 160:161]
+    below = lambda j: cf[:, 32 + j:33 + j]
+    x1, x3, x5 = ic[:, 128:192], T.n1r, ic[0:32, 0:64]
+    fill("oz", T.o1[:, 16:32], 0)
+    fill("m1z", mine1, 0)
+    turn("ic", "ict", ict[:, 96:192], ic[:, 96:192])
+    fill("xz", T.xt[:, 0:4 * XB], 0.0)
+    fill("stz", T.stu[:, 12:14], 0)
+    ts("ic ict", "bel", cf[:, 32:48], ic[:, 96:112], q15, A.is_gt)
+    ts("ic ict", "mk", mk[:], ic[:, 96:128], q15, A.is_equal)
+    ts("ict", "own", f(16), part, q15, A.subtract, 16.0 * r, A.is_equal)
+    ts("ict bel", "q7", f(5), below(8), 7.0, A.mult, q15, A.add)
 
-    o1, b1s, jf, bits = T.o1, T.b1s, T.jf, T.btw[:].indirect(cl[:, 0:1])
-    ts("ic0t", "bl", cl[:, 0:1], ict[:, 0:1], 11.0, A.min)
-    ts("sb6", "e2", o1[0:32, 0:6], T.sb6[0:32, 0:6], 513, A.mult)
-    ts("btw btz bl", "bp", b1s[:, 0:16], bits, BIG, A.mult, -0.5 * BIG, A.add)
-    ts("btw btz bl", "bq0", b1s[:, 16:32], bits, 2.0, A.is_ge, 2 * BIG + 1, A.mult)
-    ts("e2", "e3", o1[0:32, 12:18], o1[0:32, 0:6], 3, A.arith_shift_right, 511, A.bitwise_and)
-    ts("btw btz bl", "bq1", b1s[:, 32:48], bits, 2.0, A.is_ge, 2 * BIG - 1, A.mult)
-    copy("nxw", "nxf", T.nxf[0:64, :], T.nxw[0:64, :])
-    copy("e3", "off1", T.off1[0:32, :], o1[0:32, 12:18])
-    turn("ic icz", "ict", ict[:, 32:160], ic[:, 32:160])
-    ts("nxrow off1 offz", "n1r", T.n1r[:], T.nxrow[:].indirect(T.off1[:]), 2.0, A.mult)
-    ts("ioL0 ict", "iw2", iw2[:], ioL[:, 0:32], q15, A.is_equal)
+    is0, is1, is15 = below(1), mk[:, 1:2], mk[:, 15:16]
+    first = KC + U1 - 1.0 - 2 * CAP
+    ts("ict bel", "c01", f(14), part, 16.0 * r, A.not_equal, is0, A.mult)
+    turn("ic0", "ic0t", ict[:, 0:96], ic[:, 0:96])
+    ts("q7", "d1", f(15), f(5), r + 8.0, A.is_ge, f(5), A.add)
+    ts("ict", "m8", f(26), q15, 8.0, A.min, q15, A.add)
+    copy("ic0t", "pl dg", cl[:, 0:15:14], ict[:, 0:65:64])
+    copy("ict", "dg", cl[:, 2:3], part)
+    affine("ict", "lift", f(3), q15, scale=-ROW, bias=15 * ROW)
+    affine("mk", "wb", f(10), is1, scale=float(U0))
+    affine("mk", "wb", f(17), is1, scale=float(U0 + 16 + CAP * r))
+    affine("own", "fc", f(22), f(16), scale=256.0, bias=167.0 + 256 * CAP - first)
+    affine("mk", "w32", f(11), is1, scale=float(CAP))
+    affine("d1", "t1", f(18), f(15), scale=7.0, bias=-56.0 - 7 * r)
+    affine("c01", "c256", f(23), f(14), scale=256.0)
+    affine("t1 d1 bel", "t2", f(20), f(18), scale=below(8), bias=f(15))
+    affine("ioL0", "ioL", ioL[:, 132:264], ioL[:, 0:132], bias=132.0)
+    affine("fc ict", "fe", f(30), even, scale=-16.0 - 256 * CAP, bias=f(22))
+    affine("m8", "fd", f(29), f(26), scale=32.0, bias=first)
+    a, b = 16 + CAP * r, 16 + CAP * r + CAP
+    e = min(b, 264)
+    affine("ioL mk wb", "wa0", T.wa[:, 0:e], ioL[:, 0:e], scale=is1, bias=f(10))
+    affine("fd fe bel", "first", f(28), f(30), scale=is0, bias=f(29))
+    affine("ioL mk wb", "wa0", T.wa[:, e:U1], ioL[:, 0:U1 - e], scale=is1, bias=f(17))
     for k in range(2):
-        tt("bp bq%d" % k, "mk%d" % k, b1s[0:32, 48 + 8 * k:54 + 8 * k], b1s[0:32, 0:6], b1s[0:32, 16 + 16 * k:22 + 16 * k], A.subtract)
+        affine("bel w32", "wb2", f(12 + k), below(2), scale=float(A2 + NS * k), bias=f(11))
+
+    def lay(k):
+        ts("nxw", "minen", T.landn[32 * k:32 * k + 32, 16 * r:16 * r + 16], T.nxw[0:32, PART[k]:64:4], float(N * TN * r), A.add)
+
+    o1, b1s, jf, bt = T.o1, T.b1s, T.jf, T.btw[0:32, :]
+    ts("st01", "e2", o1[0:32, 0:12], T.stw[0:32, :], 513, A.mult)
+    lay(0)
+    lay(1)
+    ts("e2 oz", "e3", o1[0:32, 16:28], o1[0:32, 0:12], 3, A.arith_shift_right, 511, A.bitwise_and)
+    lay(2)
+    lay(3)
+    spread("minen", "an", "landn", minen)
+    copy("e3 oz pl", "off1", T.off1[:], o1[:, 16:32].indirect(cl[:, 0:1]))
+    ts("btw", "bp", b1s[0:32, 0:12], bt, BIG, A.mult, -0.5 * BIG, A.add)
+    ts("btw", "bq0", b1s[0:32, 12:24], bt, 2.0, A.is_ge, 2 * BIG + 1, A.mult)
+    ts("nxrow off1", "n1r", T.n1r[:], T.nxrow[:].indirect(T.off1[:, 0:12]), 2.0, A.mult)
+    ts("btw", "bq1", b1s[0:32, 24:36], bt, 2.0, A.is_ge, 2 * BIG - 1, A.mult)
+    ts("ioL0 t2", "iwe", T.iwe[:], ioL[:, 0:64], 8.0 - 8 * r, A.add, f(20), A.is_equal)
     turn("n1r", "n1t", T.n1t[0:32, :], T.n1r[0:32, :])
-    turn("nxf", "nxt", T.nxt[0:64, :], T.nxf[0:64, :])
-    ts("ict", "q31", f(3), odd, 16.0, A.mult, q15, A.add)
-    tt("n1t mk0", "j0", jf[0:32, 0:6], T.n1t[0:32, 0:96:16], b1s[0:32, 48:54], A.subtract)
-    tt("n1t mk1", "j1", jf[0:32, 6:12], T.n1t[0:32, 1:96:16], b1s[0:32, 56:62], A.add)
-    copy("rl", "rlu", cl[:, 2:14], T.rl[:])
-    ts("ict", "even", f(2), odd, -1.0, A.mult, 1.0, A.add)
-    tt("j0 j1", "jf", jf[0:32, 12:18], jf[0:32, 0:6], jf[0:32, 6:12], A.max)
-    ts("ict", "sb", f(0), ict[:, 32:33], -0.125, A.mult)
-    ts("ict", "sb", f(1), ict[:, 32:33], -0.125, A.mult, -2.0, A.add)
-    ts("jf m1z", "m1", T.m1[32 * (r // 2):32 * (r // 2) + 32, :], jf[0:32, 12:18], -0.5 * BIG, A.add)
-    for k in range(4):
-        ts("jf", "di", T.di[32 * k:32 * k + 32, 0:6], jf[0:32, 12:18], 1.0 / 1024, A.mult, -0.4995 - BIG / 2048, A.add)
-    spread("m1", "al1", "land1", T.m1[:], lambda d: T.land1[:, 6 * r:6 * r + 6], "sent")
     for k in range(2):
-        affine("ioL0 ioL iw2", "nxl", T.nxl[:, 8 + k:1032:2], ioL[:, XB:XB + TN], scale=iw2[:, 1:2])
-    affine("iw2", "b0c", f(8), iw2[:, 0:1], scale=float(N * TN))
-    act("ict", "aq", f(9), q15, F.Abs, bias=-4.5)
-    affine("ioL0 ioL iw2", "wa", T.wa[:], ioL[:, 0:A2], scale=iw2[:, 2:3])
-    for a in (0, 1032):
-        affine("ioL0 b0c", "nxe", T.nxl[:, a:a + 8], ioL[:, 0:8], scale=0.0, bias=f(8))
-    for k in range(8):
-        dma("y", "dnl", "nxt", "nxl", T.nxl[16 * k:16 * k + 1, 8:1032], T.nxt[0:64, 0:16])
-    iota("ic3", ic[:, 256:272], [[32, 2], [320, 2], [1, 4]], 1)
-    iota("ic3", ic[:, 272:288], [[32, 2], [-288, 2], [1, 4]], 289)
-    iota("ic3", ic[:, 288:320], [[256, 2], [1, 16]], 257 + LIFT, 16)
+        tt("bp bq%d" % k, "mk%d" % k, b1s[0:32, 36 + 12 * k:48 + 12 * k], b1s[0:32, 0:12], b1s[0:32, 12 + 12 * k:24 + 12 * k], A.subtract)
+    tt("n1t mk0", "j0", jf[0:32, 0:12], T.n1t[0:32, 0:V:16], b1s[0:32, 36:48], A.subtract)
+    tt("n1t mk1", "j1", jf[0:32, 12:24], T.n1t[0:32, 1:V:16], b1s[0:32, 48:60], A.add)
+    ts("iwe bel", "iw0", iw[:, 0:64], T.iwe[:], below(15), A.mult, is0, A.max)
+    tt("mk", "w8", T.w8[:], mk[:, 0:16:2], mk[:, 1:16:2], A.add)
+    tt("j0 j1", "jf", jf[0:32, 24:36], jf[0:32, 0:12], jf[0:32, 12:24], A.max)
+    ts("st01 stw", "stu", T.stu[:, 0:12], T.stw[:], float(XB), A.add)
+    ts("st01 stw own n1t", "x3", x3[:, 1:V:16], T.stw[:], float(XB), A.add, f(16), A.mult)
+    ts("jf m1z", "m1", T.land1[32 * (r // 2):32 * (r // 2) + 32, 16 * r:16 * r + 12], jf[0:32, 24:36], -0.5 * BIG, A.add)
+    for k in range(4):
+        ts("jf", "di", T.di[32 * k:32 * k + 32, :], jf[0:32, 24:36], 1.0 / 1024, A.mult, -0.4995 - BIG / 2048, A.add)
+    spread("m1", "al1", "land1", mine1)
+    iota("ic2", ic[:, 192:224], [[0, 32]], 14, 2)
+    iota("ic2", ic[:, 288:320], [[256, 2], [1, 16]], 256, 16)
+    iota("ic2", ic[:, 224:240], [[32, 4], [1, 2], [NS + 32, 2]], 0)
+    iota("ic2", ic[:, 240:256], [[32, 4], [1, 2], [-NS, 2]], NS)
+    iota("ic2", ic[:, 256:272], [[32, 2], [M + 32, 2], [1, 4]], 0)
+    iota("ic2", ic[:, 272:288], [[32, 2], [-M, 2], [1, 4]], M)
 
-    ts("stw", "stu", T.stu[:, 0:12], T.stw[:], float(XB), A.add)
-    copy("m1", "zfo", T.zf[:, 6 * r:6 * r + 6], T.m1[:])
-    tt("di diz rlu cdest", "f1", T.f1[:], T.di[:].indirect(cl[:, 2:14]), T.cdest[:], A.is_equal)
-    quant_x(0)
-    turn("f1", "f1t", T.f1t[:], T.f1[:])
-    quant_x(1)
+    affine("iw0 mk", "iw1", iw[:, r:64:8], iw[:, r:64:8], bias=is15)
+    affine("iw1 c256", "iw64", iw[:, 8 * r:8 * r + 8], iw[:, 8 * r:8 * r + 8], bias=f(23))
+    act("w8 di", "f1t", T.f1t[:], T.w8[:].indirect(T.di[:]))
+    for k in (64, 128):
+        act("iw%d" % k, "iw%d" % (2 * k), iw[:, k:2 * k], iw[:, 0:k])
+
+    nxa = T.nxa
+    quarter = lambda k, j: nxa[32 * k:32 * k + 32, PART[j]:512:4]
+
+    def lifted(k):
+        ts("landn minen lift", "na%d" % k, quarter(k, k), T.landn[32 * k:32 * k + 32, :], cf[32 * k:32 * k + 32, 3:4], A.add)
+
+    def paired(k, call):
+        call("na%d" % (k ^ 1), "nb%d" % k, quarter(k, k ^ 1), quarter(k ^ 1, k ^ 1))
+
+    for k in range(4):
+        quant_x(k)
     scan("f1t", "c1L", T.c1L[:], T.f1t[:], T.f1t[:], 0.0, A.add, A.max)
     for k in range(2):
-        act("c1L sb", "x1 sg", T.sg[:, V * k:V * k + V], T.c1L[:], F.Sign, bias=f(k), accum_out=T.x1[:, 32 * k:32 * k + 1])
-    quant_x(2)
-    quant_x(3)
-    ts("ic q31", "iwf0", iw[:, 32:64], ic[:, 96:128], f(3), A.is_equal)
-    turn("ic2", "ict2", ict[:, 160:256], ic[:, 160:256])
-    for k in (9, 11):
-        ts("ict even iwf0", "iwf", iw[:, 32 + k:64:16], ict[:, 96:98], 9.0, A.is_lt, f(2), A.mult)
-    fill("iwf", iw[:, 32:64:16], 1.0)
-    ts("ict2", "m9", f(4), part, 16.0 * r + 9, A.is_equal)
-    turn("x1", "x1t", T.x1t[:], T.x1[:])
+        act("c1L ic0t ict", "x1 sg", T.sg[:, V * k:V * k + V], T.c1L[:], F.Sign, scale=8.0, bias=ict[:, 32 + 16 * k:33 + 16 * k],
+            accum_out=x1[:, 32 * k:32 * k + 1])
+    for k in (256, 512):
+        op("g", "iw%d" % k, "iw%d" % (2 * k), lambda e: e.affine_select(iw[:, k:2 * k], iw[:, 0:k], [[0, k]], A.is_ge, 0.0, 0, 0))
+    for k in range(4):
+        lifted(k)
+    for k in (1, 0, 3, 2):
+        paired(k, (copy, act)[k // 2])
+    turn("x1", "x1t", T.x1t[:], x1)
+    op("v", "wa0", "wa", lambda e: e.memset(T.wa[:, 0:a + 1:a], 0.0))
+    copy("ioL0", "xl", cl[:, 16:28], ioL[:, 0:12])
+    ts("x1t", "w1", T.w1[:], T.x1t[:], -0.5, A.mult, V / 2.0, A.add)
+    act("na2 na3 nb2 nb3", "nc2", nxa[0:64, 1:512:2], nxa[64:128, 1:512:2])
     for k in range(8):
-        dma("y" if k % 2 else "s", "dc1", "x1t", "w1", T.w1[16 * k:16 * k + 16, :], T.x1t[0:128:32, :])
-    ts("ict2 iw2", "late", f(10), part, 16.0 * r + 15, A.is_gt, iw2[:, 9:10], A.mult)
-    ts("ict", "dg", cl[:, 14:15], ict[:, 64:65], 0.125, A.mult, 47.0, A.min)
-    turn("iwf0 iwf", "iw0", iw[:, 64:96], iw[:, 32:64])
-    pick("q0", "s0", "stq", "sts", T.stq[:], T.sts[:], T.q0[:], T.s0[:], T.stu[:, 0:13], "stu stz")
-    dma("y", "dq1", "q0", "q1x", T.q1[:, 0:A1].bitcast(dt.uint8), T.q0[:].bitcast(dt.uint8))
+        dma("ys"[k > 4], "dc1", "w1", "p1off", T.s1off[16 * k:16 * k + 16, :], T.w1[0:128:32, :])
+    dma("y", "dq1", "q0 nc2", "q1x", u8(T.q1[:, 0:A1]), u8(T.q0[:]))
     dma("y", "dq1", "s0", "q1x", T.s1[:, 0:A1], T.s0[:])
-    for k in (1, 0):
-        dma("y", "dw%d" % k, "", "wt%d" % k, T.wt[:, 1536 * k:1536 * k + 1536], T.w[:, 1536 * k:1536 * k + 1536])
-    affine("m9", "m9n", f(19), f(4), scale=-LOW)
-    affine("ioL0 ioL m9 stu", "ci", T.ci[:, 64:64 + V], ioL[:].indirect(T.stu[:, 0:12]), scale=f(4))
-    affine("iw0 m9n", "iw", iw[:, 0:32], iw[:, 64:96], bias=f(19))
-    affine("ioL0", "ci", T.ci[:, 0:64], ioL[:, 0:64], scale=0.0)
-    affine("late ict2", "first", f(16), f(10), scale=-32.0, bias=ict[:, 160:161])
-    affine("iw2", "nb", f(5), iw2[:, r + 1:r + 2], scale=-BIG, bias=BIG)
-    affine("ioL0 ioL", "tab2", T.tab2[:], ioL[:, 0:RB + 272], scale=0.0)
+    copy("land1 m1", "zf", T.zf[:], T.land1[:])
+    copy("na0 na1 nb0 nb1", "nc", nxa[64:128, 0:512:2], nxa[0:64, 0:512:2])
+    dma("y", "dw1", "", "wt1", T.wt[:, 1536:3072], T.w[:, 1536:3072])
 
-    m2, tot, px, mi, vt = T.m2, T.tot, T.px, T.mi, T.vt
-    cba, bc, pa, cbb = (T.kk[:, 12 * k:12 * k + 12] for k in range(4))
-    for a, b in ((0, 6 * r), (6 * r + 6, 6 * N)):
-        if b > a:
-            copy("land1", "zf", T.zf[:, a:b], T.land1[:, a:b])
-    ts("ic ict", "mk", T.mk[:], ic[:, 96:128], q15, A.is_equal)
-    ts("aq", "valid", f(6), f(9), 4.0, A.is_lt)
-    ts("zf zfo dg", "off2", T.off2[:], T.zf[:].indirect(cl[:, 14:15]), 8.0 - 1024 * r, A.add, 1032.0, A.min)
-    ts("zf zfo dg", "mi", mi[:], T.zf[:].indirect(cl[:, 14:15]), 1.0 / 1024, A.mult, -0.4995, A.add)
-    ts("aq even", "valid", f(7), f(9), 4.0, A.is_lt, f(2), A.mult)
-    copy("nxl nxe off2", "n2r", T.n2r[:], T.nxl[:].indirect(T.off2[:, 0:12]))
-    ts("mi", "cba", cba, mi[:, 0:12], 64.0, A.mult, float(31 - CAP * r), A.add)
-    ts("ioL0 ict2", "la", cl[:, 16:18], ioL[:, 0:129:128], ict[:, 192:193], A.add)
+    tot, px, vt, kk = T.tot, T.px, T.vt, T.kk
+    n2c, dk, dm, n1c = (kk[:, 16 * k:16 * k + 12] for k in range(4))
+    copy("zf dg", "ek", T.ek[:], T.zf[:].indirect(cl[:, 2:3]))
+    ts("zf dg", "hi", T.hi[:], T.zf[:].indirect(cl[:, 14:15]), 1.0 / 16, A.mult, -0.469, A.add)
+    act("nb0 nb1 nb2 nb3 nc nc2 hi", "n2r", T.n2r[:], nxa[:].indirect(T.hi[:, 0:12]))
+    act("s0 stu stz", "sts", T.sts[:], T.s0[:].indirect(T.stu[:, 0:13]))
+    fill("pxc", T.px[:], 0.0)
+    ts("ek", "lo", T.lo[:], T.ek[:], 15, A.bitwise_and)
+    turn("ic2", "ict2", ict[:, 192:320], ic[:, 192:320])
+    tt("lo xl iq", "nm", T.nm[:], T.lo[:].indirect(cl[:, 16:28]), T.iq[:], A.is_lt)
     turn("n2r", "n2t", T.n2t[:], T.n2r[:])
-    turn("ic3", "ict3", ict[:, 256:320], ic[:, 256:320])
-    ts("n2t", "xo", T.xo[:], T.n2t[:, 0:V:16], 1.0 / TN, A.mult, 0.501, A.add)
-    ts("w1", "p1off", T.s1off[:], T.w1[:], -0.5, A.mult, V / 2.0, A.add)
-    ts("n2t", "m2a", T.ab[:, 0:12], T.n2t[:, 0:V:16], -512.0, A.mult, 512.0 * N * TN, A.add)
-    act("iw xo", "tot fl", T.fl[:, 64:64 + V], iw[:, 0:32].indirect(T.xo[:]), F.Identity, accum_out=tot[:, 0:1])
-    affine("fl nb", "fb", T.fb[:], T.fl[:, 64:64 + V], scale=f(5))
+    copy("q0 stu stz", "stq", T.stq[:].bitcast(dt.uint32), T.q0[:].bitcast(dt.uint32).indirect(T.stu[:, 0:13]))
+    scan("nm n2t", "sel", T.sel[:], T.nm[:], T.n2t[:], 0.0, A.mult, A.max)
+    op("v", "iw1", "mk mkz", lambda e: e.memset(mk[:, 0:32:16], 0.0))
+    ts("sel", "xo", T.xo[:], T.sel[:, 15:V:16], 1.0 / TN, A.mult, -0.499, A.add)
+    act("sts p1off", "p1s", T.p1s[:], T.sts[:].indirect(T.s1off[:]))
+    act("iw1024 xo", "tot fl", T.fl[:, 64:64 + V], iw[:].indirect(T.xo[:]), F.Identity, accum_out=tot[:, 0:1])
+    affine("fl", "fb", T.fb[:], T.fl[:, 64:64 + V], scale=MARK)
+    act("zf dg", "n1c", kk[:, 48:64], T.zf[:].indirect(cl[:, 2:3]), F.Relu, scale=-0.5, bias=600.25 - XB + TN * r)
+    copy("stq p1off", "p1q", T.p1q[:].bitcast(dt.uint32), T.stq[:].bitcast(dt.uint32).indirect(T.s1off[:]))
+    at1 = lambda c: A1 + CAP * _among(T, c, core)
+    to1 = lambda buf, c: buf[:, CAP * T.rank_of(c):CAP * T.rank_of(c) + CAP]
+    send(1, 0, "s", "p1s", lambda c: to1(T.p1s, c), lambda c: T.s1[:, at1(c):at1(c) + CAP], T.hs1[:])
+    send(1, 0, "q", "p1q", lambda c: u8(to1(T.p1q, c)), lambda c: u8(T.q1[:, at1(c):at1(c) + CAP]), u8(T.hq1[:]))
+    affine("ioL ict2", "x3", x3[:, 3:V:16], ioL[:, 1:V:16], bias=ict[:, 288:289])
+    affine("n1c", "x3", x3[:, 0:V:16], n1c, scale=-1.0, bias=600.0)
+    affine("iw1024", "tab", T.tab[:, S0 - 16:P0 + M + 16], iw[:, 0:NS + M + 32], scale=0.0)
     for k in range(2):
-        leave(1, k, CAP, "stq", "sts", T.p1q, T.p1s, T.stq[:], T.sts[:], T.s1off, T.q1, T.s1, lambda d: A1 + CAP * (r - (r > d)))
-    affine("ioL0 ioL", "tab3", T.tab3[:], ioL[:, 0:RB + M + 16], scale=0.0)
+        affine("ioL bel wb2", "wa2", T.wa[:, U1 + NS * k:U1 + NS * k + NS], ioL[:, 0:NS], scale=below(2), bias=f(12 + k))
     ts("tot", "u2", tot[64:96, 1:2], tot[0:32, 0:1], tot[32:64, 0:1], A.add)
     ts("tot", "u3", tot[96:128, 1:2], tot[0:32, 0:1], tot[32:64, 0:1], A.add, tot[64:96, 0:1], A.add)
-    ts("mk tot valid", "pxa", px[32:64, 0:32], T.mk[0:32, :], tot[0:32, 0:1], A.mult, cf[0:32, 6:7], A.mult)
-    ts("iw2 tot valid", "pxb", px[:, 48:64], iw2[:, 0:16], tot[:, 0:1], A.mult, f(7), A.mult)
-    ts("mk u2 u3 valid", "pxa", px[64:128, 0:32], T.mk[64:128, :], tot[64:128, 1:2], A.mult, cf[64:128, 6:7], A.mult)
-    turn("fb", "fbt", T.fbt[:], T.fb[:])
+    ts("mkz tot pxc", "pxa", px[32:64, 0:32], mk[0:32, :], tot[0:32, 0:1], A.mult)
+    ts("mkz tot pxc", "pxb", px[:, 48:64], mk[:, 0:16], tot[:, 0:1], A.mult, even, A.mult)
+    ts("mkz u2 u3", "pxa", px[64:128, 0:32], mk[64:128, :], tot[64:128, 1:2], A.mult)
+    ts("xo", "n2c", n2c, T.xo[:], -float(TN), A.mult, float(XB), A.add)
     turn("pxa pxb pxc", "pxt", T.fl[:, 0:64], px[:])
-    ts("ioL0 ioL ict3", "le", cl[:, 18:23], ioL[:, 0:257:64], ict[:, 256:257], A.add, 590.0, A.min)
-    tt("cba fbt", "cbb", cbb, cba, T.fbt[:, 11:V:16], A.subtract)
-    scan("fl pxt ci first", "cnt", T.cnt[:], T.fl[:], T.ci[:], f(16), A.add, A.max)
+    tt("n2c sel", "x3v", x3[:, 2:V:16], n2c, T.sel[:, 15:V:16], A.add)
+    scan("fl pxt first", "cnt", T.cnt[:], T.fl[:], T.fl[:], f(28), A.add, A.max)
+    turn("x3 x3v", "x3t", T.x3t[:], x3[:])
     turn("cnt", "vt", vt[:], T.cnt[:, 64:64 + V])
-    copy("cnt", "m2c", m2[:, 12:13], T.cnt[:, 63:64])
-    copy("vt", "c0u", T.c0u[:], vt[:, 9:V:16])
+    turn("fb", "fbt", T.fbt[:], T.fb[:])
+    dma("y", "dw0", "cnt", "wt0", T.wt[:, 0:1536], T.w[:, 0:1536])
+    dma("y", "dq2", "q0", "q2x", u8(T.q2[:, 0:A1]), u8(T.q0[:]))
+    dma("y", "dq2", "s0", "q2x", T.s2[:, 0:A1], T.s0[:])
+    ts("vt ict2", "c0u", T.c0u[:], vt[:, 0:V:16], 1.0 / 256, A.mult, ict[:, 192:193], A.add)
     scan("fbt vt", "seg", T.seg[:], T.fbt[:], vt[:], 0.0, A.max, A.min)
-    tt("wa c0u n2r", "vals", T.vals[:], T.wa[:].indirect(T.c0u[:]), T.n2r[:], A.max)
-    act("seg", "m2b", T.ab[:, 12:24], T.seg[:, 8:V:16], F.Relu, bias=1.0 - RB)
-    copy("seg", "so", T.so[:], T.seg[:, 8:V:16])
-    tt("m2a m2b", "m2", m2[:, 0:12], T.ab[:, 0:12], T.ab[:, 12:24], A.add)
-    spread("m2 m2c", "al2", "land2", m2[:, 0:ML], lambda d: T.land2[:, ML * (r - (r > d)):ML * (r - (r > d)) + ML], "sent2")
-    dma("y", "dq2", "q1x q1a sent2", "q2o", T.q2[:, 0:A2].bitcast(dt.uint8), T.q1[:].bitcast(dt.uint8))
-    dma("y", "dq2", "s1a", "q2o", T.s2[:, 0:A2], T.s1[:])
-    op("v", "vals so tab2", "tab2s", lambda e: e.tensor_copy(T.tab2[:].indirect(T.so[:]), T.vals[:]))
+    tt("wa c0u x3t", "vals", T.vals[:], T.wa[:, 0:U1].indirect(T.c0u[:]), T.x3t[:], A.max)
+    copy("seg", "so", T.so[:], T.seg[:, 14:V:16])
+    ts("seg", "bcu", T.bcu[:], T.seg[:, 7:V:16], -float(KC), A.add)
+    copy("seg", "po", T.po[:], T.seg[:, 15:V:16])
+    op("v", "vals so tab", "tab2", lambda e: e.tensor_copy(T.tab[:].indirect(T.so[:]), T.vals[:]))
+    ts("ioL ict2", "la", cl[:, 30:32], ioL[:, 0:129:128], ict[:, 224:225], A.add, 2.0 * NS + 15, A.min)
+    ts("ioL ict2", "le", cl[:, 32:37], ioL[:, 0:257:64], ict[:, 256:257], A.add, 2.0 * M + 15, A.min)
+    dma("y", "dq3", "q1a", "q2o", u8(T.q2[:, A1:A2]), u8(T.q1[:, A1:A2]))
+    dma("y", "dq3", "s1a", "q2o", T.s2[:, A1:A2], T.s1[:, A1:A2])
 
-    def collect(tag, tab, y, n, lst, gg, rr, w, between):
-        turn("tab%ss" % tag, "ya" + tag, y[:, 0:n], tab[:, RB:RB + n])
-        turn("tab%ss" % tag, "yb" + tag, y[:, n:2 * n + 32], tab[:, RB - 16:RB + n + 16])
-        ys, u = "ya%s yb%s l%s" % (tag, tag, "a" if tag == "2" else "e"), min(w, n // 4)
+    def collect(tag, at, y, n, lst, gg, rr, w, u, between):
+        turn("tab" + tag, "ya" + tag, y[:, 0:n], T.tab[:, at:at + n])
+        turn("tab" + tag, "yb" + tag, y[:, n:2 * n + 32], T.tab[:, at - 16:at + n + 16])
+        ys = "ya%s yb%s l%s" % (tag, tag, "a" if tag == "2" else "e")
         between(0)
         copy(ys, "ga" + tag, gg[:, 0:w], y[:, 0:2 * n + 16].indirect(lst))
         between(1)
@@ -411,75 +451,41 @@ def rank_program(g, core, T, topo):
         tt("gb" + tag, "ra" + tag, rr[0:64, 0:u], gg[0:64, w:w + u], gg[64:128, w:w + u], A.add)
         tt("ra" + tag, "rb" + tag, rr[0:32, w:w + u], rr[0:32, 0:u], rr[32:64, 0:u], A.add)
 
-    lift = N * (RB - 1 + CAP * r) - (RB - 1)
-    affine("iw2", "al", f(11), iw2[:, 10:11], scale=-LOW)
-    affine("iw2", "al", f(12), iw2[:, 10:11], scale=LOW + BIG, bias=1.0)
-    affine("ict", "db", f(15), odd, scale=16.0, bias=1.0 + lift)
-    act("ioL0", "oh", ie[:, 16:32], ioL[:, 0:16], F.Abs, bias=-float(r))
-    act("ict", "w12", f(13), q15, F.Abs, bias=-1.5)
-    act("oh", "oh2", ie[:, 32:48], ie[:, 16:32], F.Relu, scale=-1.0, bias=1.0)
-    act("w12", "w12s", f(14), f(13), F.Relu, scale=-2.0, bias=2.0)
-    affine("iw2", "w12a", f(17), iw2[:, 1:2], scale=-32.0, bias=float(A2))
-    affine("ioL0 db", "de", T.de[:], ioL[:, 0:V], bias=f(15))
-    affine("w12s w12a", "w12b", f(18), f(14), scale=f(17))
-    affine("oh2 al", "ie", ie[:, 0:16], ie[:, 32:48], scale=f(12), bias=f(11))
-    affine("ioL0", "wb", T.wb[:, 0:8], ioL[:, 0:8], scale=0.0)
-    affine("ioL0 ioL w12s w12b", "wb", T.wb[:, 8:768], ioL[:, 8:768], scale=f(14), bias=f(18))
-    turn("vals", "x3z", T.x3[:], T.vals[:])
-    affine("ioL0 ict3 x3z", "x3", T.x3[:, 4:V:16], ioL[:, 0:V:16], bias=ict[:, 288:289])
-    collect("2", T.tab2, T.y2, 256, cl[:, 16:18], T.g2, T.r2, 32, lambda k: None)
+    collect("2", S0, T.y2, NS, cl[:, 30:32], T.g2, T.r2, 32, 28, lambda k: quant_w(5 - k))
     for k in range(4):
-        ts("rb2", "p2off", T.p2off[32 * k:32 * k + 32, :], T.r2[0:32, 32:64], float(XB), A.max)
-    for k in range(2):
-        leave(2, k, 2 * CAP, "q1x q1a", "q1x s1a", T.p2q, T.p2s, T.q1[:], T.s1[:], T.p2off, T.q2, T.s2, lambda d: A2 + 2 * CAP * r)
+        copy("rb2", "p2off", T.p2off[32 * k:32 * k + 32, :], T.r2[0:32, 32:60])
+    n = 2 * CAP
+    at2 = lambda c: A2 + n * _among(T, c, core)
+    blk = lambda buf, c: buf[:, n * _among(T, core, c):n * _among(T, core, c) + n]
+    for k, (cores, free) in enumerate(_parts(core, others, topo)):
+        a, b = n * _among(T, core, cores[0]), n * _among(T, core, cores[-1]) + n
+        pick("q1x q1a", "q1x s1a", "pq%d" % k, "pz%d" % k, T.p2q[:, a:b], T.p2s[:, a:b], T.q1[:], T.s1[:], T.p2off[:, a // 16:b // 16], "p2off")
+        send(2, k, "q", "pq%d" % k, lambda c: u8(blk(T.p2q, c)), lambda c: u8(T.q2[:, at2(c):at2(c) + n]), u8(T.hq2[:]))
+        send(2, k, "s", "pz%d" % k, lambda c: blk(T.p2s, c), lambda c: T.s2[:, at2(c):at2(c) + n], T.hs2[:])
 
-    zz, zi, l2 = T.zz, T.zi, T.land2
-    tt("land2", "za", zz[:, 0:39], l2[:, 0:39], l2[:, 39:78], A.add)
-    tt("land2 m2 m2c", "za", zz[:, 39:52], l2[:, 78:91], m2[:, 0:ML], A.add)
-    quant_w(5)
-    tt("za", "zb", zz[:, 52:78], zz[:, 0:26], zz[:, 26:52], A.add)
-    quant_w(4)
-    tt("zb", "zc", zz[:, 78:91], zz[:, 52:65], zz[:, 65:78], A.add)
-    quant_w(3)
-    an = zz[:, 78:90]
-    ts("zc", "xe", T.xe[:], an, -1.0 / (512 * TN), A.mult, N - 0.5 + 0.6 / TN, A.add)
-    act("ie xe", "fe", T.fe[:], ie[:, 0:16].indirect(T.xe[:]))
-    copy("zc", "zi", zi[:, 0:12], an)
-    ts("zc x3z", "x3", T.x3[:, 3:V:16], an, -1.0 / 512, A.mult, LIFT + XB + TN * (N - r) + 0.25, A.add)
-    ts("zi", "zj", zi[:, 12:24], zi[:, 0:12], 511, A.bitwise_and)
-    turn("x3", "x3t", T.x3t[:], T.x3[:])
-    tt("zj cbb", "bc", bc, zi[:, 12:24], cbb, A.add)
-    scan("fe de zc", "pe", T.pe[:], T.fe[:], T.de[:], zz[:, 90:91], A.add, A.max)
-    copy("bc", "bcu", T.bcu[:], bc)
-    turn("pe", "pt", T.pt[:], T.pe[:])
-    tt("wb bcu x3t", "v4", T.v4[:], T.wb[:].indirect(T.bcu[:]), T.x3t[:], A.max)
-    tt("pt", "pa", pa, T.pt[:, r + 1:V:16], T.pt[:, 10:V:16], A.min)
-    ts("pa", "po", T.po[:], pa, -float(lift), A.add)
-    op("v", "v4 po tab3", "tab3s", lambda e: e.tensor_copy(T.tab3[:].indirect(T.po[:]), T.v4[:]))
-    collect("3", T.tab3, T.y3, M, cl[:, 18:23], T.g3, T.r3, 80, lambda k: quant_w(2 - k))
-    for k in range(3):
-        ts("rb3", "fo0", T.fo[0:32, 18 * k:18 * k + 18], T.r3[0:32, (81, 80, 82)[k]:152:4], -float(LIFT * (k == 2)), A.add)
+    tt("wa wa2 bcu vals", "v4", T.v4[:], T.wa[:].indirect(T.bcu[:]), T.vals[:], A.max)
+    op("v", "v4 po tab2", "tab3", lambda e: e.tensor_copy(T.tab[:].indirect(T.po[:]), T.v4[:]))
+    collect("3", P0, T.y3, M, cl[:, 32:37], T.g3, T.r3, 80, 72, lambda k: quant_w(2 - k))
+    halves = ((0, HALF), (HALF, M))
+    where = {(2, 0): 0, (1, 0): M, (0, 0): M + HALF, (1, HALF): M + 2 * HALF, (0, HALF): 2 * M + HALF}
+    ts("rb3", "fo2", T.fo[0:32, 0:18], T.r3[0:32, 82:152:4], 0.0, A.add)
+    for a, b in halves:
+        for k in (1, 0):
+            c = where[k, a] // 16
+            ts("rb3", "fo0", T.fo[0:32, c:c + (b - a) // 16], T.r3[0:32, 81 - k + a // 4:80 + b // 4:4], 0.0, A.add)
     ki = T.ki
-    ts("rb3", "k0", ki[0:32, 0:18], T.r3[0:32, 83:152:4], -float(LIFT), A.add, 0.0, A.max)
+    copy("rb3", "k0", ki[0:32, 0:18], T.r3[0:32, 83:152:4])
     for k in range(1, 4):
-        copy("fo0", "fo", T.fo[32 * k:32 * k + 32, :], T.fo[0:32, :])
-    ts("k0", "k1", ki[0:32, 18:36], ki[0:32, 0:18], 8, A.arith_shift_right)
-    ts("k0", "k2", ki[0:32, 36:54], ki[0:32, 0:18], 255, A.bitwise_and)
+        copy("fo0 fo2", "fo", T.fo[32 * k:32 * k + 32, :], T.fo[0:32, :])
 
-    halves = ((0, 160), (160, M))
-
-    def products(k, parts):
-        a, b = parts[0][0], parts[-1][1]
-        src = ("q0", "s0", T.q0[:], T.s0[:]) if k == 2 else ("q2o q2a", "q2o s2a", T.q2[:], T.s2[:])
-        key = "%d_%d" % (k, a)
-        pick(src[0], src[1], "fq" + key, "fs" + key, T.fq[:, M * k + a:M * k + b], T.fs[:, M * k + a:M * k + b], src[2], src[3],
-             T.fo[:, 18 * k + a // 16:18 * k + b // 16], "fo0 fo")
-        for a, b in parts:
-            for o in range(2):
+    def products(steps, key, a, b):
+        for o in range(2):
+            for k in steps:
+                at = where[k, a * (k < 2)] + a * (k == 2)
                 c, bank = 128 * (2 * k + o), 512 * (2 * (a > 0) + o)
                 op("t", "fq%s fs%s wq%d" % (key, key, c // 128), "ps%d" % bank, lambda e: e.matmul_mx(
-                    T.ps[:, bank:bank + b - a], T.wq[:, c:c + 128], T.ws[:, c:c + 128], T.fq[:, M * k + a:M * k + b],
-                    T.fs[:, M * k + a:M * k + b], k == 2, k == 0))
+                    T.ps[:, bank:bank + b - a], T.wq[:, c:c + 128], T.ws[:, c:c + 128], T.fq[:, at:at + b - a],
+                    T.fs[:, at:at + b - a], k == 2, k == 0))
 
     def store(a, b):
         bank = 1024 * (a > 0)
@@ -488,15 +494,20 @@ def rank_program(g, core, T, topo):
         act("ps%d" % (bank + 512), "yo1%d" % a, T.yo1[:, a:b], T.ps[:, bank + 512:bank + 512 + b - a])
         dma("y", "dy%d" % (2 * (a > 0) + 1), "yo1%d" % a, "y1%d" % a, T.y[:, M + a:M + b], T.yo1[:, a:b])
 
-    products(2, halves)
-    for half in halves:
-        products(1, [half])
-        products(0, [half])
-    for k in range(2):
-        ts("k1 k2", "x5", T.x5[0:32, 32 * k:32 * k + 18], ki[0:32, 18 + 18 * k:36 + 18 * k], -1.0, A.add)
+    pick("q0", "s0", "fqn", "fsn", T.fq[:, 0:M], T.fs[:, 0:M], T.q0[:], T.s0[:], T.fo[:, 0:18], "fo2 fo")
+    for a, b in halves:
+        products([2], "n", a, b)
+    for a, b in halves:
+        c, e = where[1, a], where[1, a] + 2 * (b - a)
+        pick("q2x q2o q2a", "q2x q2o s2a", "fq%d" % a, "fs%d" % a, T.fq[:, c:e], T.fs[:, c:e], T.q2[:], T.s2[:], T.fo[:, c // 16:e // 16], "fo0 fo")
+        products([1, 0], str(a), a, b)
+    ts("k0", "k1", ki[0:32, 18:36], ki[0:32, 0:18], 8, A.arith_shift_right)
+    ts("k0", "k2", ki[0:32, 36:54], ki[0:32, 0:18], 255, A.bitwise_and)
     store(*halves[0])
-    turn("x5", "x5t", T.x5t[0:32, :], T.x5[0:32, :])
+    for k in range(2):
+        ts("k1 k2", "x5", x5[:, 32 * k:32 * k + 18], ki[0:32, 18 + 18 * k:36 + 18 * k], -1.0, A.add)
     store(*halves[1])
+    turn("x5", "x5t", T.x5t[0:32, :], x5)
     for k in range(2):
         dma("s", "did", "x5t", "id%d" % k, T["id"][k:k + 1, :], T.x5t[0:18, 32 * k:32 * k + 16])
     await_("g", [(s, None) for s in total])

from concourse.bass import DstId, RemoteDMATransfer
from concourse.mybir import dt, AluOpType as A, ActivationFunctionType as F

N = 8
TN, V, M, CAP = 512, 192, 288, 32
XB, A1, A2, QW = 16, 528, 752, 1200
NS = (N - 1) * CAP
U0, U1 = A1 - 16, 272
KC = 16768
S0 = KC + U1 + 2 * NS
P0 = S0 + NS
CORES = 64
HANDED = {"s1": 2, "q2": 2, "s2": 2}
HELP = 2
ACROSS = 1
HALF = 160
BIG = 8192.0
MARK = 32768.0
ROW = 32768.0
PART = (0, 2, 1, 3)
X4 = "float8_e4m3fn_x4"


def _sb(n, d="float32"):
    return ("sbuf", [128, n], d)


SCRATCH = {
    "stw": _sb(12, "int32"), "btw": _sb(12, "int32"), "nxrow": _sb(512, "int32"), "nxw": _sb(64, "int32"),
    "landn": _sb(128, "uint16"), "nxa": _sb(512), "xt": _sb(4 * A1, "bfloat16"), "wt": _sb(3072, "bfloat16"),
    "ic": _sb(320), "ict": _sb(320), "cf": _sb(48), "ioL": _sb(264), "wa": _sb(U1 + 2 * NS), "cl": _sb(48, "uint16"),
    "w8": _sb(N), "iq": _sb(V), "iw": _sb(1024), "iwe": _sb(64), "mk": _sb(32),
    "o1": _sb(32, "int32"), "off1": _sb(16, "uint16"), "stu": _sb(14, "uint16"), "b1s": _sb(64),
    "n1r": _sb(V), "n1t": _sb(V), "jf": _sb(36), "land1": _sb(128, "uint16"), "di": _sb(12, "uint16"),
    "f1t": _sb(V, "bfloat16"), "c1L": _sb(V, "bfloat16"), "sg": _sb(2 * V, "bfloat16"),
    "x1t": _sb(64), "w1": _sb(64, "uint16"), "s1off": _sb(16, "uint16"),
    "zf": _sb(128), "hi": _sb(16, "uint16"), "ek": _sb(16, "int32"), "lo": _sb(16, "int32"), "nm": _sb(V),
    "n2r": _sb(V), "n2t": _sb(V), "sel": _sb(V), "xo": _sb(12, "uint16"), "kk": _sb(96),
    "fl": _sb(64 + V), "tot": _sb(2), "px": _sb(64), "cnt": _sb(64 + V), "fb": _sb(V, "bfloat16"), "fbt": _sb(V, "bfloat16"),
    "vt": _sb(V), "seg": _sb(V), "c0u": _sb(12, "uint16"), "vals": _sb(V), "so": _sb(12, "uint16"),
    "tab": _sb(P0 + M + 16), "y2": _sb(2 * NS + 32), "g2": _sb(64), "r2": _sb(64), "p2off": _sb(28, "uint16"),
    "po": _sb(12, "uint16"), "bcu": _sb(12, "uint16"), "x3t": _sb(V), "v4": _sb(V),
    "y3": _sb(608), "g3": _sb(160), "r3": _sb(160), "fo": _sb(54, "uint16"), "ki": _sb(64, "int32"), "x5t": _sb(64),
    "q0": _sb(A1, X4), "s0": _sb(A1, "uint8"), "wq": _sb(768, X4), "ws": _sb(768, "uint8"),
    "stq": _sb(V + 16, X4), "sts": _sb(V + 16, "uint8"), "p1q": _sb(256, X4), "p1s": _sb(256, "uint8"),
    "q1": _sb(A2, X4), "s1": _sb(A2, "uint8"), "p2q": _sb(2 * NS, X4), "p2s": _sb(2 * NS, "uint8"),
    "q2": _sb(QW, X4), "s2": _sb(QW, "uint8"), "fq": _sb(3 * M, X4), "fs": _sb(3 * M, "uint8"),
    "hq1": _sb(CAP, X4), "hs1": _sb(CAP, "uint8"), "hq2": _sb(2 * CAP, X4), "hs2": _sb(2 * CAP, "uint8"),
    "yo0": _sb(M), "yo1": _sb(M), "ps": ("psum", [128, 2048], "float32"),
}
SEMAPHORES = ["cv", "cs_", "ct", "cg", "dst", "ds2", "dbt", "dnx", "dnw", "dx0", "dx1", "dw0", "dw1", "dc1", "dq1", "dq2", "dq3", "dy0", "dy1",
              "dy2", "dy3", "did", "sent", "an", "al1", "aq1", "as1", "aq2", "as2", "hq1", "hs1", "hq2", "hs2"]


def _parts(core, others, topo):
    own = topo.cores_of(core)
    far = [c for c in others if c not in own]
    near = [c for c in others if c in own]
    out, taken = [], []
    for part in (far, near):
        free = [e for e in topo.engines(core, part[0]) if e not in taken]
        out.append((part, free))
        taken += free
    return out


def _mask(engines):
    return sum(1 << e for e in engines)


def _helpers(T, topo):
    out, taken = {}, list(T.cores)
    for c in T.cores:
        own = [b for b in T.cores if b in topo.cores_of(c)]
        far = [b for b in T.cores if b not in own]
        d = far[own.index(c)]
        beside = [b for b in topo.cores_of(c) if topo.die(b) != topo.die(c)]
        beyond = [b for b in range(CORES) if topo.mates(topo.chip(b), topo.chip(d)) and topo.may_write(c, b) and topo.may_write(b, d)]
        if not beyond and own.index(c) < ACROSS:
            beyond = [b for b in range(CORES) if topo.die(b) != topo.die(c) and all(topo.same_plane(topo.chip(b), topo.chip(a)) for a in (c, d))]
        out[c] = []
        for to, free in [(d, beside)] + [(far[own.index(c) - j], beyond) for j in range(1, HELP)]:
            free = [b for b in free if b not in taken]
            if free:
                out[c].append((to, free[0]))
                taken.append(free[0])
    return out


def _calls(c, move, T, topo):
    (far, ef), (near, en) = _parts(c, [b for b in T.cores if b != c], topo)
    q = len(ef) // 4
    three = lambda e: (e[:2 * q], e[2 * q:3 * q], e[3 * q:])
    if move not in HANDED:
        return [[(d, ef[q * j:q * j + q], None) for j, d in enumerate(far)] + [(d, e, None) for d, e in zip(near, three(en))]]
    (d0, h0), *more = _helpers(T, topo)[c][:HANDED[move]]
    if move == "s2":
        more = [(d, h) for d, h in more if topo.mates(topo.chip(d), topo.chip(h))]
    ways = more + [(d, None) for d in far if d != d0 and d not in dict(more)]
    if move[1] == "1":
        pairs = [(ef + en[2 * q:])[q * j:q * j + q] for j in range(6)]
        return [[(d0, en[:2 * q], h0)] + [(d, e, h) for (d, h), e in zip(ways + [(d, None) for d in near], pairs)]]
    return [[(d0, en, h0)] + [(d, e, h) for (d, h), e in zip(ways, three(ef))], [(d, e, None) for d, e in zip(near, three(en))]]


def _among(T, c, b):
    return [a for a in T.cores if a != c].index(b)


def hand_on(g, core, T, topo):
    u8 = lambda ap: ap.bitcast(dt.uint8)
    for c, ways in _helpers(T, topo).items():
        for d in [d for d, h in ways if h == core]:
            a, b = A1 + CAP * _among(T, d, c), A2 + 2 * CAP * _among(T, d, c)
            rid, pid = topo.addr(d)[:2]
            sides = {"s1": (T.hs1[:], T.s1[:, a:a + CAP]), "q1": (u8(T.hq1[:]), u8(T.q1[:, a:a + CAP])),
                     "q2": (u8(T.hq2[:]), u8(T.q2[:, b:b + 2 * CAP])), "s2": (T.hs2[:], T.s2[:, b:b + 2 * CAP])}
            moves = [(move, len(e)) for move in HANDED for to, e, h in _calls(c, move, T, topo)[0] if h == core]
            for move, n in moves:
                g.wait_ge(T.sem["h" + move], n)
                g.remote_dma(sides[move][1], sides[move][0], T.sem["a" + move], T.sem.sent, pid, rid, topo.mask(core, d))
            g.wait_ge(T.sem.sent, len(moves) * len(topo.engines(core, d)))


def rank_program(g, core, T, topo):
    r = T.rank_of(core)
    if r is None:
        return hand_on(g, core, T, topo)
    sem = T.sem
    queues = {"v": (g.vector, "cv"), "s": (g.scalar, "cs_"), "t": (g.tensor, "ct"), "g": (g, "cg"), "y": (g.sync, None)}
    total, seen = {}, {q: {} for q in queues}
    wrote, read = {}, {}

    def await_(q, toks):
        eng, need = queues[q][0], {}
        for s, val in toks:
            val = total[s] if val is None else val
            need[s] = max(need.get(s, 0), val)
        for s in need:
            if seen[q].get(s, 0) < need[s]:
                eng.wait_ge(sem[s], need[s])
                seen[q][s] = need[s]

    def deps(q, r_, w_, own=None):
        mine = (queues[q][1], own)
        toks = []
        for k in r_:
            toks += wrote[k]
        for k in w_:
            toks += [t for t in wrote.get(k, []) + read.get(k, []) if t[0] not in mine]
        await_(q, toks)

    def note(tok, r_, w_):
        for k in r_:
            read.setdefault(k, []).append(tok)
        for k in w_:
            wrote.setdefault(k, []).append(tok)

    def op(q, r_, w_, fn):
        r_, w_ = r_.split(), w_.split()
        deps(q, r_, w_)
        s = queues[q][1]
        total[s] = total.get(s, 0) + 1
        fn(queues[q][0]).then_inc(sem[s], 1)
        note((s, total[s]), r_, w_)

    def dma(q, s, r_, w_, out, in_):
        r_, w_ = r_.split(), w_.split()
        deps(q, r_, w_, s)
        total[s] = total.get(s, 0) + 16
        queues[q][0].dma_start(out, in_).then_inc(sem[s], 16)
        note((s, None), r_, w_)

    def copy(r_, w_, out, in_):
        op("v", r_, w_, lambda e: e.tensor_copy(out, in_))

    def act(r_, w_, out, in_, fn=F.Copy, **k):
        op("s", r_, w_, lambda e: e.activation(out, in_, fn, **k))

    def affine(r_, w_, out, in_, scale=1.0, bias=0.0):
        act(r_, w_, out, in_, F.Identity, scale=scale, bias=bias)

    def ts(r_, w_, out, in0, s1, o0, s2=None, o1=None):
        if o1 is None:
            op("v", r_, w_, lambda e: e.tensor_scalar(out, in0, s1, None, o0))
        else:
            op("v", r_, w_, lambda e: e.tensor_scalar(out, in0, s1, s2, o0, o1))

    def tt(r_, w_, out, a, b, o):
        op("v", r_, w_, lambda e: e.tensor_tensor(out, a, b, o))

    def fill(w_, ap, c):
        op("v", "", w_, lambda e: e.memset(ap, c))

    def turn(r_, w_, out, in_):
        op("v", r_, w_, lambda e: e.transpose(out, in_))

    def iota(w_, ap, pat, base, mult=0, after=""):
        op("g", after, w_, lambda e: e.iota(ap, pat, base, mult, allow_small_or_imprecise_dtypes=True))

    def scan(r_, w_, out, a, b, init, o0, o1):
        op("v", r_, w_, lambda e: e.tensor_tensor_scan(out, a, b, init, o0, o1))

    def quant(r_, w_, q, s, in_):
        op("v", r_, w_, lambda e: e.quantize_mx(q, s, in_))

    def quant_x(k):
        h = A1 // 4
        quant("xt xz", "q0 s0", T.q0[:, h * k:h * k + h], T.s0[:, h * k:h * k + h], T.xt[:, 4 * h * k:4 * h * k + 4 * h])

    def quant_w(k):
        quant("wt%d" % (k // 3), "wq%d" % k, T.wq[:, 128 * k:128 * k + 128], T.ws[:, 128 * k:128 * k + 128], T.wt[:, 512 * k:512 * k + 512])

    def pick(deps_q, deps_s, w_q, w_s, oq, os_, iq, is_, off, off_key):
        copy(deps_q + " " + off_key, w_q, oq.bitcast(dt.uint32), iq.bitcast(dt.uint32).indirect(off))
        act(deps_s + " " + off_key, w_s, os_, is_.indirect(off))

    others = [c for c in T.cores if c != core]
    rest = lambda c: [b for b in T.cores if b != c]
    place = lambda c: DstId(rid=topo.addr(c)[0], pnc=topo.addr(c)[1])
    u8 = lambda ap: ap.bitcast(dt.uint8)

    def send(move, k, kind, r_, src, dst, via=None):
        deps("g", r_.split(), [])
        move = kind + str(move)
        s, ways = "a" + move, _calls(core, move, T, topo)[k]
        g.remote_dma_fused([RemoteDMATransfer(dst_ids=[place(h or c)], dma_engine_mask=_mask(e),
                                              remote_sem=sem["h" + s[1:] if h else s], src=src(c), dst=via if h else dst(c))
                            for c, e, h in ways], local_sem=sem.sent)
        total["sent"] = total.get("sent", 0) + sum(len(e) for c, e, h in ways)
        total[s] = sum(len(topo.engines(h, core) if h else e)
                       for c in others for call in _calls(c, move, T, topo) for d, e, h in call if d == core)
        wrote[move + "a"] = [(s, None)]

    def spread(r_, s, w_, block):
        deps("g", r_.split(), [])
        ways = _calls(core, 0, T, topo)[0]
        g.remote_dma_fused([RemoteDMATransfer(dst_ids=[place(c)], dma_engine_mask=_mask(e), remote_sem=sem[s], src=block, dst=block)
                            for c, e, by in ways], local_sem=sem.sent)
        total["sent"] = total.get("sent", 0) + sum(len(e) for c, e, by in ways)
        total[s] = sum(len(e) for c in others for d, e, by in _calls(c, 0, T, topo)[0] if d == core)
        wrote[w_] = [(s, None)]

    fill("nxrow", T.nxrow[:], 0)
    for k in range(2):
        dma("sy"[k], "dnw", "", "nxw", T.nxw[16 * k:16 * k + 16, :], T.nx[:])
    for k in range(2):
        dma("s", "dst", "", "st01", T.stw[16 * k:16 * k + 16, :], T.st[:])
        dma("y", "dbt", "", "btw", T.btw[16 * k:16 * k + 16, :], T.bt[:])
    for k in range(4):
        dma("ys"[k % 2], "dnx", "", "nxrow", T.nxrow[16 * (k // 2) + k % 2:16 * (k // 2) + k % 2 + 1, :], T.nx[k % 2:16:2, :])
    for k in range(2, 8):
        dma("ys"[k % 2], "ds2", "", "stw", T.stw[16 * k:16 * k + 16, :], T.st[:])
    dma("y", "dx0", "", "xt", T.xt[:, 4 * XB:4 * A1], T.x[:])

    ic, ict, cf, cl, ioL, iw, mk = T.ic, T.ict, T.cf, T.cl, T.ioL, T.iw, T.mk
    iq = T.iq
    iota("ic", ic[:, 96:128], [[0, 2], [1, 16]], 0)
    iota("ic", ic[:, 128:160], [[-1, 2], [0, 16]], 1)
    iota("ic", ic[:, 160:192], [[1, 32]], 0, 1)
    iota("ic0", ic[:, 0:32], [[1, 2], [2, 8], [0, 2]], 0)
    iota("ic0", ic[:, 32:64], [[-8, 2], [0, 8], [-128, 2]], -4, -1)
    iota("ic0", ic[:, 64:96], [[1, 2], [2, 8], [16, 2]], 0, 1)
    iota("ioL0", ioL[:, 0:132], [[1, 132]], 0)
    iota("iq", iq[:], [[0, 12], [1, 16]], 0)
    mine1, minen = T.land1[:, 16 * r:16 * r + 16], T.landn[:, 16 * r:16 * r + 16]
    f = lambda j: cf[:, j:j + 1]
    q15, even, part = ict[:, 96:97], ict[:, 128:129], ict[:, 160:161]
    below = lambda j: cf[:, 32 + j:33 + j]
    x1, x3, x5 = ic[:, 128:192], T.n1r, ic[0:32, 0:64]
    fill("oz", T.o1[:, 16:32], 0)
    fill("m1z", mine1, 0)
    turn("ic", "ict", ict[:, 96:192], ic[:, 96:192])
    fill("xz", T.xt[:, 0:4 * XB], 0.0)
    fill("stz", T.stu[:, 12:14], 0)
    ts("ic ict", "bel", cf[:, 32:48], ic[:, 96:112], q15, A.is_gt)
    ts("ic ict", "mk", mk[:], ic[:, 96:128], q15, A.is_equal)
    ts("ict", "own", f(16), part, q15, A.subtract, 16.0 * r, A.is_equal)
    ts("ict bel", "q7", f(5), below(8), 7.0, A.mult, q15, A.add)

    is0, is1, is15 = below(1), mk[:, 1:2], mk[:, 15:16]
    first = KC + U1 - 1.0 - 2 * CAP
    ts("ict bel", "c01", f(14), part, 16.0 * r, A.not_equal, is0, A.mult)
    turn("ic0", "ic0t", ict[:, 0:96], ic[:, 0:96])
    ts("q7", "d1", f(15), f(5), r + 8.0, A.is_ge, f(5), A.add)
    ts("ict", "m8", f(26), q15, 8.0, A.min, q15, A.add)
    copy("ic0t", "pl dg", cl[:, 0:15:14], ict[:, 0:65:64])
    copy("ict", "dg", cl[:, 2:3], part)
    affine("ict", "lift", f(3), q15, scale=-ROW, bias=15 * ROW)
    affine("mk", "wb", f(10), is1, scale=float(U0))
    affine("mk", "wb", f(17), is1, scale=float(U0 + 16 + CAP * r))
    affine("own", "fc", f(22), f(16), scale=256.0, bias=167.0 + 256 * CAP - first)
    affine("mk", "w32", f(11), is1, scale=float(CAP))
    affine("d1", "t1", f(18), f(15), scale=7.0, bias=-56.0 - 7 * r)
    affine("c01", "c256", f(23), f(14), scale=256.0)
    affine("t1 d1 bel", "t2", f(20), f(18), scale=below(8), bias=f(15))
    affine("ioL0", "ioL", ioL[:, 132:264], ioL[:, 0:132], bias=132.0)
    affine("fc ict", "fe", f(30), even, scale=-16.0 - 256 * CAP, bias=f(22))
    affine("m8", "fd", f(29), f(26), scale=32.0, bias=first)
    a, b = 16 + CAP * r, 16 + CAP * r + CAP
    e = min(b, 264)
    affine("ioL mk wb", "wa0", T.wa[:, 0:e], ioL[:, 0:e], scale=is1, bias=f(10))
    affine("fd fe bel", "first", f(28), f(30), scale=is0, bias=f(29))
    affine("ioL mk wb", "wa0", T.wa[:, e:U1], ioL[:, 0:U1 - e], scale=is1, bias=f(17))
    for k in range(2):
        affine("bel w32", "wb2", f(12 + k), below(2), scale=float(A2 + NS * k), bias=f(11))

    def lay(k):
        ts("nxw", "minen", T.landn[32 * k:32 * k + 32, 16 * r:16 * r + 16], T.nxw[0:32, PART[k]:64:4], float(N * TN * r), A.add)

    o1, b1s, jf, bt = T.o1, T.b1s, T.jf, T.btw[0:32, :]
    ts("st01", "e2", o1[0:32, 0:12], T.stw[0:32, :], 513, A.mult)
    lay(0)
    lay(1)
    ts("e2 oz", "e3", o1[0:32, 16:28], o1[0:32, 0:12], 3, A.arith_shift_right, 511, A.bitwise_and)
    lay(2)
    lay(3)
    spread("minen", "an", "landn", minen)
    copy("e3 oz pl", "off1", T.off1[:], o1[:, 16:32].indirect(cl[:, 0:1]))
    ts("btw", "bp", b1s[0:32, 0:12], bt, BIG, A.mult, -0.5 * BIG, A.add)
    ts("btw", "bq0", b1s[0:32, 12:24], bt, 2.0, A.is_ge, 2 * BIG + 1, A.mult)
    ts("nxrow off1", "n1r", T.n1r[:], T.nxrow[:].indirect(T.off1[:, 0:12]), 2.0, A.mult)
    ts("btw", "bq1", b1s[0:32, 24:36], bt, 2.0, A.is_ge, 2 * BIG - 1, A.mult)
    ts("ioL0 t2", "iwe", T.iwe[:], ioL[:, 0:64], 8.0 - 8 * r, A.add, f(20), A.is_equal)
    turn("n1r", "n1t", T.n1t[0:32, :], T.n1r[0:32, :])
    for k in range(2):
        tt("bp bq%d" % k, "mk%d" % k, b1s[0:32, 36 + 12 * k:48 + 12 * k], b1s[0:32, 0:12], b1s[0:32, 12 + 12 * k:24 + 12 * k], A.subtract)
    tt("n1t mk0", "j0", jf[0:32, 0:12], T.n1t[0:32, 0:V:16], b1s[0:32, 36:48], A.subtract)
    tt("n1t mk1", "j1", jf[0:32, 12:24], T.n1t[0:32, 1:V:16], b1s[0:32, 48:60], A.add)
    ts("iwe bel", "iw0", iw[:, 0:64], T.iwe[:], below(15), A.mult, is0, A.max)
    tt("mk", "w8", T.w8[:], mk[:, 0:16:2], mk[:, 1:16:2], A.add)
    tt("j0 j1", "jf", jf[0:32, 24:36], jf[0:32, 0:12], jf[0:32, 12:24], A.max)
    ts("st01 stw", "stu", T.stu[:, 0:12], T.stw[:], float(XB), A.add)
    ts("st01 stw own n1t", "x3", x3[:, 1:V:16], T.stw[:], float(XB), A.add, f(16), A.mult)
    ts("jf m1z", "m1", T.land1[32 * (r // 2):32 * (r // 2) + 32, 16 * r:16 * r + 12], jf[0:32, 24:36], -0.5 * BIG, A.add)
    for k in range(4):
        ts("jf", "di", T.di[32 * k:32 * k + 32, :], jf[0:32, 24:36], 1.0 / 1024, A.mult, -0.4995 - BIG / 2048, A.add)
    spread("m1", "al1", "land1", mine1)
    iota("ic2", ic[:, 192:224], [[0, 32]], 14, 2)
    iota("ic2", ic[:, 288:320], [[256, 2], [1, 16]], 256, 16)
    iota("ic2", ic[:, 224:240], [[32, 4], [1, 2], [NS + 32, 2]], 0)
    iota("ic2", ic[:, 240:256], [[32, 4], [1, 2], [-NS, 2]], NS)
    iota("ic2", ic[:, 256:272], [[32, 2], [M + 32, 2], [1, 4]], 0)
    iota("ic2", ic[:, 272:288], [[32, 2], [-M, 2], [1, 4]], M)

    affine("iw0 mk", "iw1", iw[:, r:64:8], iw[:, r:64:8], bias=is15)
    affine("iw1 c256", "iw64", iw[:, 8 * r:8 * r + 8], iw[:, 8 * r:8 * r + 8], bias=f(23))
    act("w8 di", "f1t", T.f1t[:], T.w8[:].indirect(T.di[:]))
    for k in (64, 128):
        act("iw%d" % k, "iw%d" % (2 * k), iw[:, k:2 * k], iw[:, 0:k])

    nxa = T.nxa
    quarter = lambda k, j: nxa[32 * k:32 * k + 32, PART[j]:512:4]

    def lifted(k):
        ts("landn minen lift", "na%d" % k, quarter(k, k), T.landn[32 * k:32 * k + 32, :], cf[32 * k:32 * k + 32, 3:4], A.add)

    def paired(k, call):
        call("na%d" % (k ^ 1), "nb%d" % k, quarter(k, k ^ 1), quarter(k ^ 1, k ^ 1))

    for k in range(4):
        quant_x(k)
    scan("f1t", "c1L", T.c1L[:], T.f1t[:], T.f1t[:], 0.0, A.add, A.max)
    for k in range(2):
        act("c1L ic0t ict", "x1 sg", T.sg[:, V * k:V * k + V], T.c1L[:], F.Sign, scale=8.0, bias=ict[:, 32 + 16 * k:33 + 16 * k],
            accum_out=x1[:, 32 * k:32 * k + 1])
    for k in (256, 512):
        op("g", "iw%d" % k, "iw%d" % (2 * k), lambda e: e.affine_select(iw[:, k:2 * k], iw[:, 0:k], [[0, k]], A.is_ge, 0.0, 0, 0))
    for k in range(4):
        lifted(k)
    for k in (1, 0, 3, 2):
        paired(k, (copy, act)[k // 2])
    turn("x1", "x1t", T.x1t[:], x1)
    op("v", "wa0", "wa", lambda e: e.memset(T.wa[:, 0:a + 1:a], 0.0))
    copy("ioL0", "xl", cl[:, 16:28], ioL[:, 0:12])
    ts("x1t", "w1", T.w1[:], T.x1t[:], -0.5, A.mult, V / 2.0, A.add)
    act("na2 na3 nb2 nb3", "nc2", nxa[0:64, 1:512:2], nxa[64:128, 1:512:2])
    for k in range(8):
        dma("ys"[k > 4], "dc1", "w1", "p1off", T.s1off[16 * k:16 * k + 16, :], T.w1[0:128:32, :])
    dma("y", "dq1", "q0 nc2", "q1x", u8(T.q1[:, 0:A1]), u8(T.q0[:]))
    dma("y", "dq1", "s0", "q1x", T.s1[:, 0:A1], T.s0[:])
    copy("land1 m1", "zf", T.zf[:], T.land1[:])
    copy("na0 na1 nb0 nb1", "nc", nxa[64:128, 0:512:2], nxa[0:64, 0:512:2])
    dma("y", "dw1", "", "wt1", T.wt[:, 1536:3072], T.w[:, 1536:3072])

    tot, px, vt, kk = T.tot, T.px, T.vt, T.kk
    n2c, dk, dm, n1c = (kk[:, 16 * k:16 * k + 12] for k in range(4))
    copy("zf dg", "ek", T.ek[:], T.zf[:].indirect(cl[:, 2:3]))
    ts("zf dg", "hi", T.hi[:], T.zf[:].indirect(cl[:, 14:15]), 1.0 / 16, A.mult, -0.469, A.add)
    act("nb0 nb1 nb2 nb3 nc nc2 hi", "n2r", T.n2r[:], nxa[:].indirect(T.hi[:, 0:12]))
    act("s0 stu stz", "sts", T.sts[:], T.s0[:].indirect(T.stu[:, 0:13]))
    fill("pxc", T.px[:], 0.0)
    ts("ek", "lo", T.lo[:], T.ek[:], 15, A.bitwise_and)
    turn("ic2", "ict2", ict[:, 192:320], ic[:, 192:320])
    tt("lo xl iq", "nm", T.nm[:], T.lo[:].indirect(cl[:, 16:28]), T.iq[:], A.is_lt)
    turn("n2r", "n2t", T.n2t[:], T.n2r[:])
    copy("q0 stu stz", "stq", T.stq[:].bitcast(dt.uint32), T.q0[:].bitcast(dt.uint32).indirect(T.stu[:, 0:13]))
    scan("nm n2t", "sel", T.sel[:], T.nm[:], T.n2t[:], 0.0, A.mult, A.max)
    op("v", "iw1", "mk mkz", lambda e: e.memset(mk[:, 0:32:16], 0.0))
    ts("sel", "xo", T.xo[:], T.sel[:, 15:V:16], 1.0 / TN, A.mult, -0.499, A.add)
    act("sts p1off", "p1s", T.p1s[:], T.sts[:].indirect(T.s1off[:]))
    act("iw1024 xo", "tot fl", T.fl[:, 64:64 + V], iw[:].indirect(T.xo[:]), F.Identity, accum_out=tot[:, 0:1])
    affine("fl", "fb", T.fb[:], T.fl[:, 64:64 + V], scale=MARK)
    act("zf dg", "n1c", kk[:, 48:64], T.zf[:].indirect(cl[:, 2:3]), F.Relu, scale=-0.5, bias=600.25 - XB + TN * r)
    copy("stq p1off", "p1q", T.p1q[:].bitcast(dt.uint32), T.stq[:].bitcast(dt.uint32).indirect(T.s1off[:]))
    at1 = lambda c: A1 + CAP * _among(T, c, core)
    to1 = lambda buf, c: buf[:, CAP * T.rank_of(c):CAP * T.rank_of(c) + CAP]
    send(1, 0, "s", "p1s", lambda c: to1(T.p1s, c), lambda c: T.s1[:, at1(c):at1(c) + CAP], T.hs1[:])
    send(1, 0, "q", "p1q", lambda c: u8(to1(T.p1q, c)), lambda c: u8(T.q1[:, at1(c):at1(c) + CAP]), u8(T.hq1[:]))
    affine("ioL ict2", "x3", x3[:, 3:V:16], ioL[:, 1:V:16], bias=ict[:, 288:289])
    affine("n1c", "x3", x3[:, 0:V:16], n1c, scale=-1.0, bias=600.0)
    affine("iw1024", "tab", T.tab[:, S0 - 16:P0 + M + 16], iw[:, 0:NS + M + 32], scale=0.0)
    for k in range(2):
        affine("ioL bel wb2", "wa2", T.wa[:, U1 + NS * k:U1 + NS * k + NS], ioL[:, 0:NS], scale=below(2), bias=f(12 + k))
    ts("tot", "u2", tot[64:96, 1:2], tot[0:32, 0:1], tot[32:64, 0:1], A.add)
    ts("tot", "u3", tot[96:128, 1:2], tot[0:32, 0:1], tot[32:64, 0:1], A.add, tot[64:96, 0:1], A.add)
    ts("mkz tot pxc", "pxa", px[32:64, 0:32], mk[0:32, :], tot[0:32, 0:1], A.mult)
    ts("mkz tot pxc", "pxb", px[:, 48:64], mk[:, 0:16], tot[:, 0:1], A.mult, even, A.mult)
    ts("mkz u2 u3", "pxa", px[64:128, 0:32], mk[64:128, :], tot[64:128, 1:2], A.mult)
    ts("xo", "n2c", n2c, T.xo[:], -float(TN), A.mult, float(XB), A.add)
    turn("pxa pxb pxc", "pxt", T.fl[:, 0:64], px[:])
    tt("n2c sel", "x3v", x3[:, 2:V:16], n2c, T.sel[:, 15:V:16], A.add)
    scan("fl pxt first", "cnt", T.cnt[:], T.fl[:], T.fl[:], f(28), A.add, A.max)
    turn("x3 x3v", "x3t", T.x3t[:], x3[:])
    turn("cnt", "vt", vt[:], T.cnt[:, 64:64 + V])
    turn("fb", "fbt", T.fbt[:], T.fb[:])
    dma("y", "dw0", "cnt", "wt0", T.wt[:, 0:1536], T.w[:, 0:1536])
    dma("y", "dq2", "q0", "q2x", u8(T.q2[:, 0:A1]), u8(T.q0[:]))
    dma("y", "dq2", "s0", "q2x", T.s2[:, 0:A1], T.s0[:])
    ts("vt ict2", "c0u", T.c0u[:], vt[:, 0:V:16], 1.0 / 256, A.mult, ict[:, 192:193], A.add)
    scan("fbt vt", "seg", T.seg[:], T.fbt[:], vt[:], 0.0, A.max, A.min)
    tt("wa c0u x3t", "vals", T.vals[:], T.wa[:, 0:U1].indirect(T.c0u[:]), T.x3t[:], A.max)
    copy("seg", "so", T.so[:], T.seg[:, 14:V:16])
    ts("seg", "bcu", T.bcu[:], T.seg[:, 7:V:16], -float(KC), A.add)
    copy("seg", "po", T.po[:], T.seg[:, 15:V:16])
    op("v", "vals so tab", "tab2", lambda e: e.tensor_copy(T.tab[:].indirect(T.so[:]), T.vals[:]))
    ts("ioL ict2", "la", cl[:, 30:32], ioL[:, 0:129:128], ict[:, 224:225], A.add, 2.0 * NS + 15, A.min)
    ts("ioL ict2", "le", cl[:, 32:37], ioL[:, 0:257:64], ict[:, 256:257], A.add, 2.0 * M + 15, A.min)
    dma("y", "dq3", "q1a", "q2o", u8(T.q2[:, A1:A2]), u8(T.q1[:, A1:A2]))
    dma("y", "dq3", "s1a", "q2o", T.s2[:, A1:A2], T.s1[:, A1:A2])

    def collect(tag, at, y, n, lst, gg, rr, w, u, between):
        turn("tab" + tag, "ya" + tag, y[:, 0:n], T.tab[:, at:at + n])
        turn("tab" + tag, "yb" + tag, y[:, n:2 * n + 32], T.tab[:, at - 16:at + n + 16])
        ys = "ya%s yb%s l%s" % (tag, tag, "a" if tag == "2" else "e")
        between(0)
        copy(ys, "ga" + tag, gg[:, 0:w], y[:, 0:2 * n + 16].indirect(lst))
        between(1)
        tt(ys + " ga" + tag, "gb" + tag, gg[:, w:2 * w], y[:, 16:2 * n + 32].indirect(lst), gg[:, 0:w], A.add)
        between(2)
        tt("gb" + tag, "ra" + tag, rr[0:64, 0:u], gg[0:64, w:w + u], gg[64:128, w:w + u], A.add)
        tt("ra" + tag, "rb" + tag, rr[0:32, w:w + u], rr[0:32, 0:u], rr[32:64, 0:u], A.add)

    collect("2", S0, T.y2, NS, cl[:, 30:32], T.g2, T.r2, 32, 28, lambda k: quant_w(5 - k))
    for k in range(4):
        copy("rb2", "p2off", T.p2off[32 * k:32 * k + 32, :], T.r2[0:32, 32:60])
    n = 2 * CAP
    at2 = lambda c: A2 + n * _among(T, c, core)
    blk = lambda buf, c: buf[:, n * _among(T, core, c):n * _among(T, core, c) + n]
    for k, (cores, free) in enumerate(_parts(core, others, topo)):
        a, b = n * _among(T, core, cores[0]), n * _among(T, core, cores[-1]) + n
        pick("q1x q1a", "q1x s1a", "pq%d" % k, "pz%d" % k, T.p2q[:, a:b], T.p2s[:, a:b], T.q1[:], T.s1[:], T.p2off[:, a // 16:b // 16], "p2off")
        send(2, k, "q", "pq%d" % k, lambda c: u8(blk(T.p2q, c)), lambda c: u8(T.q2[:, at2(c):at2(c) + n]), u8(T.hq2[:]))
        send(2, k, "s", "pz%d" % k, lambda c: blk(T.p2s, c), lambda c: T.s2[:, at2(c):at2(c) + n], T.hs2[:])

    tt("wa wa2 bcu vals", "v4", T.v4[:], T.wa[:].indirect(T.bcu[:]), T.vals[:], A.max)
    op("v", "v4 po tab2", "tab3", lambda e: e.tensor_copy(T.tab[:].indirect(T.po[:]), T.v4[:]))
    collect("3", P0, T.y3, M, cl[:, 32:37], T.g3, T.r3, 80, 72, lambda k: quant_w(2 - k))
    halves = ((0, HALF), (HALF, M))
    where = {(2, 0): 0, (1, 0): M, (0, 0): M + HALF, (1, HALF): M + 2 * HALF, (0, HALF): 2 * M + HALF}
    ts("rb3", "fo2", T.fo[0:32, 0:18], T.r3[0:32, 82:152:4], 0.0, A.add)
    for a, b in halves:
        for k in (1, 0):
            c = where[k, a] // 16
            ts("rb3", "fo0", T.fo[0:32, c:c + (b - a) // 16], T.r3[0:32, 81 - k + a // 4:80 + b // 4:4], 0.0, A.add)
    ki = T.ki
    copy("rb3", "k0", ki[0:32, 0:18], T.r3[0:32, 83:152:4])
    for k in range(1, 4):
        copy("fo0 fo2", "fo", T.fo[32 * k:32 * k + 32, :], T.fo[0:32, :])

    def products(steps, key, a, b):
        for o in range(2):
            for k in steps:
                at = where[k, a * (k < 2)] + a * (k == 2)
                c, bank = 128 * (2 * k + o), 512 * (2 * (a > 0) + o)
                op("t", "fq%s fs%s wq%d" % (key, key, c // 128), "ps%d" % bank, lambda e: e.matmul_mx(
                    T.ps[:, bank:bank + b - a], T.wq[:, c:c + 128], T.ws[:, c:c + 128], T.fq[:, at:at + b - a],
                    T.fs[:, at:at + b - a], k == 2, k == 0))

    def store(a, b):
        bank = 1024 * (a > 0)
        copy("ps%d" % bank, "yo0%d" % a, T.yo0[:, a:b], T.ps[:, bank:bank + b - a])
        dma("y", "dy%d" % (2 * (a > 0)), "yo0%d" % a, "y0%d" % a, T.y[:, a:b], T.yo0[:, a:b])
        act("ps%d" % (bank + 512), "yo1%d" % a, T.yo1[:, a:b], T.ps[:, bank + 512:bank + 512 + b - a])
        dma("y", "dy%d" % (2 * (a > 0) + 1), "yo1%d" % a, "y1%d" % a, T.y[:, M + a:M + b], T.yo1[:, a:b])

    pick("q0", "s0", "fqn", "fsn", T.fq[:, 0:M], T.fs[:, 0:M], T.q0[:], T.s0[:], T.fo[:, 0:18], "fo2 fo")
    for a, b in halves:
        products([2], "n", a, b)
    for a, b in halves:
        c, e = where[1, a], where[1, a] + 2 * (b - a)
        pick("q2x q2o q2a", "q2x q2o s2a", "fq%d" % a, "fs%d" % a, T.fq[:, c:e], T.fs[:, c:e], T.q2[:], T.s2[:], T.fo[:, c // 16:e // 16], "fo0 fo")
        products([1, 0], str(a), a, b)
    ts("k0", "k1", ki[0:32, 18:36], ki[0:32, 0:18], 8, A.arith_shift_right)
    ts("k0", "k2", ki[0:32, 36:54], ki[0:32, 0:18], 255, A.bitwise_and)
    store(*halves[0])
    for k in range(2):
        ts("k1 k2", "x5", x5[:, 32 * k:32 * k + 18], ki[0:32, 18 + 18 * k:36 + 18 * k], -1.0, A.add)
    store(*halves[1])
    turn("x5", "x5t", T.x5t[0:32, :], x5)
    for k in range(2):
        dma("s", "did", "x5t", "id%d" % k, T["id"][k:k + 1, :], T.x5t[0:18, 32 * k:32 * k + 16])
    await_("g", [(s, None) for s in total])
